import numpy as np
import ml_dtypes


def mxq(x, axis, fmt="e4m3"):
    dtype, down = {"e4m3": (ml_dtypes.float8_e4m3fn, 7), "e5m2": (ml_dtypes.float8_e5m2, 14)}[fmt]
    v = np.moveaxis(np.asarray(x, np.float32).astype(ml_dtypes.bfloat16).astype(np.float64), axis, -1)
    blocks = v.reshape(v.shape[:-1] + (-1, 32))
    amax = np.abs(blocks).max(-1, keepdims=True)
    byte = np.maximum(np.where(amax > 0, np.frexp(amax)[1] - 1 + 127, 0) - down, 1)
    scale = np.exp2(byte - 127.0)
    codes = (blocks / scale).astype(np.float32).astype(dtype).astype(np.float64)
    return np.moveaxis((codes * scale).reshape(v.shape), -1, axis)


WIDE = False


def mx_kscale(k):
    if not WIDE:
        return np.ones(k)
    levels = np.array([24, -24, 12, -12, 0])
    if k % 512:
        return np.exp2(np.random.permutation(np.resize(levels, k // 32))).repeat(32)
    a = np.empty((k // 512, 16))
    for p in range(k // 512):
        a[p, :8] = np.random.permutation(np.resize(levels, 8))
        for g in range(8):
            far = levels[np.abs(levels - a[p, g]) >= 10]
            a[p, g + 8] = far[np.random.randint(len(far))]
    return np.exp2(a.ravel()).repeat(32)


def f64(x):
    return np.asarray(x).astype(np.float64)


def striped8(idx):
    return np.concatenate([v.reshape(-1, 16).T for v in idx]).astype(np.uint16)


def unstriped8(offs):
    return np.stack([offs[16 * g:16 * g + 16].T.reshape(-1) for g in range(8)]).astype(np.int64)


E2M1 = np.array([0.0, 0.5, 1.0, 1.5, 2.0, 3.0, 4.0, 6.0, -0.0, -0.5, -1.0, -1.5, -2.0, -3.0, -4.0, -6.0])


def pack_weight(w, fmt):
    k, n = w.shape
    w = f64(np.asarray(w, np.float32).astype(ml_dtypes.bfloat16)).reshape(k // 32, 32, n)
    amax = np.abs(w).max(1)
    if fmt == "e4m3":
        byte = np.frexp(amax)[1] - 1 + 127 - 7
    else:
        mant, ex = np.frexp(amax / 6.0)
        byte = np.where(mant > 0.5, ex, ex - 1) + 127
    byte = np.clip(np.where(amax > 0, byte, 1), 1, 254)
    scaled = (w * np.exp2(127.0 - byte)[:, None, :]).reshape(k, n).astype(np.float32)
    by_word = np.ascontiguousarray(scaled.reshape(k // 512, 128, 4, n).transpose(0, 1, 3, 2))
    if fmt == "e4m3":
        words = by_word.astype(ml_dtypes.float8_e4m3fn).view(np.uint8)
    else:
        c = by_word.astype(ml_dtypes.float4_e2m1fn).view(np.uint8) & 0xF
        words = (c[..., 0::2] | (c[..., 1::2] << 4)).reshape(k // 512, 128, 2 * n)
    return np.ascontiguousarray(words), np.ascontiguousarray(byte.astype(np.uint8).reshape(k // 512, 16, n))


def unpack_weight(words, scales, fmt):
    g, _, n = scales.shape
    words = np.ascontiguousarray(words).reshape(g, 128, n, -1)
    if fmt == "e4m3":
        vals = words.view(ml_dtypes.float8_e4m3fn).astype(np.float64)
    else:
        nib = np.empty((g, 128, n, 4), np.uint8)
        nib[..., 0::2] = words & 0xF
        nib[..., 1::2] = words >> 4
        vals = E2M1[nib]
    vals = vals * np.repeat(np.exp2(scales.astype(np.float64) - 127.0), 8, axis=1)[..., None]
    return vals.transpose(0, 1, 3, 2).reshape(g * 512, n)


def planes(y):
    n, m = y.shape
    v = y.astype(np.float32).astype(ml_dtypes.bfloat16).astype(np.float64).reshape(n // 32, 32, m)
    top = np.abs(v).max(1)
    byte = np.clip(np.where(top > 0, np.frexp(top)[1] - 1 + 127 - 7, 1), 1, 254)
    codes = (v * np.exp2(127.0 - byte)[:, None, :]).reshape(n, m).astype(np.float32).astype(ml_dtypes.float8_e4m3fn).view(np.uint8)
    words = codes.reshape(n // 512, 128, 4, m).transpose(0, 1, 3, 2)
    return np.ascontiguousarray(words), np.ascontiguousarray(byte.astype(np.uint8).reshape(n // 512, 16, m))


def sigm(f):
    return 1.0 / (1.0 + np.exp(-np.maximum(f, -700.0)))


K, R, N, T, J = 512, 1024, 512, 2048, 1024


def setup_inputs():
    n = np.random.standard_normal
    s = mx_kscale(K)[:, None]
    u = mx_kscale(R)[:, None]
    p_wu = pack_weight(n((K, R)) / np.sqrt(K) / s * u.T, "e2m1")
    p_wd = pack_weight(n((R, N)) / np.sqrt(R) / u, "e4m3")
    return {
        "xT": (n((K, T)) * s).astype(np.float32),
        "wgt": np.repeat(np.random.uniform(0.5, 2.0, (8, J)), 16, axis=0).astype(np.float32),
        "wg": (n((K, R)) / np.sqrt(K) / s).astype(np.float32),
        "wu_words": p_wu[0],
        "wu_scales": p_wu[1],
        "wd_words": p_wd[0],
        "wd_scales": p_wd[1],
        "g": (n((N, J))).astype(np.float32),
        "offs": striped8(np.stack([np.random.permutation(T)[:J] for _ in range(8)])),
    }


def reference(xT, wgt, wg, wu_words, wu_scales, wd_words, wd_scales, g, offs):
    idx = unstriped8(offs)
    rows = np.arange(K)
    xg = f64(wgt)[rows // 4 % 128] * f64(xT)[rows[:, None], idx[rows % 512 // 64]]
    xT_ = mxq(xg, 0, "e4m3")
    wg_ = mxq(f64(wg), 0, "e4m3")
    wu_ = unpack_weight(wu_words, wu_scales, "e2m1")
    ga = wg_.T @ xT_
    ub = wu_.T @ xT_
    h = sigm(ga) * ub
    h_ = mxq(h, 0, "e4m3")
    wd_ = unpack_weight(wd_words, wd_scales, "e4m3")
    y = wd_.T @ h_
    out_0 = y * f64(g)
    return (out_0,) + planes(out_0)

@@ -1,0 +1,250 @@
+from contextlib import ExitStack
+
+import concourse.mybir as mybir
+
+K, R, N, T, J = 512, 1024, 512, 2048, 1024
+FLOPS = 2 * (2 * K * R * J + R * N * J)
+
+F32 = mybir.dt.float32
+BF16 = mybir.dt.bfloat16
+I32 = mybir.dt.int32
+U32 = mybir.dt.uint32
+U16 = mybir.dt.uint16
+U8 = mybir.dt.uint8
+FP8X4 = mybir.dt.float8_e4m3fn_x4
+FP4X4 = mybir.dt.float4_e2m1fn_x4
+MULT = mybir.AluOpType.mult
+SIGMOID = mybir.ActivationFunctionType.Sigmoid
+
+P = 128
+PACK = 4
+PASS = P * PACK
+R_PASSES = R // PASS
+XW = 256
+STEP = 128
+GW = 512
+WG_PIECE = 256
+
+
+def tile_list_sigm_mulP_kernel(
+    tc, xT, wgt, wg, wu_words, wu_scales, wd_words, wd_scales, g, offs, out_0, out_1, out_2
+):
+    nc = tc.nc
+    with ExitStack() as ctx:
+        keep = ctx.enter_context(tc.tile_pool(name="keep", bufs=1))
+        ring = ctx.enter_context(tc.tile_pool(name="ring", bufs=3))
+        psum = ctx.enter_context(tc.psum_pool(name="psum", bufs=1))
+
+        offsets = keep.tile([P, J // 16], U16, name="offsets")
+        nc.sync.dma_start(offsets[:], offs)
+
+        warm_in = keep.tile([P, 1], F32, name="warm_in")
+        warm_out = keep.tile([P, 1], F32, name="warm_out")
+        wu_s_raw = keep.tile([P, R], U8, name="wu_s_raw", align_bytes=64)
+        wd_s_raw = keep.tile([P, N], U8, name="wd_s_raw", align_bytes=64)
+        nc.vector.memset(wu_s_raw[:].bitcast(I32), 0)
+        nc.vector.memset(wd_s_raw[:].bitcast(I32), 0)
+        nc.vector.memset(warm_in[:], 0.0)
+        for q in range(4):
+            nc.scalar.dma_start(
+                wu_s_raw[32 * q : 32 * q + 4, :].bitcast(I32), wu_scales[0, 4 * q : 4 * q + 4, :].bitcast(I32)
+            )
+            nc.scalar.dma_start(
+                wd_s_raw[32 * q : 32 * q + 8, :].bitcast(I32), wd_scales[:, 4 * q : 4 * q + 4, :].bitcast(I32)
+            )
+        nc.scalar.activation(warm_out[:], warm_in[:], SIGMOID)
+
+        wu_raw = keep.tile([P, 2 * R], U8, name="wu_raw", align_bytes=64)
+        nc.sync.dma_start(wu_raw[:].bitcast(I32), wu_words[0].bitcast(I32))
+
+        x_rows = xT.rearrange("(p i) t -> p i t", i=PACK)
+        wg_rows = wg.rearrange("(p i) r -> p i r", i=PACK)
+        g_rows = g.rearrange("(p t) j -> p t j", t=PACK)
+        out_rows = out_0.rearrange("(p t) j -> p t j", t=PACK)
+        x = [keep.tile([P, T], F32, name=f"x{i}") for i in range(PACK)]
+        wgt_first = keep.tile([P, XW], F32, name="wgt_first")
+        wgt_rest = keep.tile([P, J - XW], F32, name="wgt_rest")
+        wg_raw = [keep.tile([P, PACK, WG_PIECE], F32, name=f"wg_raw{u}") for u in range(R // WG_PIECE)]
+        g_sb = [keep.tile([P, PACK, GW], F32, name=f"g{c}") for c in range(J // GW)]
+        wd_raw = keep.tile([P, R_PASSES, N], I32, name="wd_raw")
+
+        def load_wg(u):
+            nc.sync.dma_start(wg_raw[u][:], wg_rows[:, :, u * WG_PIECE : (u + 1) * WG_PIECE])
+
+        nc.sync.dma_start(wgt_first[:], wgt[:, :XW])
+        nc.sync.dma_start(x[0][:], x_rows[:, 0, :])
+        nc.sync.dma_start(wgt_rest[:], wgt[:, XW:])
+        nc.sync.dma_start(x[1][:], x_rows[:, 1, :])
+        load_wg(0)
+        load_wg(1)
+        nc.sync.dma_start(x[2][:], x_rows[:, 2, :])
+        load_wg(2)
+        nc.sync.dma_start(x[3][:], x_rows[:, 3, :])
+        load_wg(3)
+        nc.sync.dma_start(wd_raw[:], wd_words.rearrange("a p n i -> p a (n i)").bitcast(I32))
+        for c in range(J // GW):
+            nc.sync.dma_start(g_sb[c][:], g_rows[:, :, c * GW : (c + 1) * GW])
+
+        wu_codes = keep.tile([P, 2 * R], U8, name="wu_codes", align_bytes=64)
+        wu_s = keep.tile([P, R], U8, name="wu_s", align_bytes=64)
+        nc.vector.tensor_copy(
+            wu_codes[:].bitcast(U16).rearrange("p (b t m) -> p b t m", b=R_PASSES, t=PACK),
+            wu_raw[:].bitcast(U16).rearrange("p (b m t) -> p b t m", b=R_PASSES, t=PACK),
+        )
+        nc.vector.tensor_copy(
+            wu_s[:].rearrange("p (b t m) -> p b t m", b=R_PASSES, t=PACK),
+            wu_s_raw[:].rearrange("p (b m t) -> p b t m", b=R_PASSES, t=PACK),
+        )
+
+        wg_codes = [keep.tile([P, PASS], U32, name=f"wg_codes{b}", align_bytes=64) for b in range(R_PASSES)]
+        wg_s = [keep.tile([P, PASS], U8, name=f"wg_s{b}", align_bytes=64) for b in range(R_PASSES)]
+        wg_bf = [keep.tile([P, PASS * PACK], BF16, name=f"wg_bf{b}", align_bytes=64) for b in range(R_PASSES)]
+
+        def round_wg(u):
+            b, m0 = divmod(u * WG_PIECE // PACK, P)
+            nc.scalar.copy(
+                wg_bf[b][:].rearrange("p (t m i) -> p m t i", t=PACK, i=PACK)[:, m0 : m0 + WG_PIECE // PACK],
+                wg_raw[u][:].rearrange("p i (m t) -> p m t i", t=PACK),
+            )
+
+        def quantize_wg(b):
+            nc.vector.quantize_mx(out=wg_codes[b][:].bitcast(FP8X4), scales=wg_s[b][:], in_=wg_bf[b][:])
+
+        chunks = J // XW
+        picked = [keep.tile([P, PACK, XW], F32, name=f"picked{c}") for c in range(chunks)]
+        xg_bf = [keep.tile([P, XW * PACK], BF16, name=f"xg_bf{c}", align_bytes=64) for c in range(chunks)]
+        xg_codes = [keep.tile([P, XW], U32, name=f"xg_codes{c}", align_bytes=64) for c in range(chunks)]
+        xg_s = [keep.tile([P, XW], U8, name=f"xg_s{c}", align_bytes=64) for c in range(chunks)]
+
+        def gather(i, c):
+            j0 = c * XW
+            weights = wgt_first[:] if c == 0 else wgt_rest[:, j0 - XW : j0]
+            nc.vector.tensor_tensor(
+                picked[c][:, i, :],
+                x[i][:].indirect(offsets[:, j0 // 16 : (j0 + XW) // 16]),
+                weights,
+                MULT,
+            )
+
+        def interleave(dst, src):
+            nc.scalar.copy(
+                dst.rearrange("p (c e i) -> p c i e", e=4, i=PACK),
+                src.rearrange("p i (c e) -> p c i e", e=4),
+            )
+
+        for i in range(PACK - 1):
+            for c in range(chunks):
+                gather(i, c)
+
+        def quantize_xg(c):
+            interleave(xg_bf[c][:], picked[c][:])
+            nc.vector.quantize_mx(out=xg_codes[c][:].bitcast(FP8X4), scales=xg_s[c][:], in_=xg_bf[c][:])
+
+        round_wg(0)
+        round_wg(1)
+        quantize_wg(0)
+        round_wg(2)
+        gather(PACK - 1, 0)
+        quantize_xg(0)
+        round_wg(3)
+        quantize_wg(1)
+        for c in range(1, chunks):
+            gather(PACK - 1, c)
+
+        wd_codes = keep.tile([P, R_PASSES * N], I32, name="wd_codes", align_bytes=64)
+        wd_s = keep.tile([P, N], U8, name="wd_s", align_bytes=64)
+        nc.vector.tensor_copy(
+            wd_codes[:].rearrange("p (a t c e) -> p a c t e", a=R_PASSES, t=PACK, e=4),
+            wd_raw[:].rearrange("p a (c e t) -> p a c t e", t=PACK, e=4),
+        )
+        nc.vector.tensor_copy(
+            wd_s[:].rearrange("p (t m) -> p t m", t=PACK),
+            wd_s_raw[:].rearrange("p (m t) -> p t m", t=PACK),
+        )
+
+        out_codes = keep.tile([P, J], U32, name="out_codes", align_bytes=64)
+        out_s = keep.tile([P, J], U8, name="out_s", align_bytes=64)
+        steps = J // STEP
+        h_bf, h_codes, h_s, y_ps, y_f32, y_bf = {}, {}, {}, {}, {}, {}
+
+        def first_stage(s, b):
+            c, j0 = divmod(s * STEP, XW)
+            rhs = xg_codes[c][:, j0 : j0 + STEP].bitcast(FP8X4)
+            rhs_scale = xg_s[c][:, j0 : j0 + STEP]
+            ga = psum.tile([P, PACK, STEP], F32, name="ga", bufs=3)
+            ub = psum.tile([P, PACK, STEP], F32, name="ub", bufs=3)
+            for t in range(PACK):
+                cols = slice(t * P, (t + 1) * P)
+                nc.tensor.matmul_mx(
+                    out=ga[:, t, :], lhsT=wg_codes[b][:, cols].bitcast(FP8X4), lhsT_scale=wg_s[b][:, cols],
+                    rhs=rhs, rhs_scale=rhs_scale, start=True, stop=True,
+                )
+            for t in range(PACK):
+                r0 = b * PASS + t * P
+                nc.tensor.matmul_mx(
+                    out=ub[:, t, :], lhsT=wu_codes[:, 2 * r0 : 2 * (r0 + P)].bitcast(FP4X4),
+                    lhsT_scale=wu_s[:, r0 : r0 + P],
+                    rhs=rhs, rhs_scale=rhs_scale, start=True, stop=True,
+                )
+            gate = ring.tile([P, STEP, PACK], F32, name="gate")
+            nc.scalar.activation(gate[:], ga[:].rearrange("p t j -> p j t"), SIGMOID)
+            if b == 0:
+                h_bf[s] = ring.tile([P, R_PASSES, STEP, PACK], BF16, name="h_bf", align_bytes=64)
+            nc.vector.tensor_tensor(h_bf[s][:, b, :, :], ub[:].rearrange("p t j -> p j t"), gate[:], MULT)
+
+        def quantize_h(s):
+            h_codes[s] = ring.tile([P, R_PASSES * STEP], U32, name="h_codes", align_bytes=64)
+            h_s[s] = ring.tile([P, R_PASSES * STEP], U8, name="h_s", align_bytes=64)
+            nc.vector.quantize_mx(
+                out=h_codes[s][:].bitcast(FP8X4), scales=h_s[s][:], in_=h_bf[s][:].rearrange("p b j t -> p (b j t)")
+            )
+
+        def second_stage(s):
+            y_ps[s] = psum.tile([P, PACK, STEP], F32, name="y_ps", bufs=2)
+            for t in range(PACK):
+                for b in range(R_PASSES):
+                    n0 = b * N + t * P
+                    cols = slice(b * STEP, (b + 1) * STEP)
+                    nc.tensor.matmul_mx(
+                        out=y_ps[s][:, t, :], lhsT=wd_codes[:, n0 : n0 + P].bitcast(FP8X4),
+                        lhsT_scale=wd_s[4 * b : P, t * P : (t + 1) * P],
+                        rhs=h_codes[s][:, cols].bitcast(FP8X4), rhs_scale=h_s[s][:, cols],
+                        start=(b == 0), stop=(b == R_PASSES - 1),
+                    )
+
+        def gate_y(s):
+            c, j0 = divmod(s * STEP, GW)
+            y_f32[s] = ring.tile([P, PACK, STEP], F32, name="y_f32", bufs=4)
+            nc.vector.tensor_tensor(y_f32[s][:], y_ps[s][:], g_sb[c][:, :, j0 : j0 + STEP], MULT)
+            nc.sync.dma_start(out_rows[:, :, s * STEP : (s + 1) * STEP], y_f32[s][:])
+            y_bf[s] = ring.tile([P, STEP * PACK], BF16, name="y_bf", align_bytes=64)
+            interleave(y_bf[s][:], y_f32[s][:])
+
+        def quantize_y(s):
+            cols = slice(s * STEP, (s + 1) * STEP)
+            nc.vector.quantize_mx(out=out_codes[:, cols].bitcast(FP8X4), scales=out_s[:, cols], in_=y_bf[s][:])
+            if s % 2 == 1:
+                pair = slice((s - 1) * STEP, (s + 1) * STEP)
+                nc.sync.dma_start(
+                    out_1[0].rearrange("p j i -> p (j i)").bitcast(I32)[:, pair], out_codes[:, pair].bitcast(I32)
+                )
+
+        for s in range(steps + 2):
+            if s < steps:
+                first_stage(s, 0)
+                first_stage(s, 1)
+            if s % 2 == 0 and s // 2 + 1 < chunks:
+                quantize_xg(s // 2 + 1)
+            if 0 <= s - 1 < steps:
+                gate_y(s - 1)
+            if s < steps:
+                quantize_h(s)
+                second_stage(s)
+            if 0 <= s - 2 < steps:
+                quantize_y(s - 2)
+
+        for q in range(4):
+            queue = nc.sync if q % 2 == 0 else nc.scalar
+            queue.dma_start(
+                out_2[0, 4 * q : 4 * q + 4, :].bitcast(I32), out_s[32 * q : 32 * q + 4, :].bitcast(I32)
+            )

@@ -20,8 +20,11 @@ P = 128
 PACK = 4
 PASS = P * PACK
 R_PASSES = R // PASS
-XW = 256
-STEP = 128
+BANK = 512
+WIDE = 256
+NARROW = 128
+PICKS = [(0, 256), (256, 256), (512, 512)]
+PIECES = [(0, 256), (256, 256), (512, 256), (768, 128), (896, 128)]
 GW = 512
 WG_PIECE = 256
 
@@ -32,61 +35,60 @@ def tile_list_sigm_mulP_kernel(
     nc = tc.nc
     with ExitStack() as ctx:
         keep = ctx.enter_context(tc.tile_pool(name="keep", bufs=1))
-        ring = ctx.enter_context(tc.tile_pool(name="ring", bufs=3))
+        ring = ctx.enter_context(tc.tile_pool(name="ring", bufs=2))
         psum = ctx.enter_context(tc.psum_pool(name="psum", bufs=1))
 
         offsets = keep.tile([P, J // 16], U16, name="offsets")
         nc.sync.dma_start(offsets[:], offs)
 
-        warm_in = keep.tile([P, 1], F32, name="warm_in")
-        warm_out = keep.tile([P, 1], F32, name="warm_out")
         wu_s_raw = keep.tile([P, R], U8, name="wu_s_raw", align_bytes=64)
         wd_s_raw = keep.tile([P, N], U8, name="wd_s_raw", align_bytes=64)
-        nc.vector.memset(wu_s_raw[:].bitcast(I32), 0)
-        nc.vector.memset(wd_s_raw[:].bitcast(I32), 0)
-        nc.vector.memset(warm_in[:], 0.0)
-        for q in range(4):
-            nc.scalar.dma_start(
-                wu_s_raw[32 * q : 32 * q + 4, :].bitcast(I32), wu_scales[0, 4 * q : 4 * q + 4, :].bitcast(I32)
-            )
-            nc.scalar.dma_start(
-                wd_s_raw[32 * q : 32 * q + 8, :].bitcast(I32), wd_scales[:, 4 * q : 4 * q + 4, :].bitcast(I32)
-            )
-        nc.scalar.activation(warm_out[:], warm_in[:], SIGMOID)
-
-        wu_raw = keep.tile([P, 2 * R], U8, name="wu_raw", align_bytes=64)
-        nc.sync.dma_start(wu_raw[:].bitcast(I32), wu_words[0].bitcast(I32))
+        nc.gpsimd.memset(wu_s_raw[:].bitcast(I32), 0)
+        nc.gpsimd.memset(wd_s_raw[:].bitcast(I32), 0)
 
         x_rows = xT.rearrange("(p i) t -> p i t", i=PACK)
         wg_rows = wg.rearrange("(p i) r -> p i r", i=PACK)
         g_rows = g.rearrange("(p t) j -> p t j", t=PACK)
         out_rows = out_0.rearrange("(p t) j -> p t j", t=PACK)
+        out_words = out_1[0].rearrange("p j i -> p (j i)").bitcast(I32)
+        wu_raw = keep.tile([P, 2 * R], U8, name="wu_raw", align_bytes=64)
         x = [keep.tile([P, T], F32, name=f"x{i}") for i in range(PACK)]
-        wgt_first = keep.tile([P, XW], F32, name="wgt_first")
-        wgt_rest = keep.tile([P, J - XW], F32, name="wgt_rest")
+        wgt_first = keep.tile([P, WIDE], F32, name="wgt_first")
+        wgt_rest = keep.tile([P, J - WIDE], F32, name="wgt_rest")
         wg_raw = [keep.tile([P, PACK, WG_PIECE], F32, name=f"wg_raw{u}") for u in range(R // WG_PIECE)]
         g_sb = [keep.tile([P, PACK, GW], F32, name=f"g{c}") for c in range(J // GW)]
         wd_raw = keep.tile([P, R_PASSES, N], I32, name="wd_raw")
 
+        def load_x(i):
+            nc.sync.dma_start(x[i][:], x_rows[:, i, :])
+
         def load_wg(u):
             nc.sync.dma_start(wg_raw[u][:], wg_rows[:, :, u * WG_PIECE : (u + 1) * WG_PIECE])
 
-        nc.sync.dma_start(wgt_first[:], wgt[:, :XW])
-        nc.sync.dma_start(x[0][:], x_rows[:, 0, :])
-        nc.sync.dma_start(wgt_rest[:], wgt[:, XW:])
-        nc.sync.dma_start(x[1][:], x_rows[:, 1, :])
-        load_wg(0)
-        load_wg(1)
-        nc.sync.dma_start(x[2][:], x_rows[:, 2, :])
-        load_wg(2)
-        nc.sync.dma_start(x[3][:], x_rows[:, 3, :])
-        load_wg(3)
+        nc.sync.dma_start(wu_raw[:].bitcast(I32), wu_words[0].bitcast(I32))
+        nc.sync.dma_start(wgt_first[:], wgt[:, :WIDE])
+        load_x(0)
+        for q in range(4):
+            nc.sync.dma_start(
+                wu_s_raw[32 * q : 32 * q + 4, :].bitcast(I32), wu_scales[0, 4 * q : 4 * q + 4, :].bitcast(I32)
+            )
+        nc.sync.dma_start(wgt_rest[:], wgt[:, WIDE:])
+        for i in range(1, PACK):
+            load_x(i)
+        for u in range(R // WG_PIECE):
+            load_wg(u)
         nc.sync.dma_start(wd_raw[:], wd_words.rearrange("a p n i -> p a (n i)").bitcast(I32))
+        for q in range(4):
+            nc.sync.dma_start(
+                wd_s_raw[32 * q : 32 * q + 8, :].bitcast(I32), wd_scales[:, 4 * q : 4 * q + 4, :].bitcast(I32)
+            )
         for c in range(J // GW):
             nc.sync.dma_start(g_sb[c][:], g_rows[:, :, c * GW : (c + 1) * GW])
 
         wu_codes = keep.tile([P, 2 * R], U8, name="wu_codes", align_bytes=64)
         wu_s = keep.tile([P, R], U8, name="wu_s", align_bytes=64)
+        wd_codes = keep.tile([P, R_PASSES * N], I32, name="wd_codes", align_bytes=64)
+        wd_s = keep.tile([P, N], U8, name="wd_s", align_bytes=64)
         nc.vector.tensor_copy(
             wu_codes[:].bitcast(U16).rearrange("p (b t m) -> p b t m", b=R_PASSES, t=PACK),
             wu_raw[:].bitcast(U16).rearrange("p (b m t) -> p b t m", b=R_PASSES, t=PACK),
@@ -96,83 +98,68 @@ def tile_list_sigm_mulP_kernel(
             wu_s_raw[:].rearrange("p (b m t) -> p b t m", b=R_PASSES, t=PACK),
         )
 
+        def deal_wd():
+            nc.vector.tensor_copy(
+                wd_s[:].rearrange("p (t m) -> p t m", t=PACK),
+                wd_s_raw[:].rearrange("p (m t) -> p t m", t=PACK),
+            )
+            nc.vector.tensor_copy(
+                wd_codes[:].rearrange("p (a t c e) -> p a c t e", a=R_PASSES, t=PACK, e=4),
+                wd_raw[:].rearrange("p a (c e t) -> p a c t e", t=PACK, e=4),
+            )
+
         wg_codes = [keep.tile([P, PASS], U32, name=f"wg_codes{b}", align_bytes=64) for b in range(R_PASSES)]
         wg_s = [keep.tile([P, PASS], U8, name=f"wg_s{b}", align_bytes=64) for b in range(R_PASSES)]
         wg_bf = [keep.tile([P, PASS * PACK], BF16, name=f"wg_bf{b}", align_bytes=64) for b in range(R_PASSES)]
 
-        def round_wg(u):
-            b, m0 = divmod(u * WG_PIECE // PACK, P)
-            nc.scalar.copy(
-                wg_bf[b][:].rearrange("p (t m i) -> p m t i", t=PACK, i=PACK)[:, m0 : m0 + WG_PIECE // PACK],
-                wg_raw[u][:].rearrange("p i (m t) -> p m t i", t=PACK),
+        def round_wg(copy, u, r0=0, width=WG_PIECE):
+            b, m0 = divmod((u * WG_PIECE + r0) // PACK, P)
+            copy(
+                wg_bf[b][:].rearrange("p (t m i) -> p m t i", t=PACK, i=PACK)[:, m0 : m0 + width // PACK],
+                wg_raw[u][:, :, r0 : r0 + width].rearrange("p i (m t) -> p m t i", t=PACK),
             )
 
         def quantize_wg(b):
             nc.vector.quantize_mx(out=wg_codes[b][:].bitcast(FP8X4), scales=wg_s[b][:], in_=wg_bf[b][:])
 
-        chunks = J // XW
-        picked = [keep.tile([P, PACK, XW], F32, name=f"picked{c}") for c in range(chunks)]
-        xg_bf = [keep.tile([P, XW * PACK], BF16, name=f"xg_bf{c}", align_bytes=64) for c in range(chunks)]
-        xg_codes = [keep.tile([P, XW], U32, name=f"xg_codes{c}", align_bytes=64) for c in range(chunks)]
-        xg_s = [keep.tile([P, XW], U8, name=f"xg_s{c}", align_bytes=64) for c in range(chunks)]
+        picked = [keep.tile([P, PACK, width], F32, name=f"picked{j0}") for j0, width in PICKS]
+        chunks = J // WIDE
+        xg_bf = [keep.tile([P, WIDE * PACK], BF16, name=f"xg_bf{c}", align_bytes=64) for c in range(chunks)]
+        xg_codes = [keep.tile([P, WIDE], U32, name=f"xg_codes{c}", align_bytes=64) for c in range(chunks)]
+        xg_s = [keep.tile([P, WIDE], U8, name=f"xg_s{c}", align_bytes=64) for c in range(chunks)]
 
-        def gather(i, c):
-            j0 = c * XW
-            weights = wgt_first[:] if c == 0 else wgt_rest[:, j0 - XW : j0]
+        def gather(i, u):
+            j0, width = PICKS[u]
+            weights = wgt_first[:] if u == 0 else wgt_rest[:, j0 - WIDE : j0 - WIDE + width]
             nc.vector.tensor_tensor(
-                picked[c][:, i, :],
-                x[i][:].indirect(offsets[:, j0 // 16 : (j0 + XW) // 16]),
-                weights,
-                MULT,
+                picked[u][:, i, :], x[i][:].indirect(offsets[:, j0 // 16 : (j0 + width) // 16]), weights, MULT
             )
 
         def interleave(dst, src):
-            nc.scalar.copy(
-                dst.rearrange("p (c e i) -> p c i e", e=4, i=PACK),
-                src.rearrange("p i (c e) -> p c i e", e=4),
-            )
-
-        for i in range(PACK - 1):
-            for c in range(chunks):
-                gather(i, c)
+            width = src.shape[2]
+            for j0 in range(0, width, NARROW):
+                nc.scalar.copy(
+                    dst[:, j0 * PACK : (j0 + NARROW) * PACK].rearrange("p (c e i) -> p c i e", e=4, i=PACK),
+                    src[:, :, j0 : j0 + NARROW].rearrange("p i (c e) -> p c i e", e=4),
+                )
 
         def quantize_xg(c):
-            interleave(xg_bf[c][:], picked[c][:])
+            u = min(c, len(PICKS) - 1)
+            j0 = c * WIDE - PICKS[u][0]
+            interleave(xg_bf[c][:], picked[u][:, :, j0 : j0 + WIDE])
             nc.vector.quantize_mx(out=xg_codes[c][:].bitcast(FP8X4), scales=xg_s[c][:], in_=xg_bf[c][:])
-
-        round_wg(0)
-        round_wg(1)
-        quantize_wg(0)
-        round_wg(2)
-        gather(PACK - 1, 0)
-        quantize_xg(0)
-        round_wg(3)
-        quantize_wg(1)
-        for c in range(1, chunks):
-            gather(PACK - 1, c)
-
-        wd_codes = keep.tile([P, R_PASSES * N], I32, name="wd_codes", align_bytes=64)
-        wd_s = keep.tile([P, N], U8, name="wd_s", align_bytes=64)
-        nc.vector.tensor_copy(
-            wd_codes[:].rearrange("p (a t c e) -> p a c t e", a=R_PASSES, t=PACK, e=4),
-            wd_raw[:].rearrange("p a (c e t) -> p a c t e", t=PACK, e=4),
-        )
-        nc.vector.tensor_copy(
-            wd_s[:].rearrange("p (t m) -> p t m", t=PACK),
-            wd_s_raw[:].rearrange("p (m t) -> p t m", t=PACK),
-        )
 
         out_codes = keep.tile([P, J], U32, name="out_codes", align_bytes=64)
         out_s = keep.tile([P, J], U8, name="out_s", align_bytes=64)
-        steps = J // STEP
-        h_bf, h_codes, h_s, y_ps, y_f32, y_bf = {}, {}, {}, {}, {}, {}
+        steps = J // NARROW
+        h_bf, y_ps, y_bf = {}, {}, {}
 
         def first_stage(s, b):
-            c, j0 = divmod(s * STEP, XW)
-            rhs = xg_codes[c][:, j0 : j0 + STEP].bitcast(FP8X4)
-            rhs_scale = xg_s[c][:, j0 : j0 + STEP]
-            ga = psum.tile([P, PACK, STEP], F32, name="ga", bufs=3)
-            ub = psum.tile([P, PACK, STEP], F32, name="ub", bufs=3)
+            c, j0 = divmod(s * NARROW, WIDE)
+            rhs = xg_codes[c][:, j0 : j0 + NARROW].bitcast(FP8X4)
+            rhs_scale = xg_s[c][:, j0 : j0 + NARROW]
+            ga = psum.tile([P, PACK, NARROW], F32, name="ga", bufs=3)
+            ub = psum.tile([P, PACK, NARROW], F32, name="ub", bufs=3)
             for t in range(PACK):
                 cols = slice(t * P, (t + 1) * P)
                 nc.tensor.matmul_mx(
@@ -186,62 +173,75 @@ def tile_list_sigm_mulP_kernel(
                     lhsT_scale=wu_s[:, r0 : r0 + P],
                     rhs=rhs, rhs_scale=rhs_scale, start=True, stop=True,
                 )
-            gate = ring.tile([P, STEP, PACK], F32, name="gate")
+            gate = ring.tile([P, NARROW, PACK], F32, name="gate", bufs=3)
             nc.scalar.activation(gate[:], ga[:].rearrange("p t j -> p j t"), SIGMOID)
             if b == 0:
-                h_bf[s] = ring.tile([P, R_PASSES, STEP, PACK], BF16, name="h_bf", align_bytes=64)
+                h_bf[s] = ring.tile([P, R_PASSES, NARROW, PACK], BF16, name="h_bf", align_bytes=64, bufs=4)
             nc.vector.tensor_tensor(h_bf[s][:, b, :, :], ub[:].rearrange("p t j -> p j t"), gate[:], MULT)
 
-        def quantize_h(s):
-            h_codes[s] = ring.tile([P, R_PASSES * STEP], U32, name="h_codes", align_bytes=64)
-            h_s[s] = ring.tile([P, R_PASSES * STEP], U8, name="h_s", align_bytes=64)
-            nc.vector.quantize_mx(
-                out=h_codes[s][:].bitcast(FP8X4), scales=h_s[s][:], in_=h_bf[s][:].rearrange("p b j t -> p (b j t)")
-            )
-
         def second_stage(s):
-            y_ps[s] = psum.tile([P, PACK, STEP], F32, name="y_ps", bufs=2)
+            h_codes = ring.tile([P, R_PASSES * NARROW], U32, name="h_codes", align_bytes=64, bufs=3)
+            h_s = ring.tile([P, R_PASSES * NARROW], U8, name="h_s", align_bytes=64, bufs=3)
+            nc.vector.quantize_mx(
+                out=h_codes[:].bitcast(FP8X4), scales=h_s[:], in_=h_bf[s][:].rearrange("p b j t -> p (b j t)")
+            )
+            y_ps[s] = psum.tile([P, PACK, NARROW], F32, name="y_ps", bufs=2)
             for t in range(PACK):
                 for b in range(R_PASSES):
                     n0 = b * N + t * P
-                    cols = slice(b * STEP, (b + 1) * STEP)
+                    cols = slice(b * NARROW, (b + 1) * NARROW)
                     nc.tensor.matmul_mx(
                         out=y_ps[s][:, t, :], lhsT=wd_codes[:, n0 : n0 + P].bitcast(FP8X4),
                         lhsT_scale=wd_s[4 * b : P, t * P : (t + 1) * P],
-                        rhs=h_codes[s][:, cols].bitcast(FP8X4), rhs_scale=h_s[s][:, cols],
+                        rhs=h_codes[:, cols].bitcast(FP8X4), rhs_scale=h_s[:, cols],
                         start=(b == 0), stop=(b == R_PASSES - 1),
                     )
 
         def gate_y(s):
-            c, j0 = divmod(s * STEP, GW)
-            y_f32[s] = ring.tile([P, PACK, STEP], F32, name="y_f32", bufs=4)
-            nc.vector.tensor_tensor(y_f32[s][:], y_ps[s][:], g_sb[c][:, :, j0 : j0 + STEP], MULT)
-            nc.sync.dma_start(out_rows[:, :, s * STEP : (s + 1) * STEP], y_f32[s][:])
-            y_bf[s] = ring.tile([P, STEP * PACK], BF16, name="y_bf", align_bytes=64)
-            interleave(y_bf[s][:], y_f32[s][:])
+            c, j0 = divmod(s * NARROW, GW)
+            y_f32 = ring.tile([P, PACK, NARROW], F32, name="y_f32", bufs=4)
+            nc.vector.tensor_tensor(y_f32[:], y_ps[s][:], g_sb[c][:, :, j0 : j0 + NARROW], MULT)
+            nc.sync.dma_start(out_rows[:, :, s * NARROW : (s + 1) * NARROW], y_f32[:])
+            if s % 2 == 0:
+                y_bf[s // 2] = ring.tile([P, 2, NARROW * PACK], BF16, name="y_bf", align_bytes=64, bufs=3)
+            interleave(y_bf[s // 2][:, s % 2, :], y_f32[:])
 
-        def quantize_y(s):
-            cols = slice(s * STEP, (s + 1) * STEP)
-            nc.vector.quantize_mx(out=out_codes[:, cols].bitcast(FP8X4), scales=out_s[:, cols], in_=y_bf[s][:])
-            if s % 2 == 1:
-                pair = slice((s - 1) * STEP, (s + 1) * STEP)
-                nc.sync.dma_start(
-                    out_1[0].rearrange("p j i -> p (j i)").bitcast(I32)[:, pair], out_codes[:, pair].bitcast(I32)
-                )
+        def quantize_y(first, count):
+            cols = slice(first * NARROW, (first + count) * NARROW)
+            rounded = y_bf[first // 2][:, first % 2 : first % 2 + count, :].rearrange("p s x -> p (s x)")
+            nc.vector.quantize_mx(out=out_codes[:, cols].bitcast(FP8X4), scales=out_s[:, cols], in_=rounded)
+            nc.sync.dma_start(out_words[:, cols], out_codes[:, cols].bitcast(I32))
 
-        for s in range(steps + 2):
-            if s < steps:
+        for i in range(PACK):
+            for u in range(len(PICKS)):
+                gather(i, u)
+        quantize_xg(0)
+        round_wg(nc.scalar.copy, 0)
+        round_wg(nc.vector.tensor_copy, 1)
+        quantize_wg(0)
+        first_stage(0, 0)
+        first_stage(1, 0)
+        round_wg(nc.vector.tensor_copy, 2)
+        round_wg(nc.scalar.copy, 3, 0, NARROW)
+        round_wg(nc.scalar.copy, 3, NARROW, NARROW)
+        quantize_wg(1)
+        quantize_xg(1)
+        deal_wd()
+        for s in range(steps + 1):
+            if 2 <= s < steps:
                 first_stage(s, 0)
+            if s < steps:
                 first_stage(s, 1)
-            if s % 2 == 0 and s // 2 + 1 < chunks:
-                quantize_xg(s // 2 + 1)
-            if 0 <= s - 1 < steps:
+            if s in (1, 3):
+                quantize_xg(2 + s // 2)
+            if s >= 1:
                 gate_y(s - 1)
             if s < steps:
-                quantize_h(s)
                 second_stage(s)
-            if 0 <= s - 2 < steps:
-                quantize_y(s - 2)
+            if s in (3, 5, 7):
+                quantize_y(s - 3, 2)
+        quantize_y(steps - 2, 1)
+        quantize_y(steps - 1, 1)
 
         for q in range(4):
             queue = nc.sync if q % 2 == 0 else nc.scalar

@@ -20,13 +20,20 @@ P = 128
 PACK = 4
 PASS = P * PACK
 R_PASSES = R // PASS
-BANK = 512
-WIDE = 256
-NARROW = 128
-PICKS = [(0, 256), (256, 256), (512, 512)]
-PIECES = [(0, 256), (256, 256), (512, 256), (768, 128), (896, 128)]
-GW = 512
-WG_PIECE = 256
+QUADRANTS, QUADRANT = 4, 32
+SCALE_ROWS = 4
+HEAD = 16
+CUT = J // HEAD
+LINE = 4
+STEP = 128
+STEPS = J // STEP
+CHUNK = 256
+CHUNKS = J // CHUNK
+HALF = J // 2
+PICKS = [(0, CHUNK), (CHUNK, CHUNK), (HALF, HALF)]
+WG_PIECES = [(0, PASS // 2), (PASS // 2, PASS // 2), (PASS, PASS)]
+LEAD = 2
+ALIGN = 64
 
 
 def tile_list_sigm_mulP_kernel(
@@ -35,14 +42,14 @@ def tile_list_sigm_mulP_kernel(
     nc = tc.nc
     with ExitStack() as ctx:
         keep = ctx.enter_context(tc.tile_pool(name="keep", bufs=1))
-        ring = ctx.enter_context(tc.tile_pool(name="ring", bufs=2))
+        ring = ctx.enter_context(tc.tile_pool(name="ring", bufs=3))
         psum = ctx.enter_context(tc.psum_pool(name="psum", bufs=1))
 
-        offsets = keep.tile([P, J // 16], U16, name="offsets")
+        offsets = keep.tile([P, J // HEAD], U16, name="offsets")
         nc.sync.dma_start(offsets[:], offs)
 
-        wu_s_raw = keep.tile([P, R], U8, name="wu_s_raw", align_bytes=64)
-        wd_s_raw = keep.tile([P, N], U8, name="wd_s_raw", align_bytes=64)
+        wu_s_raw = keep.tile([P, R], U8, name="wu_s_raw", align_bytes=ALIGN)
+        wd_s_raw = keep.tile([P, N], U8, name="wd_s_raw", align_bytes=ALIGN)
         nc.gpsimd.memset(wu_s_raw[:].bitcast(I32), 0)
         nc.gpsimd.memset(wd_s_raw[:].bitcast(I32), 0)
 
@@ -51,44 +58,53 @@ def tile_list_sigm_mulP_kernel(
         g_rows = g.rearrange("(p t) j -> p t j", t=PACK)
         out_rows = out_0.rearrange("(p t) j -> p t j", t=PACK)
         out_words = out_1[0].rearrange("p j i -> p (j i)").bitcast(I32)
-        wu_raw = keep.tile([P, 2 * R], U8, name="wu_raw", align_bytes=64)
-        x = [keep.tile([P, T], F32, name=f"x{i}") for i in range(PACK)]
-        wgt_first = keep.tile([P, WIDE], F32, name="wgt_first")
-        wgt_rest = keep.tile([P, J - WIDE], F32, name="wgt_rest")
-        wg_raw = [keep.tile([P, PACK, WG_PIECE], F32, name=f"wg_raw{u}") for u in range(R // WG_PIECE)]
-        g_sb = [keep.tile([P, PACK, GW], F32, name=f"g{c}") for c in range(J // GW)]
+        wu_raw = keep.tile([P, 2 * R], U8, name="wu_raw", align_bytes=ALIGN)
+        planes = [keep.tile([P, T], F32, name=f"plane{i}") for i in range(PACK)]
+        wgt_cut = keep.tile([P, CUT], F32, name="wgt_cut", align_bytes=ALIGN)
+        wg_raw = [keep.tile([P, PACK, width], F32, name=f"wg_raw{r0}") for r0, width in WG_PIECES]
+        g_sb = [keep.tile([P, PACK, HALF], F32, name=f"g{half}") for half in range(2)]
         wd_raw = keep.tile([P, R_PASSES, N], I32, name="wd_raw")
 
-        def load_x(i):
-            nc.sync.dma_start(x[i][:], x_rows[:, i, :])
-
-        def load_wg(u):
-            nc.sync.dma_start(wg_raw[u][:], wg_rows[:, :, u * WG_PIECE : (u + 1) * WG_PIECE])
-
+        nc.sync.dma_start(wgt_cut[:], wgt[0:P:HEAD, :].rearrange("a (c j) -> a c j", j=CUT))
         nc.sync.dma_start(wu_raw[:].bitcast(I32), wu_words[0].bitcast(I32))
-        nc.sync.dma_start(wgt_first[:], wgt[:, :WIDE])
-        load_x(0)
-        for q in range(4):
+        nc.sync.dma_start(planes[0][:], x_rows[:, 0, :])
+        for q in range(QUADRANTS):
             nc.sync.dma_start(
-                wu_s_raw[32 * q : 32 * q + 4, :].bitcast(I32), wu_scales[0, 4 * q : 4 * q + 4, :].bitcast(I32)
+                wu_s_raw[QUADRANT * q : QUADRANT * q + SCALE_ROWS, :].bitcast(I32),
+                wu_scales[0, SCALE_ROWS * q : SCALE_ROWS * (q + 1), :].bitcast(I32),
             )
-        nc.sync.dma_start(wgt_rest[:], wgt[:, WIDE:])
         for i in range(1, PACK):
-            load_x(i)
-        for u in range(R // WG_PIECE):
-            load_wg(u)
-        nc.sync.dma_start(wd_raw[:], wd_words.rearrange("a p n i -> p a (n i)").bitcast(I32))
-        for q in range(4):
+            nc.sync.dma_start(planes[i][:], x_rows[:, i, :])
+        for piece, (r0, width) in zip(wg_raw, WG_PIECES):
+            nc.sync.dma_start(piece[:], wg_rows[:, :, r0 : r0 + width])
+        nc.sync.dma_start(wd_raw[:], wd_words.rearrange("b p n i -> p b (n i)").bitcast(I32))
+        for q in range(QUADRANTS):
             nc.sync.dma_start(
-                wd_s_raw[32 * q : 32 * q + 8, :].bitcast(I32), wd_scales[:, 4 * q : 4 * q + 4, :].bitcast(I32)
+                wd_s_raw[QUADRANT * q : QUADRANT * q + R_PASSES * SCALE_ROWS, :].bitcast(I32),
+                wd_scales[:, SCALE_ROWS * q : SCALE_ROWS * (q + 1), :].bitcast(I32),
             )
-        for c in range(J // GW):
-            nc.sync.dma_start(g_sb[c][:], g_rows[:, :, c * GW : (c + 1) * GW])
+        for half in range(2):
+            nc.sync.dma_start(g_sb[half][:], g_rows[:, :, half * HALF : (half + 1) * HALF])
 
-        wu_codes = keep.tile([P, 2 * R], U8, name="wu_codes", align_bytes=64)
-        wu_s = keep.tile([P, R], U8, name="wu_s", align_bytes=64)
-        wd_codes = keep.tile([P, R_PASSES * N], I32, name="wd_codes", align_bytes=64)
-        wd_s = keep.tile([P, N], U8, name="wd_s", align_bytes=64)
+        wgt_turned = keep.tile([P, CUT], F32, name="wgt_turned", align_bytes=ALIGN)
+        for j0 in range(0, CUT, QUADRANT):
+            nc.vector.transpose(wgt_turned[:, j0 : j0 + QUADRANT], wgt_cut[:, j0 : j0 + QUADRANT])
+        wgt_sb = []
+        cuts = HALF // CUT
+        for half in range(2):
+            repeated = keep.tile([P, HALF], F32, name=f"wgt_repeated{half}", align_bytes=ALIGN)
+            source = wgt_turned[:].rearrange("p (sa c) -> p c sa", c=HEAD)[:, half * cuts : (half + 1) * cuts, :]
+            nc.scalar.copy(
+                repeated[:].rearrange("p (c sa rep) -> p c sa rep", c=cuts, rep=HEAD),
+                source.unsqueeze(3).to_broadcast([P, cuts, CUT // HEAD, HEAD]),
+            )
+            wgt_sb.append(keep.tile([P, HALF], F32, name=f"wgt{half}", align_bytes=ALIGN))
+            nc.vector.transpose(wgt_sb[half][:], repeated[:])
+
+        wu_codes = keep.tile([P, 2 * R], U8, name="wu_codes", align_bytes=ALIGN)
+        wu_s = keep.tile([P, R], U8, name="wu_s", align_bytes=ALIGN)
+        wd_codes = keep.tile([P, R_PASSES * N], I32, name="wd_codes", align_bytes=ALIGN)
+        wd_s = keep.tile([P, N], U8, name="wd_s", align_bytes=ALIGN)
         nc.vector.tensor_copy(
             wu_codes[:].bitcast(U16).rearrange("p (b t m) -> p b t m", b=R_PASSES, t=PACK),
             wu_raw[:].bitcast(U16).rearrange("p (b m t) -> p b t m", b=R_PASSES, t=PACK),
@@ -104,62 +120,63 @@ def tile_list_sigm_mulP_kernel(
                 wd_s_raw[:].rearrange("p (m t) -> p t m", t=PACK),
             )
             nc.vector.tensor_copy(
-                wd_codes[:].rearrange("p (a t c e) -> p a c t e", a=R_PASSES, t=PACK, e=4),
-                wd_raw[:].rearrange("p a (c e t) -> p a c t e", t=PACK, e=4),
+                wd_codes[:].rearrange("p (b t c e) -> p b c t e", b=R_PASSES, t=PACK, e=LINE),
+                wd_raw[:].rearrange("p b (c e t) -> p b c t e", t=PACK, e=LINE),
             )
 
-        wg_codes = [keep.tile([P, PASS], U32, name=f"wg_codes{b}", align_bytes=64) for b in range(R_PASSES)]
-        wg_s = [keep.tile([P, PASS], U8, name=f"wg_s{b}", align_bytes=64) for b in range(R_PASSES)]
-        wg_bf = [keep.tile([P, PASS * PACK], BF16, name=f"wg_bf{b}", align_bytes=64) for b in range(R_PASSES)]
+        wg_codes = [keep.tile([P, PASS], U32, name=f"wg_codes{b}", align_bytes=ALIGN) for b in range(R_PASSES)]
+        wg_s = [keep.tile([P, PASS], U8, name=f"wg_s{b}", align_bytes=ALIGN) for b in range(R_PASSES)]
+        wg_bf = [keep.tile([P, PASS * PACK], BF16, name=f"wg_bf{b}", align_bytes=ALIGN) for b in range(R_PASSES)]
 
-        def round_wg(copy, u, r0=0, width=WG_PIECE):
-            b, m0 = divmod((u * WG_PIECE + r0) // PACK, P)
+        def round_wg(copy, u):
+            r0, width = WG_PIECES[u]
+            b, m0 = divmod(r0 // PACK, P)
             copy(
                 wg_bf[b][:].rearrange("p (t m i) -> p m t i", t=PACK, i=PACK)[:, m0 : m0 + width // PACK],
-                wg_raw[u][:, :, r0 : r0 + width].rearrange("p i (m t) -> p m t i", t=PACK),
+                wg_raw[u][:].rearrange("p i (m t) -> p m t i", t=PACK),
             )
 
         def quantize_wg(b):
             nc.vector.quantize_mx(out=wg_codes[b][:].bitcast(FP8X4), scales=wg_s[b][:], in_=wg_bf[b][:])
 
         picked = [keep.tile([P, PACK, width], F32, name=f"picked{j0}") for j0, width in PICKS]
-        chunks = J // WIDE
-        xg_bf = [keep.tile([P, WIDE * PACK], BF16, name=f"xg_bf{c}", align_bytes=64) for c in range(chunks)]
-        xg_codes = [keep.tile([P, WIDE], U32, name=f"xg_codes{c}", align_bytes=64) for c in range(chunks)]
-        xg_s = [keep.tile([P, WIDE], U8, name=f"xg_s{c}", align_bytes=64) for c in range(chunks)]
+        staging = keep.tile([P, CHUNK * PACK], BF16, name="staging", align_bytes=ALIGN)
+        xg_codes = [keep.tile([P, CHUNK], U32, name=f"xg_codes{c}", align_bytes=ALIGN) for c in range(CHUNKS)]
+        xg_s = [keep.tile([P, CHUNK], U8, name=f"xg_s{c}", align_bytes=ALIGN) for c in range(CHUNKS)]
 
         def gather(i, u):
             j0, width = PICKS[u]
-            weights = wgt_first[:] if u == 0 else wgt_rest[:, j0 - WIDE : j0 - WIDE + width]
+            half, inside = divmod(j0, HALF)
             nc.vector.tensor_tensor(
-                picked[u][:, i, :], x[i][:].indirect(offsets[:, j0 // 16 : (j0 + width) // 16]), weights, MULT
+                picked[u][:, i, :],
+                planes[i][:].indirect(offsets[:, j0 // HEAD : (j0 + width) // HEAD]),
+                wgt_sb[half][:, inside : inside + width],
+                MULT,
             )
 
         def interleave(dst, src):
-            width = src.shape[2]
-            for j0 in range(0, width, NARROW):
+            for j0 in range(0, src.shape[2], STEP):
                 nc.scalar.copy(
-                    dst[:, j0 * PACK : (j0 + NARROW) * PACK].rearrange("p (c e i) -> p c i e", e=4, i=PACK),
-                    src[:, :, j0 : j0 + NARROW].rearrange("p i (c e) -> p c i e", e=4),
+                    dst[:, j0 * PACK : (j0 + STEP) * PACK].rearrange("p (c e i) -> p c i e", e=LINE, i=PACK),
+                    src[:, :, j0 : j0 + STEP].rearrange("p i (c e) -> p c i e", e=LINE),
                 )
 
         def quantize_xg(c):
             u = min(c, len(PICKS) - 1)
-            j0 = c * WIDE - PICKS[u][0]
-            interleave(xg_bf[c][:], picked[u][:, :, j0 : j0 + WIDE])
-            nc.vector.quantize_mx(out=xg_codes[c][:].bitcast(FP8X4), scales=xg_s[c][:], in_=xg_bf[c][:])
+            inside = c * CHUNK - PICKS[u][0]
+            interleave(staging[:], picked[u][:, :, inside : inside + CHUNK])
+            nc.vector.quantize_mx(out=xg_codes[c][:].bitcast(FP8X4), scales=xg_s[c][:], in_=staging[:])
 
-        out_codes = keep.tile([P, J], U32, name="out_codes", align_bytes=64)
-        out_s = keep.tile([P, J], U8, name="out_s", align_bytes=64)
-        steps = J // NARROW
+        out_codes = keep.tile([P, J], U32, name="out_codes", align_bytes=ALIGN)
+        out_s = keep.tile([P, J], U8, name="out_s", align_bytes=ALIGN)
         h_bf, y_ps, y_bf = {}, {}, {}
 
         def first_stage(s, b):
-            c, j0 = divmod(s * NARROW, WIDE)
-            rhs = xg_codes[c][:, j0 : j0 + NARROW].bitcast(FP8X4)
-            rhs_scale = xg_s[c][:, j0 : j0 + NARROW]
-            ga = psum.tile([P, PACK, NARROW], F32, name="ga", bufs=3)
-            ub = psum.tile([P, PACK, NARROW], F32, name="ub", bufs=3)
+            c, inside = divmod(s * STEP, CHUNK)
+            rhs = xg_codes[c][:, inside : inside + STEP].bitcast(FP8X4)
+            rhs_scale = xg_s[c][:, inside : inside + STEP]
+            ga = psum.tile([P, PACK, STEP], F32, name="ga", bufs=3)
+            ub = psum.tile([P, PACK, STEP], F32, name="ub", bufs=3)
             for t in range(PACK):
                 cols = slice(t * P, (t + 1) * P)
                 nc.tensor.matmul_mx(
@@ -167,50 +184,55 @@ def tile_list_sigm_mulP_kernel(
                     rhs=rhs, rhs_scale=rhs_scale, start=True, stop=True,
                 )
             for t in range(PACK):
-                r0 = b * PASS + t * P
+                col = b * PASS + t * P
                 nc.tensor.matmul_mx(
-                    out=ub[:, t, :], lhsT=wu_codes[:, 2 * r0 : 2 * (r0 + P)].bitcast(FP4X4),
-                    lhsT_scale=wu_s[:, r0 : r0 + P],
+                    out=ub[:, t, :], lhsT=wu_codes[:, 2 * col : 2 * (col + P)].bitcast(FP4X4),
+                    lhsT_scale=wu_s[:, col : col + P],
                     rhs=rhs, rhs_scale=rhs_scale, start=True, stop=True,
                 )
-            gate = ring.tile([P, NARROW, PACK], F32, name="gate", bufs=3)
-            nc.scalar.activation(gate[:], ga[:].rearrange("p t j -> p j t"), SIGMOID)
+            if (s, b) == (0, 0):
+                gate = staging[:].bitcast(F32).rearrange("p (j t) -> p j t", t=PACK)
+            else:
+                gate = ring.tile([P, STEP, PACK], F32, name="gate")[:]
+            nc.scalar.activation(gate, ga[:].rearrange("p t j -> p j t"), SIGMOID)
             if b == 0:
-                h_bf[s] = ring.tile([P, R_PASSES, NARROW, PACK], BF16, name="h_bf", align_bytes=64, bufs=4)
-            nc.vector.tensor_tensor(h_bf[s][:, b, :, :], ub[:].rearrange("p t j -> p j t"), gate[:], MULT)
+                h_bf[s] = ring.tile([P, R_PASSES, STEP, PACK], BF16, name="h_bf", align_bytes=ALIGN, bufs=4)
+            nc.vector.tensor_tensor(h_bf[s][:, b, :, :], ub[:].rearrange("p t j -> p j t"), gate, MULT)
 
         def second_stage(s):
-            h_codes = ring.tile([P, R_PASSES * NARROW], U32, name="h_codes", align_bytes=64, bufs=3)
-            h_s = ring.tile([P, R_PASSES * NARROW], U8, name="h_s", align_bytes=64, bufs=3)
+            h_codes = ring.tile([P, R_PASSES * STEP], U32, name="h_codes", align_bytes=ALIGN)
+            h_s = ring.tile([P, R_PASSES * STEP], U8, name="h_s", align_bytes=ALIGN)
             nc.vector.quantize_mx(
                 out=h_codes[:].bitcast(FP8X4), scales=h_s[:], in_=h_bf[s][:].rearrange("p b j t -> p (b j t)")
             )
-            y_ps[s] = psum.tile([P, PACK, NARROW], F32, name="y_ps", bufs=2)
+            y_ps[s] = psum.tile([P, PACK, STEP], F32, name="y_ps", bufs=2)
             for t in range(PACK):
                 for b in range(R_PASSES):
-                    n0 = b * N + t * P
-                    cols = slice(b * NARROW, (b + 1) * NARROW)
+                    col = b * N + t * P
+                    tokens = slice(b * STEP, (b + 1) * STEP)
                     nc.tensor.matmul_mx(
-                        out=y_ps[s][:, t, :], lhsT=wd_codes[:, n0 : n0 + P].bitcast(FP8X4),
-                        lhsT_scale=wd_s[4 * b : P, t * P : (t + 1) * P],
-                        rhs=h_codes[:, cols].bitcast(FP8X4), rhs_scale=h_s[:, cols],
+                        out=y_ps[s][:, t, :], lhsT=wd_codes[:, col : col + P].bitcast(FP8X4),
+                        lhsT_scale=wd_s[SCALE_ROWS * b : P, t * P : (t + 1) * P],
+                        rhs=h_codes[:, tokens].bitcast(FP8X4), rhs_scale=h_s[:, tokens],
                         start=(b == 0), stop=(b == R_PASSES - 1),
                     )
 
-        def gate_y(s):
-            c, j0 = divmod(s * NARROW, GW)
-            y_f32 = ring.tile([P, PACK, NARROW], F32, name="y_f32", bufs=4)
-            nc.vector.tensor_tensor(y_f32[:], y_ps[s][:], g_sb[c][:, :, j0 : j0 + NARROW], MULT)
-            nc.sync.dma_start(out_rows[:, :, s * NARROW : (s + 1) * NARROW], y_f32[:])
-            if s % 2 == 0:
-                y_bf[s // 2] = ring.tile([P, 2, NARROW * PACK], BF16, name="y_bf", align_bytes=64, bufs=3)
-            interleave(y_bf[s // 2][:, s % 2, :], y_f32[:])
+        def finish_out(s):
+            half, inside = divmod(s * STEP, HALF)
+            result = ring.tile([P, PACK, STEP], F32, name="result", bufs=4)
+            nc.vector.tensor_tensor(result[:], y_ps[s][:], g_sb[half][:, :, inside : inside + STEP], MULT)
+            nc.sync.dma_start(out_rows[:, :, s * STEP : (s + 1) * STEP], result[:])
+            pair, member = divmod(s, 2)
+            if member == 0:
+                y_bf[pair] = ring.tile([P, 2, STEP * PACK], BF16, name="y_bf", align_bytes=ALIGN)
+            interleave(y_bf[pair][:, member, :], result[:])
 
-        def quantize_y(first, count):
-            cols = slice(first * NARROW, (first + count) * NARROW)
-            rounded = y_bf[first // 2][:, first % 2 : first % 2 + count, :].rearrange("p s x -> p (s x)")
-            nc.vector.quantize_mx(out=out_codes[:, cols].bitcast(FP8X4), scales=out_s[:, cols], in_=rounded)
-            nc.sync.dma_start(out_words[:, cols], out_codes[:, cols].bitcast(I32))
+        def quantize_out(first, count):
+            pair, member = divmod(first, 2)
+            tokens = slice(first * STEP, (first + count) * STEP)
+            rounded = y_bf[pair][:, member : member + count, :].rearrange("p s x -> p (s x)")
+            nc.vector.quantize_mx(out=out_codes[:, tokens].bitcast(FP8X4), scales=out_s[:, tokens], in_=rounded)
+            nc.sync.dma_start(out_words[:, tokens], out_codes[:, tokens].bitcast(I32))
 
         for i in range(PACK):
             for u in range(len(PICKS)):
@@ -219,32 +241,31 @@ def tile_list_sigm_mulP_kernel(
         round_wg(nc.scalar.copy, 0)
         round_wg(nc.vector.tensor_copy, 1)
         quantize_wg(0)
-        first_stage(0, 0)
-        first_stage(1, 0)
+        for s in range(LEAD):
+            first_stage(s, 0)
         round_wg(nc.vector.tensor_copy, 2)
-        round_wg(nc.scalar.copy, 3, 0, NARROW)
-        round_wg(nc.scalar.copy, 3, NARROW, NARROW)
         quantize_wg(1)
         quantize_xg(1)
         deal_wd()
-        for s in range(steps + 1):
-            if 2 <= s < steps:
+        for s in range(STEPS + 1):
+            if LEAD <= s < STEPS:
                 first_stage(s, 0)
-            if s < steps:
+            if s < STEPS:
                 first_stage(s, 1)
-            if s in (1, 3):
-                quantize_xg(2 + s // 2)
+            if s % 2 == 1 and s + 3 < STEPS:
+                quantize_xg((s + 3) * STEP // CHUNK)
             if s >= 1:
-                gate_y(s - 1)
-            if s < steps:
+                finish_out(s - 1)
+            if s < STEPS:
                 second_stage(s)
-            if s in (3, 5, 7):
-                quantize_y(s - 3, 2)
-        quantize_y(steps - 2, 1)
-        quantize_y(steps - 1, 1)
+            if s % 2 == 1 and s >= 3:
+                quantize_out(s - 3, 2)
+        quantize_out(STEPS - 2, 1)
+        quantize_out(STEPS - 1, 1)
 
-        for q in range(4):
+        for q in range(QUADRANTS):
             queue = nc.sync if q % 2 == 0 else nc.scalar
             queue.dma_start(
-                out_2[0, 4 * q : 4 * q + 4, :].bitcast(I32), out_s[32 * q : 32 * q + 4, :].bitcast(I32)
+                out_2[0, SCALE_ROWS * q : SCALE_ROWS * (q + 1), :].bitcast(I32),
+                out_s[QUADRANT * q : QUADRANT * q + SCALE_ROWS, :].bitcast(I32),
             )

@@ -16,6 +16,8 @@ FP4X4 = mybir.dt.float4_e2m1fn_x4
 MULT = mybir.AluOpType.mult
 SIGMOID = mybir.ActivationFunctionType.Sigmoid
 
+ADD = mybir.AluOpType.add
+
 P = 128
 PACK = 4
 PASS = P * PACK
@@ -27,11 +29,9 @@ CUT = J // HEAD
 LINE = 4
 STEP = 128
 STEPS = J // STEP
-CHUNK = 256
-CHUNKS = J // CHUNK
 HALF = J // 2
-PICKS = [(0, CHUNK), (CHUNK, CHUNK), (HALF, HALF)]
-WG_PIECES = [(0, PASS // 2), (PASS // 2, PASS // 2), (PASS, PASS)]
+CHUNKS = [(0, STEP), (STEP, STEP), (2 * STEP, 2 * STEP), (HALF, HALF)]
+PIECE = PASS // 2
 LEAD = 2
 ALIGN = 64
 
@@ -45,51 +45,57 @@ def tile_list_sigm_mulP_kernel(
         ring = ctx.enter_context(tc.tile_pool(name="ring", bufs=3))
         psum = ctx.enter_context(tc.psum_pool(name="psum", bufs=1))
 
-        offsets = keep.tile([P, J // HEAD], U16, name="offsets")
-        nc.sync.dma_start(offsets[:], offs)
-
-        wu_s_raw = keep.tile([P, R], U8, name="wu_s_raw", align_bytes=ALIGN)
-        wd_s_raw = keep.tile([P, N], U8, name="wd_s_raw", align_bytes=ALIGN)
-        nc.gpsimd.memset(wu_s_raw[:].bitcast(I32), 0)
-        nc.gpsimd.memset(wd_s_raw[:].bitcast(I32), 0)
+        scales_raw = keep.tile([P, R], U8, name="scales_raw", align_bytes=ALIGN)
+        nc.vector.memset(scales_raw[:].bitcast(I32), 0)
 
         x_rows = xT.rearrange("(p i) t -> p i t", i=PACK)
         wg_rows = wg.rearrange("(p i) r -> p i r", i=PACK)
         g_rows = g.rearrange("(p t) j -> p t j", t=PACK)
         out_rows = out_0.rearrange("(p t) j -> p t j", t=PACK)
         out_words = out_1[0].rearrange("p j i -> p (j i)").bitcast(I32)
+        offsets = keep.tile([P, J // HEAD], U16, name="offsets")
         wu_raw = keep.tile([P, 2 * R], U8, name="wu_raw", align_bytes=ALIGN)
         planes = [keep.tile([P, T], F32, name=f"plane{i}") for i in range(PACK)]
         wgt_cut = keep.tile([P, CUT], F32, name="wgt_cut", align_bytes=ALIGN)
-        wg_raw = [keep.tile([P, PACK, width], F32, name=f"wg_raw{r0}") for r0, width in WG_PIECES]
+        wg_raw = [keep.tile([P, PACK, PIECE], F32, name=f"wg_raw{u}") for u in range(R // PIECE)]
         g_sb = [keep.tile([P, PACK, HALF], F32, name=f"g{half}") for half in range(2)]
         wd_raw = keep.tile([P, R_PASSES, N], I32, name="wd_raw")
 
+        def load_wg(u):
+            nc.sync.dma_start(wg_raw[u][:], wg_rows[:, :, u * PIECE : (u + 1) * PIECE])
+
         nc.sync.dma_start(wgt_cut[:], wgt[0:P:HEAD, :].rearrange("a (c j) -> a c j", j=CUT))
+        nc.sync.dma_start(offsets[:], offs)
         nc.sync.dma_start(wu_raw[:].bitcast(I32), wu_words[0].bitcast(I32))
         nc.sync.dma_start(planes[0][:], x_rows[:, 0, :])
+        nc.sync.dma_start(planes[1][:], x_rows[:, 1, :])
         for q in range(QUADRANTS):
             nc.sync.dma_start(
-                wu_s_raw[QUADRANT * q : QUADRANT * q + SCALE_ROWS, :].bitcast(I32),
+                scales_raw[QUADRANT * q : QUADRANT * q + SCALE_ROWS, :].bitcast(I32),
                 wu_scales[0, SCALE_ROWS * q : SCALE_ROWS * (q + 1), :].bitcast(I32),
             )
-        for i in range(1, PACK):
-            nc.sync.dma_start(planes[i][:], x_rows[:, i, :])
-        for piece, (r0, width) in zip(wg_raw, WG_PIECES):
-            nc.sync.dma_start(piece[:], wg_rows[:, :, r0 : r0 + width])
-        nc.sync.dma_start(wd_raw[:], wd_words.rearrange("b p n i -> p b (n i)").bitcast(I32))
+        nc.sync.dma_start(planes[2][:], x_rows[:, 2, :])
         for q in range(QUADRANTS):
             nc.sync.dma_start(
-                wd_s_raw[QUADRANT * q : QUADRANT * q + R_PASSES * SCALE_ROWS, :].bitcast(I32),
+                scales_raw[QUADRANT * q + SCALE_ROWS : QUADRANT * q + 3 * SCALE_ROWS, 0:N].bitcast(I32),
                 wd_scales[:, SCALE_ROWS * q : SCALE_ROWS * (q + 1), :].bitcast(I32),
             )
+        load_wg(0)
+        nc.sync.dma_start(planes[3][:], x_rows[:, 3, :])
+        load_wg(1)
+        load_wg(2)
+        load_wg(3)
+        nc.sync.dma_start(wd_raw[:], wd_words.rearrange("b p n i -> p b (n i)").bitcast(I32))
         for half in range(2):
             nc.sync.dma_start(g_sb[half][:], g_rows[:, :, half * HALF : (half + 1) * HALF])
+
+        warm = keep.tile([P, 1], F32, name="warm")
+        nc.scalar.activation(warm[:], wgt_cut[:, 0:1], SIGMOID)
 
         wgt_turned = keep.tile([P, CUT], F32, name="wgt_turned", align_bytes=ALIGN)
         for j0 in range(0, CUT, QUADRANT):
             nc.vector.transpose(wgt_turned[:, j0 : j0 + QUADRANT], wgt_cut[:, j0 : j0 + QUADRANT])
-        wgt_sb = []
+        wgt_sb = keep.tile([P, J], F32, name="wgt_sb", align_bytes=ALIGN)
         cuts = HALF // CUT
         for half in range(2):
             repeated = keep.tile([P, HALF], F32, name=f"wgt_repeated{half}", align_bytes=ALIGN)
@@ -98,27 +104,25 @@ def tile_list_sigm_mulP_kernel(
                 repeated[:].rearrange("p (c sa rep) -> p c sa rep", c=cuts, rep=HEAD),
                 source.unsqueeze(3).to_broadcast([P, cuts, CUT // HEAD, HEAD]),
             )
-            wgt_sb.append(keep.tile([P, HALF], F32, name=f"wgt{half}", align_bytes=ALIGN))
-            nc.vector.transpose(wgt_sb[half][:], repeated[:])
+            nc.vector.transpose(wgt_sb[:, half * HALF : (half + 1) * HALF], repeated[:])
 
         wu_codes = keep.tile([P, 2 * R], U8, name="wu_codes", align_bytes=ALIGN)
-        wu_s = keep.tile([P, R], U8, name="wu_s", align_bytes=ALIGN)
+        scales = keep.tile([P, R], U8, name="scales", align_bytes=ALIGN)
         wd_codes = keep.tile([P, R_PASSES * N], I32, name="wd_codes", align_bytes=ALIGN)
-        wd_s = keep.tile([P, N], U8, name="wd_s", align_bytes=ALIGN)
-        nc.vector.tensor_copy(
-            wu_codes[:].bitcast(U16).rearrange("p (b t m) -> p b t m", b=R_PASSES, t=PACK),
-            wu_raw[:].bitcast(U16).rearrange("p (b m t) -> p b t m", b=R_PASSES, t=PACK),
-        )
-        nc.vector.tensor_copy(
-            wu_s[:].rearrange("p (b t m) -> p b t m", b=R_PASSES, t=PACK),
-            wu_s_raw[:].rearrange("p (b m t) -> p b t m", b=R_PASSES, t=PACK),
-        )
+
+        def deal_wu():
+            nc.vector.tensor_copy(
+                wu_codes[:].bitcast(U16).rearrange("p (b t m) -> p b t m", b=R_PASSES, t=PACK),
+                wu_raw[:].bitcast(U16).rearrange("p (b m t) -> p b t m", b=R_PASSES, t=PACK),
+            )
+
+        def deal_scales():
+            nc.vector.tensor_copy(
+                scales[:].rearrange("p (b t m) -> p b t m", b=R_PASSES, t=PACK),
+                scales_raw[:].rearrange("p (b m t) -> p b t m", b=R_PASSES, t=PACK),
+            )
 
         def deal_wd():
-            nc.vector.tensor_copy(
-                wd_s[:].rearrange("p (t m) -> p t m", t=PACK),
-                wd_s_raw[:].rearrange("p (m t) -> p t m", t=PACK),
-            )
             nc.vector.tensor_copy(
                 wd_codes[:].rearrange("p (b t c e) -> p b c t e", b=R_PASSES, t=PACK, e=LINE),
                 wd_raw[:].rearrange("p b (c e t) -> p b c t e", t=PACK, e=LINE),
@@ -129,52 +133,63 @@ def tile_list_sigm_mulP_kernel(
         wg_bf = [keep.tile([P, PASS * PACK], BF16, name=f"wg_bf{b}", align_bytes=ALIGN) for b in range(R_PASSES)]
 
         def round_wg(copy, u):
-            r0, width = WG_PIECES[u]
-            b, m0 = divmod(r0 // PACK, P)
+            b, m0 = divmod(u * PIECE // PACK, P)
             copy(
-                wg_bf[b][:].rearrange("p (t m i) -> p m t i", t=PACK, i=PACK)[:, m0 : m0 + width // PACK],
-                wg_raw[u][:].rearrange("p i (m t) -> p m t i", t=PACK),
+                wg_bf[b][:].rearrange("p (t m i) -> p m i t", t=PACK, i=PACK)[:, m0 : m0 + PIECE // PACK],
+                wg_raw[u][:].rearrange("p i (m t) -> p m i t", t=PACK),
             )
 
         def quantize_wg(b):
             nc.vector.quantize_mx(out=wg_codes[b][:].bitcast(FP8X4), scales=wg_s[b][:], in_=wg_bf[b][:])
 
-        picked = [keep.tile([P, PACK, width], F32, name=f"picked{j0}") for j0, width in PICKS]
-        staging = keep.tile([P, CHUNK * PACK], BF16, name="staging", align_bytes=ALIGN)
-        xg_codes = [keep.tile([P, CHUNK], U32, name=f"xg_codes{c}", align_bytes=ALIGN) for c in range(CHUNKS)]
-        xg_s = [keep.tile([P, CHUNK], U8, name=f"xg_s{c}", align_bytes=ALIGN) for c in range(CHUNKS)]
+        picked = keep.tile([P, PACK, J], F32, name="picked")
+        xg_bf = keep.tile([P, J * PACK], BF16, name="xg_bf", align_bytes=ALIGN)
+        xg_codes = keep.tile([P, J], U32, name="xg_codes", align_bytes=ALIGN)
+        xg_s = keep.tile([P, J], U8, name="xg_s", align_bytes=ALIGN)
 
-        def gather(i, u):
-            j0, width = PICKS[u]
-            half, inside = divmod(j0, HALF)
+        def gather(i, j0, width):
             nc.vector.tensor_tensor(
-                picked[u][:, i, :],
+                picked[:, i, j0 : j0 + width],
                 planes[i][:].indirect(offsets[:, j0 // HEAD : (j0 + width) // HEAD]),
-                wgt_sb[half][:, inside : inside + width],
+                wgt_sb[:, j0 : j0 + width],
                 MULT,
             )
 
-        def interleave(dst, src):
-            for j0 in range(0, src.shape[2], STEP):
-                nc.scalar.copy(
-                    dst[:, j0 * PACK : (j0 + STEP) * PACK].rearrange("p (c e i) -> p c i e", e=LINE, i=PACK),
-                    src[:, :, j0 : j0 + STEP].rearrange("p i (c e) -> p c i e", e=LINE),
-                )
+        def round_on_gpsimd(dst, src):
+            nc.gpsimd.tensor_scalar(dst, src, 1.0, -0.0, MULT, ADD)
+
+        def interleave(copy, dst, src):
+            copy(
+                dst.rearrange("p (c e i) -> p c i e", e=LINE, i=PACK),
+                src.rearrange("p i (c e) -> p c i e", e=LINE),
+            )
+
+        def round_xg(s):
+            interleave(
+                nc.scalar.copy,
+                xg_bf[:, s * STEP * PACK : (s + 1) * STEP * PACK],
+                picked[:, :, s * STEP : (s + 1) * STEP],
+            )
 
         def quantize_xg(c):
-            u = min(c, len(PICKS) - 1)
-            inside = c * CHUNK - PICKS[u][0]
-            interleave(staging[:], picked[u][:, :, inside : inside + CHUNK])
-            nc.vector.quantize_mx(out=xg_codes[c][:].bitcast(FP8X4), scales=xg_s[c][:], in_=staging[:])
+            j0, width = CHUNKS[c]
+            for s in range(j0 // STEP, (j0 + width) // STEP):
+                round_xg(s)
+            nc.vector.quantize_mx(
+                out=xg_codes[:, j0 : j0 + width].bitcast(FP8X4),
+                scales=xg_s[:, j0 : j0 + width],
+                in_=xg_bf[:, j0 * PACK : (j0 + width) * PACK],
+            )
 
         out_codes = keep.tile([P, J], U32, name="out_codes", align_bytes=ALIGN)
         out_s = keep.tile([P, J], U8, name="out_s", align_bytes=ALIGN)
-        h_bf, y_ps, y_bf = {}, {}, {}
+        y_bf = keep.tile([P, J * PACK], BF16, name="y_bf", align_bytes=ALIGN)
+        h_bf, y_ps = {}, {}
 
         def first_stage(s, b):
-            c, inside = divmod(s * STEP, CHUNK)
-            rhs = xg_codes[c][:, inside : inside + STEP].bitcast(FP8X4)
-            rhs_scale = xg_s[c][:, inside : inside + STEP]
+            tokens = slice(s * STEP, (s + 1) * STEP)
+            rhs = xg_codes[:, tokens].bitcast(FP8X4)
+            rhs_scale = xg_s[:, tokens]
             ga = psum.tile([P, PACK, STEP], F32, name="ga", bufs=3)
             ub = psum.tile([P, PACK, STEP], F32, name="ub", bufs=3)
             for t in range(PACK):
@@ -187,17 +202,14 @@ def tile_list_sigm_mulP_kernel(
                 col = b * PASS + t * P
                 nc.tensor.matmul_mx(
                     out=ub[:, t, :], lhsT=wu_codes[:, 2 * col : 2 * (col + P)].bitcast(FP4X4),
-                    lhsT_scale=wu_s[:, col : col + P],
+                    lhsT_scale=scales[:, col : col + P],
                     rhs=rhs, rhs_scale=rhs_scale, start=True, stop=True,
                 )
-            if (s, b) == (0, 0):
-                gate = staging[:].bitcast(F32).rearrange("p (j t) -> p j t", t=PACK)
-            else:
-                gate = ring.tile([P, STEP, PACK], F32, name="gate")[:]
-            nc.scalar.activation(gate, ga[:].rearrange("p t j -> p j t"), SIGMOID)
+            gate = ring.tile([P, STEP, PACK], F32, name="gate")
+            nc.scalar.activation(gate[:], ga[:].rearrange("p t j -> p j t"), SIGMOID)
             if b == 0:
                 h_bf[s] = ring.tile([P, R_PASSES, STEP, PACK], BF16, name="h_bf", align_bytes=ALIGN, bufs=4)
-            nc.vector.tensor_tensor(h_bf[s][:, b, :, :], ub[:].rearrange("p t j -> p j t"), gate, MULT)
+            nc.vector.tensor_tensor(h_bf[s][:, b, :, :], ub[:].rearrange("p t j -> p j t"), gate[:], MULT)
 
         def second_stage(s):
             h_codes = ring.tile([P, R_PASSES * STEP], U32, name="h_codes", align_bytes=ALIGN)
@@ -212,50 +224,54 @@ def tile_list_sigm_mulP_kernel(
                     tokens = slice(b * STEP, (b + 1) * STEP)
                     nc.tensor.matmul_mx(
                         out=y_ps[s][:, t, :], lhsT=wd_codes[:, col : col + P].bitcast(FP8X4),
-                        lhsT_scale=wd_s[SCALE_ROWS * b : P, t * P : (t + 1) * P],
+                        lhsT_scale=scales[SCALE_ROWS * (b + 1) : P, t * P : (t + 1) * P],
                         rhs=h_codes[:, tokens].bitcast(FP8X4), rhs_scale=h_s[:, tokens],
                         start=(b == 0), stop=(b == R_PASSES - 1),
                     )
 
-        def finish_out(s):
+        def finish_out(s, copy):
             half, inside = divmod(s * STEP, HALF)
             result = ring.tile([P, PACK, STEP], F32, name="result", bufs=4)
             nc.vector.tensor_tensor(result[:], y_ps[s][:], g_sb[half][:, :, inside : inside + STEP], MULT)
             nc.sync.dma_start(out_rows[:, :, s * STEP : (s + 1) * STEP], result[:])
-            pair, member = divmod(s, 2)
-            if member == 0:
-                y_bf[pair] = ring.tile([P, 2, STEP * PACK], BF16, name="y_bf", align_bytes=ALIGN)
-            interleave(y_bf[pair][:, member, :], result[:])
+            interleave(copy, y_bf[:, s * STEP * PACK : (s + 1) * STEP * PACK], result[:])
 
         def quantize_out(first, count):
-            pair, member = divmod(first, 2)
             tokens = slice(first * STEP, (first + count) * STEP)
-            rounded = y_bf[pair][:, member : member + count, :].rearrange("p s x -> p (s x)")
+            rounded = y_bf[:, first * STEP * PACK : (first + count) * STEP * PACK]
             nc.vector.quantize_mx(out=out_codes[:, tokens].bitcast(FP8X4), scales=out_s[:, tokens], in_=rounded)
             nc.sync.dma_start(out_words[:, tokens], out_codes[:, tokens].bitcast(I32))
 
-        for i in range(PACK):
-            for u in range(len(PICKS)):
-                gather(i, u)
-        quantize_xg(0)
+        deal_wu()
+        for half in range(2):
+            gather(0, half * HALF, HALF)
+        gather(1, 0, J)
+        gather(2, 0, J)
+        deal_scales()
         round_wg(nc.scalar.copy, 0)
-        round_wg(nc.vector.tensor_copy, 1)
+        for c, (j0, width) in enumerate(CHUNKS):
+            gather(PACK - 1, j0, width)
+            if c == 1:
+                quantize_xg(0)
+        round_wg(nc.scalar.copy, 1)
         quantize_wg(0)
-        for s in range(LEAD):
-            first_stage(s, 0)
-        round_wg(nc.vector.tensor_copy, 2)
-        quantize_wg(1)
         quantize_xg(1)
+        first_stage(0, 0)
+        round_wg(nc.scalar.copy, 2)
+        round_wg(nc.vector.tensor_copy, 3)
+        quantize_wg(1)
+        first_stage(1, 0)
         deal_wd()
+        quantize_xg(2)
         for s in range(STEPS + 1):
             if LEAD <= s < STEPS:
                 first_stage(s, 0)
             if s < STEPS:
                 first_stage(s, 1)
-            if s % 2 == 1 and s + 3 < STEPS:
-                quantize_xg((s + 3) * STEP // CHUNK)
+            if s == 2:
+                quantize_xg(3)
             if s >= 1:
-                finish_out(s - 1)
+                finish_out(s - 1, nc.scalar.copy)
             if s < STEPS:
                 second_stage(s)
             if s % 2 == 1 and s >= 3:

@@ -16,7 +16,6 @@ FP4X4 = mybir.dt.float4_e2m1fn_x4
 MULT = mybir.AluOpType.mult
 SIGMOID = mybir.ActivationFunctionType.Sigmoid
 
-ADD = mybir.AluOpType.add
 
 P = 128
 PACK = 4
@@ -30,7 +29,9 @@ LINE = 4
 STEP = 128
 STEPS = J // STEP
 HALF = J // 2
-CHUNKS = [(0, STEP), (STEP, STEP), (2 * STEP, 2 * STEP), (HALF, HALF)]
+CHUNKS = [(0, 2 * STEP), (2 * STEP, 2 * STEP), (HALF, HALF)]
+GROUPS = [(0, 2), (2, 2), (4, 1), (5, 1), (6, 1), (7, 1)]
+GROUP_OF = {first + member: (group, member) for group, (first, steps) in enumerate(GROUPS) for member in range(steps)}
 PIECE = PASS // 2
 LEAD = 2
 ALIGN = 64
@@ -155,9 +156,6 @@ def tile_list_sigm_mulP_kernel(
                 MULT,
             )
 
-        def round_on_gpsimd(dst, src):
-            nc.gpsimd.tensor_scalar(dst, src, 1.0, -0.0, MULT, ADD)
-
         def interleave(copy, dst, src):
             copy(
                 dst.rearrange("p (c e i) -> p c i e", e=LINE, i=PACK),
@@ -205,36 +203,55 @@ def tile_list_sigm_mulP_kernel(
                     lhsT_scale=scales[:, col : col + P],
                     rhs=rhs, rhs_scale=rhs_scale, start=True, stop=True,
                 )
-            gate = ring.tile([P, STEP, PACK], F32, name="gate")
+            gate = ring.tile([P, STEP, PACK], F32, name="gate", bufs=4)
             nc.scalar.activation(gate[:], ga[:].rearrange("p t j -> p j t"), SIGMOID)
-            if b == 0:
-                h_bf[s] = ring.tile([P, R_PASSES, STEP, PACK], BF16, name="h_bf", align_bytes=ALIGN, bufs=4)
-            nc.vector.tensor_tensor(h_bf[s][:, b, :, :], ub[:].rearrange("p t j -> p j t"), gate[:], MULT)
+            group, member = GROUP_OF[s]
+            if (b, member) == (0, 0):
+                steps = GROUPS[group][1]
+                h_bf[group] = ring.tile([P, R_PASSES, steps, STEP, PACK], BF16, name="h_bf", align_bytes=ALIGN)
+            nc.vector.tensor_tensor(h_bf[group][:, b, member], ub[:].rearrange("p t j -> p j t"), gate[:], MULT)
 
-        def second_stage(s):
-            h_codes = ring.tile([P, R_PASSES * STEP], U32, name="h_codes", align_bytes=ALIGN)
-            h_s = ring.tile([P, R_PASSES * STEP], U8, name="h_s", align_bytes=ALIGN)
-            nc.vector.quantize_mx(
-                out=h_codes[:].bitcast(FP8X4), scales=h_s[:], in_=h_bf[s][:].rearrange("p b j t -> p (b j t)")
-            )
-            y_ps[s] = psum.tile([P, PACK, STEP], F32, name="y_ps", bufs=2)
-            for t in range(PACK):
-                for b in range(R_PASSES):
-                    col = b * N + t * P
-                    tokens = slice(b * STEP, (b + 1) * STEP)
-                    nc.tensor.matmul_mx(
-                        out=y_ps[s][:, t, :], lhsT=wd_codes[:, col : col + P].bitcast(FP8X4),
-                        lhsT_scale=scales[SCALE_ROWS * (b + 1) : P, t * P : (t + 1) * P],
-                        rhs=h_codes[:, tokens].bitcast(FP8X4), rhs_scale=h_s[:, tokens],
-                        start=(b == 0), stop=(b == R_PASSES - 1),
+        def second_stage(group, first, count):
+            steps = GROUPS[group][1]
+            width = steps * STEP
+            h_codes = ring.tile([P, count * width], U32, name="h_codes", align_bytes=ALIGN)
+            h_s = ring.tile([P, count * width], U8, name="h_s", align_bytes=ALIGN)
+            rounded = h_bf[group][:, first : first + count].rearrange("p b s j t -> p (b s j t)")
+            nc.vector.quantize_mx(out=h_codes[:].bitcast(FP8X4), scales=h_s[:], in_=rounded)
+            slices = PACK // steps
+            if first == 0:
+                y_ps[group] = [psum.tile([P, slices, width], F32, name="y_ps", bufs=2) for bank in range(steps)]
+            for bank in range(steps):
+                for b in range(first, first + count):
+                    for u in range(slices):
+                        t = bank * slices + u
+                        col = b * N + t * P
+                        tokens = slice((b - first) * width, (b - first + 1) * width)
+                        nc.tensor.matmul_mx(
+                            out=y_ps[group][bank][:, u, :], lhsT=wd_codes[:, col : col + P].bitcast(FP8X4),
+                            lhsT_scale=scales[SCALE_ROWS * (b + 1) : P, t * P : (t + 1) * P],
+                            rhs=h_codes[:, tokens].bitcast(FP8X4), rhs_scale=h_s[:, tokens],
+                            start=(b == 0 and u == 0), stop=(b == R_PASSES - 1 and u == slices - 1),
+                        )
+
+        def finish_out(group, parts=1):
+            first, steps = GROUPS[group]
+            slices = PACK // steps
+            result = ring.tile([P, PACK, steps * STEP], F32, name="result")
+            width = steps * STEP // parts
+            for j0 in range(0, steps * STEP, width):
+                half, inside = divmod(first * STEP + j0, HALF)
+                for bank in range(steps):
+                    rows = slice(bank * slices, (bank + 1) * slices)
+                    nc.vector.tensor_tensor(
+                        result[:, rows, j0 : j0 + width], y_ps[group][bank][:, :, j0 : j0 + width],
+                        g_sb[half][:, rows, inside : inside + width], MULT,
                     )
-
-        def finish_out(s, copy):
-            half, inside = divmod(s * STEP, HALF)
-            result = ring.tile([P, PACK, STEP], F32, name="result", bufs=4)
-            nc.vector.tensor_tensor(result[:], y_ps[s][:], g_sb[half][:, :, inside : inside + STEP], MULT)
-            nc.sync.dma_start(out_rows[:, :, s * STEP : (s + 1) * STEP], result[:])
-            interleave(copy, y_bf[:, s * STEP * PACK : (s + 1) * STEP * PACK], result[:])
+                for j1 in range(j0, j0 + width, STEP):
+                    piece = min(width, STEP)
+                    at = (first * STEP + j1) * PACK
+                    interleave(nc.scalar.copy, y_bf[:, at : at + piece * PACK], result[:, :, j1 : j1 + piece])
+            nc.sync.dma_start(out_rows[:, :, first * STEP : (first + steps) * STEP], result[:])
 
         def quantize_out(first, count):
             tokens = slice(first * STEP, (first + count) * STEP)
@@ -249,33 +266,38 @@ def tile_list_sigm_mulP_kernel(
         gather(2, 0, J)
         deal_scales()
         round_wg(nc.scalar.copy, 0)
-        for c, (j0, width) in enumerate(CHUNKS):
-            gather(PACK - 1, j0, width)
-            if c == 1:
-                quantize_xg(0)
+        gather(PACK - 1, 0, CHUNKS[0][1])
+        gather(PACK - 1, CHUNKS[0][1], J - CHUNKS[0][1])
+        quantize_xg(0)
         round_wg(nc.scalar.copy, 1)
         quantize_wg(0)
-        quantize_xg(1)
         first_stage(0, 0)
         round_wg(nc.scalar.copy, 2)
         round_wg(nc.vector.tensor_copy, 3)
-        quantize_wg(1)
         first_stage(1, 0)
+        quantize_wg(1)
         deal_wd()
-        quantize_xg(2)
-        for s in range(STEPS + 1):
-            if LEAD <= s < STEPS:
-                first_stage(s, 0)
-            if s < STEPS:
+        quantize_xg(1)
+        for group, (first, steps) in enumerate(GROUPS[:-1]):
+            for s in range(first, first + steps):
+                if s >= LEAD:
+                    first_stage(s, 0)
                 first_stage(s, 1)
-            if s == 2:
-                quantize_xg(3)
-            if s >= 1:
-                finish_out(s - 1, nc.scalar.copy)
-            if s < STEPS:
-                second_stage(s)
-            if s % 2 == 1 and s >= 3:
-                quantize_out(s - 3, 2)
+            if group == 1:
+                quantize_xg(2)
+            if group >= 1:
+                finish_out(group - 1)
+            second_stage(group, 0, R_PASSES)
+            if group == 3:
+                quantize_out(0, 4)
+        last = len(GROUPS) - 1
+        first_stage(STEPS - 1, 0)
+        quantize_out(4, 2)
+        first_stage(STEPS - 1, 1)
+        second_stage(last, 0, 1)
+        second_stage(last, 1, 1)
+        finish_out(last - 1)
+        finish_out(last, parts=2)
         quantize_out(STEPS - 2, 1)
         quantize_out(STEPS - 1, 1)
 

@@ -70,10 +70,9 @@ def tile_list_sigm_mulP_kernel(
         nc.sync.dma_start(wu_raw[:].bitcast(I32), wu_words[0].bitcast(I32))
         nc.sync.dma_start(planes[0][:], x_rows[:, 0, :])
         nc.sync.dma_start(planes[1][:], x_rows[:, 1, :])
-        for q in range(QUADRANTS):
+        for row in range(SCALE_ROWS):
             nc.sync.dma_start(
-                scales_raw[QUADRANT * q : QUADRANT * q + SCALE_ROWS, :].bitcast(I32),
-                wu_scales[0, SCALE_ROWS * q : SCALE_ROWS * (q + 1), :].bitcast(I32),
+                scales_raw[row:P:QUADRANT, :].bitcast(I32), wu_scales[0, row::SCALE_ROWS, :].bitcast(I32)
             )
         nc.sync.dma_start(planes[2][:], x_rows[:, 2, :])
         for q in range(QUADRANTS):
@@ -125,8 +124,8 @@ def tile_list_sigm_mulP_kernel(
 
         def deal_wd():
             nc.vector.tensor_copy(
-                wd_codes[:].rearrange("p (b t c e) -> p b c t e", b=R_PASSES, t=PACK, e=LINE),
-                wd_raw[:].rearrange("p b (c e t) -> p b c t e", t=PACK, e=LINE),
+                wd_codes[:].rearrange("p (b t m) -> p b m t", b=R_PASSES, t=PACK),
+                wd_raw[:].rearrange("p b (m t) -> p b m t", t=PACK),
             )
 
         wg_codes = [keep.tile([P, PASS], U32, name=f"wg_codes{b}", align_bytes=ALIGN) for b in range(R_PASSES)]
@@ -259,6 +258,13 @@ def tile_list_sigm_mulP_kernel(
             nc.vector.quantize_mx(out=out_codes[:, tokens].bitcast(FP8X4), scales=out_s[:, tokens], in_=rounded)
             nc.sync.dma_start(out_words[:, tokens], out_codes[:, tokens].bitcast(I32))
 
+        def store_scales(first, count, queues):
+            tokens = slice(first * STEP, (first + count) * STEP)
+            for row in range(SCALE_ROWS):
+                queues[row % len(queues)].dma_start(
+                    out_2[0, row::SCALE_ROWS, tokens].bitcast(I32), out_s[row:P:QUADRANT, tokens].bitcast(I32)
+                )
+
         deal_wu()
         for half in range(2):
             gather(0, half * HALF, HALF)
@@ -280,9 +286,11 @@ def tile_list_sigm_mulP_kernel(
         quantize_xg(1)
         for group, (first, steps) in enumerate(GROUPS[:-1]):
             for s in range(first, first + steps):
-                if s >= LEAD:
+                if s > LEAD:
                     first_stage(s, 0)
                 first_stage(s, 1)
+            if group == 0:
+                first_stage(LEAD, 0)
             if group == 1:
                 quantize_xg(2)
             if group >= 1:
@@ -296,14 +304,9 @@ def tile_list_sigm_mulP_kernel(
         first_stage(STEPS - 1, 1)
         second_stage(last, 0, 1)
         second_stage(last, 1, 1)
+        store_scales(0, STEPS - 2, [nc.sync])
         finish_out(last - 1)
         finish_out(last, parts=2)
         quantize_out(STEPS - 2, 1)
         quantize_out(STEPS - 1, 1)
-
-        for q in range(QUADRANTS):
-            queue = nc.sync if q % 2 == 0 else nc.scalar
-            queue.dma_start(
-                out_2[0, SCALE_ROWS * q : SCALE_ROWS * (q + 1), :].bitcast(I32),
-                out_s[QUADRANT * q : QUADRANT * q + SCALE_ROWS, :].bitcast(I32),
-            )
+        store_scales(STEPS - 2, 2, [nc.scalar, nc.sync])

@@ -14,6 +14,7 @@ U8 = mybir.dt.uint8
 FP8X4 = mybir.dt.float8_e4m3fn_x4
 FP4X4 = mybir.dt.float4_e2m1fn_x4
 MULT = mybir.AluOpType.mult
+ADD = mybir.AluOpType.add
 SIGMOID = mybir.ActivationFunctionType.Sigmoid
 
 
@@ -32,6 +33,8 @@ HALF = J // 2
 CHUNKS = [(0, 2 * STEP), (2 * STEP, 2 * STEP), (HALF, HALF)]
 GROUPS = [(0, 2), (2, 2), (4, 1), (5, 1), (6, 1), (7, 1)]
 GROUP_OF = {first + member: (group, member) for group, (first, steps) in enumerate(GROUPS) for member in range(steps)}
+ON_GPSIMD = (0, 1, 2, 4)
+STAGED_AT = {1: 0, 2: 2, 3: 4}
 PIECE = PASS // 2
 LEAD = 2
 ALIGN = 64
@@ -181,7 +184,7 @@ def tile_list_sigm_mulP_kernel(
         out_codes = keep.tile([P, J], U32, name="out_codes", align_bytes=ALIGN)
         out_s = keep.tile([P, J], U8, name="out_s", align_bytes=ALIGN)
         y_bf = keep.tile([P, J * PACK], BF16, name="y_bf", align_bytes=ALIGN)
-        h_bf, y_ps = {}, {}
+        h_bf, y_ps, results = {}, {}, {}
 
         def first_stage(s, b):
             tokens = slice(s * STEP, (s + 1) * STEP)
@@ -207,7 +210,13 @@ def tile_list_sigm_mulP_kernel(
             group, member = GROUP_OF[s]
             if (b, member) == (0, 0):
                 steps = GROUPS[group][1]
-                h_bf[group] = ring.tile([P, R_PASSES, steps, STEP, PACK], BF16, name="h_bf", align_bytes=ALIGN)
+                if group in STAGED_AT:
+                    at = STAGED_AT[group] * STEP * PACK
+                    h_bf[group] = y_bf[:, at : at + R_PASSES * steps * STEP * PACK].rearrange(
+                        "p (b s j t) -> p b s j t", b=R_PASSES, s=steps, t=PACK
+                    )
+                else:
+                    h_bf[group] = ring.tile([P, R_PASSES, steps, STEP, PACK], BF16, name="h_bf", align_bytes=ALIGN)
             nc.vector.tensor_tensor(h_bf[group][:, b, member], ub[:].rearrange("p t j -> p j t"), gate[:], MULT)
 
         def second_stage(group, first, count):
@@ -246,11 +255,23 @@ def tile_list_sigm_mulP_kernel(
                         result[:, rows, j0 : j0 + width], y_ps[group][bank][:, :, j0 : j0 + width],
                         g_sb[half][:, rows, inside : inside + width], MULT,
                     )
-                for j1 in range(j0, j0 + width, STEP):
-                    piece = min(width, STEP)
-                    at = (first * STEP + j1) * PACK
-                    interleave(nc.scalar.copy, y_bf[:, at : at + piece * PACK], result[:, :, j1 : j1 + piece])
+                if group + 1 not in STAGED_AT:
+                    at = (first * STEP + j0) * PACK
+                    interleave(nc.scalar.copy, y_bf[:, at : at + width * PACK], result[:, :, j0 : j0 + width])
             nc.sync.dma_start(out_rows[:, :, first * STEP : (first + steps) * STEP], result[:])
+            results[group] = result
+
+        def round_out(group):
+            first, steps = GROUPS[group]
+            for s in range(first, first + steps):
+                dst = y_bf[:, s * STEP * PACK : (s + 1) * STEP * PACK]
+                src = results[group][:, :, (s - first) * STEP : (s - first + 1) * STEP]
+                if s in ON_GPSIMD:
+                    nc.gpsimd.tensor_scalar(
+                        dst.rearrange("p (j t) -> p j t", t=PACK), src.rearrange("p t j -> p j t"), 1.0, 0.0, MULT, ADD
+                    )
+                else:
+                    interleave(nc.scalar.copy, dst, src)
 
         def quantize_out(first, count):
             tokens = slice(first * STEP, (first + count) * STEP)
@@ -296,6 +317,8 @@ def tile_list_sigm_mulP_kernel(
             if group >= 1:
                 finish_out(group - 1)
             second_stage(group, 0, R_PASSES)
+            if group in STAGED_AT:
+                round_out(group - 1)
             if group == 3:
                 quantize_out(0, 4)
         last = len(GROUPS) - 1

@@ -30,11 +30,13 @@ LINE = 4
 STEP = 128
 STEPS = J // STEP
 HALF = J // 2
-CHUNKS = [(0, 2 * STEP), (2 * STEP, 2 * STEP), (HALF, HALF)]
+CHUNK = 2 * STEP
+CHUNKS = [(j0, CHUNK) for j0 in range(0, J, CHUNK)]
 GROUPS = [(0, 2), (2, 2), (4, 1), (5, 1), (6, 1), (7, 1)]
 GROUP_OF = {first + member: (group, member) for group, (first, steps) in enumerate(GROUPS) for member in range(steps)}
-ON_GPSIMD = (0, 1, 2, 4)
-STAGED_AT = {1: 0, 2: 2, 3: 4}
+ON_GPSIMD = ()
+STAGED_AT = {}
+GATE_TAG = {(1, 0): "xg2", (1, 1): "wd_codes"}
 PIECE = PASS // 2
 LEAD = 2
 ALIGN = 64
@@ -78,10 +80,10 @@ def tile_list_sigm_mulP_kernel(
                 scales_raw[row:P:QUADRANT, :].bitcast(I32), wu_scales[0, row::SCALE_ROWS, :].bitcast(I32)
             )
         nc.sync.dma_start(planes[2][:], x_rows[:, 2, :])
-        for q in range(QUADRANTS):
+        for row in range(SCALE_ROWS):
             nc.sync.dma_start(
-                scales_raw[QUADRANT * q + SCALE_ROWS : QUADRANT * q + 3 * SCALE_ROWS, 0:N].bitcast(I32),
-                wd_scales[:, SCALE_ROWS * q : SCALE_ROWS * (q + 1), :].bitcast(I32),
+                scales_raw[SCALE_ROWS + row : P : QUADRANT, :].bitcast(I32).rearrange("q (b n) -> q b n", b=R_PASSES),
+                wd_scales[:, row::SCALE_ROWS, :].bitcast(I32).rearrange("b q n -> q b n"),
             )
         load_wg(0)
         nc.sync.dma_start(planes[3][:], x_rows[:, 3, :])
@@ -111,7 +113,7 @@ def tile_list_sigm_mulP_kernel(
 
         wu_codes = keep.tile([P, 2 * R], U8, name="wu_codes", align_bytes=ALIGN)
         scales = keep.tile([P, R], U8, name="scales", align_bytes=ALIGN)
-        wd_codes = keep.tile([P, R_PASSES * N], I32, name="wd_codes", align_bytes=ALIGN)
+        dealt = {}
 
         def deal_wu():
             nc.vector.tensor_copy(
@@ -126,8 +128,9 @@ def tile_list_sigm_mulP_kernel(
             )
 
         def deal_wd():
+            dealt["wd"] = keep.tile([P, R_PASSES * N], I32, name="wd_codes", align_bytes=ALIGN)
             nc.vector.tensor_copy(
-                wd_codes[:].rearrange("p (b t m) -> p b m t", b=R_PASSES, t=PACK),
+                dealt["wd"][:].rearrange("p (b t m) -> p b m t", b=R_PASSES, t=PACK),
                 wd_raw[:].rearrange("p b (m t) -> p b m t", t=PACK),
             )
 
@@ -146,7 +149,9 @@ def tile_list_sigm_mulP_kernel(
             nc.vector.quantize_mx(out=wg_codes[b][:].bitcast(FP8X4), scales=wg_s[b][:], in_=wg_bf[b][:])
 
         picked = keep.tile([P, PACK, J], F32, name="picked")
-        xg_bf = keep.tile([P, J * PACK], BF16, name="xg_bf", align_bytes=ALIGN)
+        staging = keep.tile([P, CHUNK * PACK], BF16, name="staging", align_bytes=ALIGN)
+        first_h = keep.tile([P, R_PASSES * CHUNK * PACK], BF16, name="first_h", align_bytes=ALIGN)
+        xg_bf = {0: staging[:], 1: wg_bf[1][:, 0 : CHUNK * PACK], 3: first_h[:, 0 : CHUNK * PACK]}
         xg_codes = keep.tile([P, J], U32, name="xg_codes", align_bytes=ALIGN)
         xg_s = keep.tile([P, J], U8, name="xg_s", align_bytes=ALIGN)
 
@@ -164,114 +169,125 @@ def tile_list_sigm_mulP_kernel(
                 src.rearrange("p i (c e) -> p c i e", e=LINE),
             )
 
-        def round_xg(s):
-            interleave(
-                nc.scalar.copy,
-                xg_bf[:, s * STEP * PACK : (s + 1) * STEP * PACK],
-                picked[:, :, s * STEP : (s + 1) * STEP],
+        def round_on_gpsimd(dst, src):
+            nc.gpsimd.tensor_scalar(
+                dst.rearrange("p (j t) -> p j t", t=PACK), src.rearrange("p t j -> p j t"), 1.0, 0.0, MULT, ADD
             )
+
+        def round_xg(c):
+            j0, width = CHUNKS[c]
+            if c == 2:
+                late = keep.tile([P, CHUNK * PACK], BF16, name="xg2", align_bytes=ALIGN)
+                xg_bf[c] = late[:]
+            if c % 2 == 1:
+                round_on_gpsimd(xg_bf[c], picked[:, :, j0 : j0 + width])
+            else:
+                for at in range(0, width, STEP):
+                    interleave(nc.scalar.copy, xg_bf[c][:, at * PACK : (at + STEP) * PACK], picked[:, :, j0 + at : j0 + at + STEP])
 
         def quantize_xg(c):
             j0, width = CHUNKS[c]
-            for s in range(j0 // STEP, (j0 + width) // STEP):
-                round_xg(s)
             nc.vector.quantize_mx(
-                out=xg_codes[:, j0 : j0 + width].bitcast(FP8X4),
-                scales=xg_s[:, j0 : j0 + width],
-                in_=xg_bf[:, j0 * PACK : (j0 + width) * PACK],
+                out=xg_codes[:, j0 : j0 + width].bitcast(FP8X4), scales=xg_s[:, j0 : j0 + width], in_=xg_bf[c]
             )
 
         out_codes = keep.tile([P, J], U32, name="out_codes", align_bytes=ALIGN)
         out_s = keep.tile([P, J], U8, name="out_s", align_bytes=ALIGN)
         y_bf = keep.tile([P, J * PACK], BF16, name="y_bf", align_bytes=ALIGN)
-        h_bf, y_ps, results = {}, {}, {}
+        gates, h_bf, h_mx, y_ps, results, emptied = {}, {}, {}, {}, {}, {}
 
-        def first_stage(s, b):
+        def make_gate(s, b):
             tokens = slice(s * STEP, (s + 1) * STEP)
-            rhs = xg_codes[:, tokens].bitcast(FP8X4)
-            rhs_scale = xg_s[:, tokens]
             ga = psum.tile([P, PACK, STEP], F32, name="ga", bufs=3)
-            ub = psum.tile([P, PACK, STEP], F32, name="ub", bufs=3)
             for t in range(PACK):
                 cols = slice(t * P, (t + 1) * P)
                 nc.tensor.matmul_mx(
                     out=ga[:, t, :], lhsT=wg_codes[b][:, cols].bitcast(FP8X4), lhsT_scale=wg_s[b][:, cols],
-                    rhs=rhs, rhs_scale=rhs_scale, start=True, stop=True,
+                    rhs=xg_codes[:, tokens].bitcast(FP8X4), rhs_scale=xg_s[:, tokens], start=True, stop=True,
                 )
+            if (s, b) in GATE_TAG:
+                gates[s, b] = keep.tile([P, STEP, PACK], F32, name=GATE_TAG[s, b], align_bytes=ALIGN)
+            else:
+                gates[s, b] = ring.tile([P, STEP, PACK], F32, name="gate", bufs=6)
+            nc.scalar.activation(gates[s, b][:], ga[:].rearrange("p t j -> p j t"), SIGMOID)
+
+        def make_h(s, b):
+            tokens = slice(s * STEP, (s + 1) * STEP)
+            ub = psum.tile([P, PACK, STEP], F32, name="ub", bufs=3)
             for t in range(PACK):
                 col = b * PASS + t * P
                 nc.tensor.matmul_mx(
                     out=ub[:, t, :], lhsT=wu_codes[:, 2 * col : 2 * (col + P)].bitcast(FP4X4),
                     lhsT_scale=scales[:, col : col + P],
-                    rhs=rhs, rhs_scale=rhs_scale, start=True, stop=True,
+                    rhs=xg_codes[:, tokens].bitcast(FP8X4), rhs_scale=xg_s[:, tokens], start=True, stop=True,
                 )
-            gate = ring.tile([P, STEP, PACK], F32, name="gate", bufs=4)
-            nc.scalar.activation(gate[:], ga[:].rearrange("p t j -> p j t"), SIGMOID)
+            gate = gates[s, b]
             group, member = GROUP_OF[s]
             if (b, member) == (0, 0):
                 steps = GROUPS[group][1]
-                if group in STAGED_AT:
-                    at = STAGED_AT[group] * STEP * PACK
-                    h_bf[group] = y_bf[:, at : at + R_PASSES * steps * STEP * PACK].rearrange(
-                        "p (b s j t) -> p b s j t", b=R_PASSES, s=steps, t=PACK
-                    )
+                if group == 0:
+                    h_bf[group] = first_h[:].rearrange("p (b s j t) -> p b s j t", b=R_PASSES, s=steps, t=PACK)
                 else:
-                    h_bf[group] = ring.tile([P, R_PASSES, steps, STEP, PACK], BF16, name="h_bf", align_bytes=ALIGN)
+                    h_tile = keep.tile([P, R_PASSES, steps, STEP, PACK], BF16, name=f"h{group}", align_bytes=ALIGN)
+                    h_bf[group] = h_tile[:]
             nc.vector.tensor_tensor(h_bf[group][:, b, member], ub[:].rearrange("p t j -> p j t"), gate[:], MULT)
 
-        def second_stage(group, first, count):
-            steps = GROUPS[group][1]
-            width = steps * STEP
+        def quantize_h(group, first=0, count=R_PASSES):
+            width = GROUPS[group][1] * STEP
             h_codes = ring.tile([P, count * width], U32, name="h_codes", align_bytes=ALIGN)
             h_s = ring.tile([P, count * width], U8, name="h_s", align_bytes=ALIGN)
             rounded = h_bf[group][:, first : first + count].rearrange("p b s j t -> p (b s j t)")
             nc.vector.quantize_mx(out=h_codes[:].bitcast(FP8X4), scales=h_s[:], in_=rounded)
-            slices = PACK // steps
-            if first == 0:
-                y_ps[group] = [psum.tile([P, slices, width], F32, name="y_ps", bufs=2) for bank in range(steps)]
-            for bank in range(steps):
+            h_mx[group, first] = (h_codes, h_s)
+
+        def second_stage(group, first=0, count=R_PASSES):
+            step0, steps = GROUPS[group]
+            width = steps * STEP
+            h_codes, h_s = h_mx[group, first]
+            for member in range(steps):
+                s = step0 + member
+                if first == 0:
+                    y_ps[s] = psum.tile([P, PACK, STEP], F32, name="y_ps", bufs=2)
                 for b in range(first, first + count):
-                    for u in range(slices):
-                        t = bank * slices + u
+                    at = (b - first) * width + member * STEP
+                    for t in range(PACK):
                         col = b * N + t * P
-                        tokens = slice((b - first) * width, (b - first + 1) * width)
                         nc.tensor.matmul_mx(
-                            out=y_ps[group][bank][:, u, :], lhsT=wd_codes[:, col : col + P].bitcast(FP8X4),
-                            lhsT_scale=scales[SCALE_ROWS * (b + 1) : P, t * P : (t + 1) * P],
-                            rhs=h_codes[:, tokens].bitcast(FP8X4), rhs_scale=h_s[:, tokens],
-                            start=(b == 0 and u == 0), stop=(b == R_PASSES - 1 and u == slices - 1),
+                            out=y_ps[s][:, t, :], lhsT=dealt["wd"][:, col : col + P].bitcast(FP8X4),
+                            lhsT_scale=scales[SCALE_ROWS:P, col : col + P],
+                            rhs=h_codes[:, at : at + STEP].bitcast(FP8X4), rhs_scale=h_s[:, at : at + STEP],
+                            start=(b == 0 and t == 0), stop=(b == R_PASSES - 1 and t == PACK - 1),
                         )
 
-        def finish_out(group, parts=1):
-            first, steps = GROUPS[group]
-            slices = PACK // steps
-            result = ring.tile([P, PACK, steps * STEP], F32, name="result")
-            width = steps * STEP // parts
-            for j0 in range(0, steps * STEP, width):
-                half, inside = divmod(first * STEP + j0, HALF)
-                for bank in range(steps):
-                    rows = slice(bank * slices, (bank + 1) * slices)
-                    nc.vector.tensor_tensor(
-                        result[:, rows, j0 : j0 + width], y_ps[group][bank][:, :, j0 : j0 + width],
-                        g_sb[half][:, rows, inside : inside + width], MULT,
-                    )
-                if group + 1 not in STAGED_AT:
-                    at = (first * STEP + j0) * PACK
-                    interleave(nc.scalar.copy, y_bf[:, at : at + width * PACK], result[:, :, j0 : j0 + width])
-            nc.sync.dma_start(out_rows[:, :, first * STEP : (first + steps) * STEP], result[:])
-            results[group] = result
+        def g_of(s, j0, width):
+            half, inside = divmod(s * STEP + j0, HALF)
+            return g_sb[half][:, :, inside : inside + width]
 
-        def round_out(group):
-            first, steps = GROUPS[group]
-            for s in range(first, first + steps):
-                dst = y_bf[:, s * STEP * PACK : (s + 1) * STEP * PACK]
-                src = results[group][:, :, (s - first) * STEP : (s - first + 1) * STEP]
-                if s in ON_GPSIMD:
-                    nc.gpsimd.tensor_scalar(
-                        dst.rearrange("p (j t) -> p j t", t=PACK), src.rearrange("p t j -> p j t"), 1.0, 0.0, MULT, ADD
-                    )
-                else:
-                    interleave(nc.scalar.copy, dst, src)
+        def round_out(s, j0=0, width=STEP):
+            at = (s * STEP + j0) * PACK
+            interleave(nc.scalar.copy, y_bf[:, at : at + width * PACK], results[s][:, :, j0 : j0 + width])
+
+        def store_out(s):
+            nc.sync.dma_start(out_rows[:, :, s * STEP : (s + 1) * STEP], results[s][:])
+
+        def finish_on_vector(s, parts=1):
+            results[s] = ring.tile([P, PACK, STEP], F32, name="result")
+            width = STEP // parts
+            for j0 in range(0, STEP, width):
+                nc.vector.tensor_tensor(
+                    results[s][:, :, j0 : j0 + width], y_ps[s][:, :, j0 : j0 + width], g_of(s, j0, width), MULT
+                )
+                round_out(s, j0, width)
+            store_out(s)
+
+        def empty_bank(s):
+            emptied[s] = ring.tile([P, PACK, STEP], F32, name="emptied", bufs=2)
+            nc.scalar.copy(emptied[s][:], y_ps[s][:])
+
+        def multiply_on_gpsimd(s, group):
+            results[s] = keep.tile([P, PACK, STEP], F32, name=f"h{group}", align_bytes=ALIGN)
+            nc.gpsimd.tensor_tensor(results[s][:], emptied[s][:], g_of(s, 0, STEP), MULT)
+            store_out(s)
 
         def quantize_out(first, count):
             tokens = slice(first * STEP, (first + count) * STEP)
@@ -293,43 +309,79 @@ def tile_list_sigm_mulP_kernel(
         gather(2, 0, J)
         deal_scales()
         round_wg(nc.scalar.copy, 0)
-        gather(PACK - 1, 0, CHUNKS[0][1])
-        gather(PACK - 1, CHUNKS[0][1], J - CHUNKS[0][1])
+        gather(PACK - 1, 0, CHUNK)
+        gather(PACK - 1, CHUNK, J - CHUNK)
+        round_xg(0)
         quantize_xg(0)
         round_wg(nc.scalar.copy, 1)
         quantize_wg(0)
-        first_stage(0, 0)
+        make_gate(0, 0)
         round_wg(nc.scalar.copy, 2)
         round_wg(nc.vector.tensor_copy, 3)
-        first_stage(1, 0)
         quantize_wg(1)
-        deal_wd()
+        round_xg(1)
+        make_gate(1, 0)
+        make_h(0, 0)
+        make_gate(0, 1)
+        make_h(1, 0)
+        make_gate(1, 1)
+        make_h(0, 1)
         quantize_xg(1)
-        for group, (first, steps) in enumerate(GROUPS[:-1]):
-            for s in range(first, first + steps):
-                if s > LEAD:
-                    first_stage(s, 0)
-                first_stage(s, 1)
-            if group == 0:
-                first_stage(LEAD, 0)
-            if group == 1:
-                quantize_xg(2)
-            if group >= 1:
-                finish_out(group - 1)
-            second_stage(group, 0, R_PASSES)
-            if group in STAGED_AT:
-                round_out(group - 1)
-            if group == 3:
-                quantize_out(0, 4)
+        make_gate(2, 0)
+        make_h(1, 1)
+        make_gate(2, 1)
+        deal_wd()
+        round_xg(2)
+        quantize_h(0)
+        quantize_xg(2)
+        round_xg(3)
+
+        def step(s):
+            for b in range(R_PASSES):
+                if s + 1 < STEPS:
+                    make_gate(s + 1, b)
+                make_h(s, b)
+
+        step(2)
+        step(3)
+        second_stage(0)
+        empty_bank(1)
+        finish_on_vector(0)
+        quantize_h(1)
+        quantize_xg(3)
+        multiply_on_gpsimd(1, 1)
+
+        step(4)
+        second_stage(1)
+        empty_bank(3)
+        finish_on_vector(2)
+        quantize_h(2)
+        multiply_on_gpsimd(3, 2)
+
+        step(5)
+        second_stage(2)
+        finish_on_vector(4)
+        round_out(1)
+        quantize_h(3)
+
+        step(6)
+        second_stage(3)
+        finish_on_vector(5)
+        round_out(3)
+        quantize_h(4)
+        quantize_out(0, 4)
+
         last = len(GROUPS) - 1
-        first_stage(STEPS - 1, 0)
+        make_h(STEPS - 1, 0)
         quantize_out(4, 2)
-        first_stage(STEPS - 1, 1)
-        second_stage(last, 0, 1)
-        second_stage(last, 1, 1)
+        make_h(STEPS - 1, 1)
+        second_stage(4)
+        for b in range(R_PASSES):
+            quantize_h(last, b, 1)
+            second_stage(last, b, 1)
         store_scales(0, STEPS - 2, [nc.sync])
-        finish_out(last - 1)
-        finish_out(last, parts=2)
+        finish_on_vector(STEPS - 2)
+        finish_on_vector(STEPS - 1, parts=2)
         quantize_out(STEPS - 2, 1)
         quantize_out(STEPS - 1, 1)
         store_scales(STEPS - 2, 2, [nc.scalar, nc.sync])

@@ -36,7 +36,7 @@ GROUPS = [(0, 2), (2, 2), (4, 1), (5, 1), (6, 1), (7, 1)]
 GROUP_OF = {first + member: (group, member) for group, (first, steps) in enumerate(GROUPS) for member in range(steps)}
 ON_GPSIMD = ()
 STAGED_AT = {}
-GATE_TAG = {(1, 0): "xg2", (1, 1): "wd_codes"}
+GATE_TAG = {(1, 0): "wd_codes"}
 PIECE = PASS // 2
 LEAD = 2
 ALIGN = 64
@@ -149,9 +149,9 @@ def tile_list_sigm_mulP_kernel(
             nc.vector.quantize_mx(out=wg_codes[b][:].bitcast(FP8X4), scales=wg_s[b][:], in_=wg_bf[b][:])
 
         picked = keep.tile([P, PACK, J], F32, name="picked")
-        staging = keep.tile([P, CHUNK * PACK], BF16, name="staging", align_bytes=ALIGN)
+        staging = keep.tile([P, 2 * CHUNK * PACK], BF16, name="staging", align_bytes=ALIGN)
         first_h = keep.tile([P, R_PASSES * CHUNK * PACK], BF16, name="first_h", align_bytes=ALIGN)
-        xg_bf = {0: staging[:], 1: wg_bf[1][:, 0 : CHUNK * PACK], 3: first_h[:, 0 : CHUNK * PACK]}
+        xg_bf = {0: staging[:, 0 : CHUNK * PACK], 1: staging[:, CHUNK * PACK :], 2: wg_bf[1][:, 0 : CHUNK * PACK], 3: first_h[:, 0 : CHUNK * PACK]}
         xg_codes = keep.tile([P, J], U32, name="xg_codes", align_bytes=ALIGN)
         xg_s = keep.tile([P, J], U8, name="xg_s", align_bytes=ALIGN)
 
@@ -176,10 +176,7 @@ def tile_list_sigm_mulP_kernel(
 
         def round_xg(c):
             j0, width = CHUNKS[c]
-            if c == 2:
-                late = keep.tile([P, CHUNK * PACK], BF16, name="xg2", align_bytes=ALIGN)
-                xg_bf[c] = late[:]
-            if c % 2 == 1:
+            if c >= 2:
                 round_on_gpsimd(xg_bf[c], picked[:, :, j0 : j0 + width])
             else:
                 for at in range(0, width, STEP):
@@ -315,23 +312,26 @@ def tile_list_sigm_mulP_kernel(
         quantize_xg(0)
         round_wg(nc.scalar.copy, 1)
         quantize_wg(0)
-        make_gate(0, 0)
-        round_wg(nc.scalar.copy, 2)
-        round_wg(nc.vector.tensor_copy, 3)
-        quantize_wg(1)
+        round_wg(nc.vector.tensor_copy, 2)
         round_xg(1)
-        make_gate(1, 0)
-        make_h(0, 0)
-        make_gate(0, 1)
-        make_h(1, 0)
-        make_gate(1, 1)
-        make_h(0, 1)
         quantize_xg(1)
-        make_gate(2, 0)
-        make_h(1, 1)
-        make_gate(2, 1)
+        make_gate(0, 0)
+        make_gate(1, 0)
+        round_wg(nc.scalar.copy, 3)
+        make_h(0, 0)
+        make_h(1, 0)
         deal_wd()
+        quantize_wg(1)
         round_xg(2)
+
+        for s, b in ((2, 0), (3, 0), (0, 1), (1, 1)):
+            make_gate(s, b)
+        make_h(2, 0)
+        make_h(3, 0)
+        make_gate(2, 1)
+        make_h(0, 1)
+        make_gate(3, 1)
+        make_h(1, 1)
         quantize_h(0)
         quantize_xg(2)
         round_xg(3)
@@ -342,38 +342,39 @@ def tile_list_sigm_mulP_kernel(
                     make_gate(s + 1, b)
                 make_h(s, b)
 
-        step(2)
-        step(3)
+        make_gate(4, 0)
+        make_h(2, 1)
+        make_gate(4, 1)
+        make_h(3, 1)
         second_stage(0)
         empty_bank(1)
         finish_on_vector(0)
-        quantize_h(1)
-        quantize_xg(3)
-        multiply_on_gpsimd(1, 1)
-
         step(4)
+        quantize_h(1)
+        quantize_h(2)
+        quantize_xg(3)
+        multiply_on_gpsimd(1, 2)
+
         second_stage(1)
         empty_bank(3)
         finish_on_vector(2)
-        quantize_h(2)
-        multiply_on_gpsimd(3, 2)
-
         step(5)
         second_stage(2)
-        finish_on_vector(4)
         round_out(1)
+        finish_on_vector(4)
         quantize_h(3)
+        multiply_on_gpsimd(3, 3)
 
         step(6)
         second_stage(3)
         finish_on_vector(5)
         round_out(3)
         quantize_h(4)
-        quantize_out(0, 4)
+        quantize_out(0, 2)
 
         last = len(GROUPS) - 1
         make_h(STEPS - 1, 0)
-        quantize_out(4, 2)
+        quantize_out(2, 4)
         make_h(STEPS - 1, 1)
         second_stage(4)
         for b in range(R_PASSES):

@@ -36,7 +36,7 @@ GROUPS = [(0, 2), (2, 2), (4, 1), (5, 1), (6, 1), (7, 1)]
 GROUP_OF = {first + member: (group, member) for group, (first, steps) in enumerate(GROUPS) for member in range(steps)}
 ON_GPSIMD = ()
 STAGED_AT = {}
-GATE_TAG = {(1, 0): "wd_codes"}
+GATE_TAG = {}
 PIECE = PASS // 2
 LEAD = 2
 ALIGN = 64
@@ -318,11 +318,11 @@ def tile_list_sigm_mulP_kernel(
         make_gate(0, 0)
         make_gate(1, 0)
         round_wg(nc.scalar.copy, 3)
-        make_h(0, 0)
-        make_h(1, 0)
         deal_wd()
         quantize_wg(1)
         round_xg(2)
+        make_h(0, 0)
+        make_h(1, 0)
 
         for s, b in ((2, 0), (3, 0), (0, 1), (1, 1)):
             make_gate(s, b)

@@ -37,6 +37,8 @@ GROUP_OF = {first + member: (group, member) for group, (first, steps) in enumera
 ON_GPSIMD = ()
 STAGED_AT = {}
 GATE_TAG = {}
+PITCH = J + (PACK - 1) * STEP
+FIRST_PITCH = PITCH - STEP
 PIECE = PASS // 2
 LEAD = 2
 ALIGN = 64
@@ -148,7 +150,9 @@ def tile_list_sigm_mulP_kernel(
         def quantize_wg(b):
             nc.vector.quantize_mx(out=wg_codes[b][:].bitcast(FP8X4), scales=wg_s[b][:], in_=wg_bf[b][:])
 
-        picked = keep.tile([P, PACK, J], F32, name="picked")
+        picks = keep.tile([P, (PACK + 1) * FIRST_PITCH], F32, name="picks")
+        picked = picks[:, 0 : PACK * PITCH].rearrange("p (i w) -> p i w", i=PACK)
+        first_picked = picks[:, FIRST_PITCH:].rearrange("p (i w) -> p i w", i=PACK)[:, :, 0:STEP]
         staging = keep.tile([P, 2 * CHUNK * PACK], BF16, name="staging", align_bytes=ALIGN)
         first_h = keep.tile([P, R_PASSES * CHUNK * PACK], BF16, name="first_h", align_bytes=ALIGN)
         xg_bf = {0: staging[:, 0 : CHUNK * PACK], 1: staging[:, CHUNK * PACK :], 2: wg_bf[1][:, 0 : CHUNK * PACK], 3: first_h[:, 0 : CHUNK * PACK]}
@@ -157,7 +161,7 @@ def tile_list_sigm_mulP_kernel(
 
         def gather(i, j0, width):
             nc.vector.tensor_tensor(
-                picked[:, i, j0 : j0 + width],
+                picked[:, i, j0 : j0 + width] if j0 > 0 else first_picked[:, i, :],
                 planes[i][:].indirect(offsets[:, j0 // HEAD : (j0 + width) // HEAD]),
                 wgt_sb[:, j0 : j0 + width],
                 MULT,
@@ -182,6 +186,17 @@ def tile_list_sigm_mulP_kernel(
                 for at in range(0, width, STEP):
                     interleave(nc.scalar.copy, xg_bf[c][:, at * PACK : (at + STEP) * PACK], picked[:, :, j0 + at : j0 + at + STEP])
 
+        def round_first(s):
+            source = first_picked if s == 0 else picked[:, :, STEP : 2 * STEP]
+            interleave(nc.scalar.copy, xg_bf[0][:, s * STEP * PACK : (s + 1) * STEP * PACK], source)
+
+        def quantize_first(s):
+            tokens = slice(s * STEP, (s + 1) * STEP)
+            nc.vector.quantize_mx(
+                out=xg_codes[:, tokens].bitcast(FP8X4), scales=xg_s[:, tokens],
+                in_=xg_bf[0][:, s * STEP * PACK : (s + 1) * STEP * PACK],
+            )
+
         def quantize_xg(c):
             j0, width = CHUNKS[c]
             nc.vector.quantize_mx(
@@ -191,7 +206,7 @@ def tile_list_sigm_mulP_kernel(
         out_codes = keep.tile([P, J], U32, name="out_codes", align_bytes=ALIGN)
         out_s = keep.tile([P, J], U8, name="out_s", align_bytes=ALIGN)
         y_bf = keep.tile([P, J * PACK], BF16, name="y_bf", align_bytes=ALIGN)
-        gates, h_bf, h_mx, y_ps, results, emptied = {}, {}, {}, {}, {}, {}
+        gates, h_bf, h_mx, y_ps, results, emptied, ubs = {}, {}, {}, {}, {}, {}, {}
 
         def make_gate(s, b):
             tokens = slice(s * STEP, (s + 1) * STEP)
@@ -208,9 +223,13 @@ def tile_list_sigm_mulP_kernel(
                 gates[s, b] = ring.tile([P, STEP, PACK], F32, name="gate", bufs=6)
             nc.scalar.activation(gates[s, b][:], ga[:].rearrange("p t j -> p j t"), SIGMOID)
 
-        def make_h(s, b):
+        def make_ub(s, b, early=False):
             tokens = slice(s * STEP, (s + 1) * STEP)
-            ub = psum.tile([P, PACK, STEP], F32, name="ub", bufs=3)
+            if early:
+                ub = psum.tile([P, PACK, STEP], F32, name="y_ps", bufs=2)
+            else:
+                ub = psum.tile([P, PACK, STEP], F32, name="ub", bufs=3)
+            ubs[s, b] = ub
             for t in range(PACK):
                 col = b * PASS + t * P
                 nc.tensor.matmul_mx(
@@ -218,6 +237,11 @@ def tile_list_sigm_mulP_kernel(
                     lhsT_scale=scales[:, col : col + P],
                     rhs=xg_codes[:, tokens].bitcast(FP8X4), rhs_scale=xg_s[:, tokens], start=True, stop=True,
                 )
+
+        def make_h(s, b):
+            if (s, b) not in ubs:
+                make_ub(s, b)
+            ub = ubs[s, b]
             gate = gates[s, b]
             group, member = GROUP_OF[s]
             if (b, member) == (0, 0):
@@ -300,16 +324,23 @@ def tile_list_sigm_mulP_kernel(
                 )
 
         deal_wu()
-        for half in range(2):
-            gather(0, half * HALF, HALF)
-        gather(1, 0, J)
-        gather(2, 0, J)
+        gather(0, 0, STEP)
+        gather(0, STEP, HALF - STEP)
+        gather(0, HALF, HALF)
+        for i in (1, 2):
+            gather(i, 0, STEP)
+            gather(i, STEP, J - STEP)
         deal_scales()
         round_wg(nc.scalar.copy, 0)
-        gather(PACK - 1, 0, CHUNK)
-        gather(PACK - 1, CHUNK, J - CHUNK)
-        round_xg(0)
-        quantize_xg(0)
+        gather(PACK - 1, 0, STEP)
+        round_first(0)
+        gather(PACK - 1, STEP, CHUNK)
+        quantize_first(0)
+        make_ub(0, 0)
+        make_ub(0, 1, early=True)
+        round_first(1)
+        gather(PACK - 1, STEP + CHUNK, J - STEP - CHUNK)
+        quantize_first(1)
         round_wg(nc.scalar.copy, 1)
         quantize_wg(0)
         round_wg(nc.vector.tensor_copy, 2)
@@ -317,6 +348,8 @@ def tile_list_sigm_mulP_kernel(
         quantize_xg(1)
         make_gate(0, 0)
         make_gate(1, 0)
+        make_ub(1, 0)
+        make_ub(1, 1, early=True)
         round_wg(nc.scalar.copy, 3)
         deal_wd()
         quantize_wg(1)

@@ -140,11 +140,11 @@ def tile_list_sigm_mulP_kernel(
         wg_s = [keep.tile([P, PASS], U8, name=f"wg_s{b}", align_bytes=ALIGN) for b in range(R_PASSES)]
         wg_bf = [keep.tile([P, PASS * PACK], BF16, name=f"wg_bf{b}", align_bytes=ALIGN) for b in range(R_PASSES)]
 
-        def round_wg(copy, u):
+        def round_wg(copy, u, first=0, count=PIECE // PACK):
             b, m0 = divmod(u * PIECE // PACK, P)
             copy(
-                wg_bf[b][:].rearrange("p (t m i) -> p m i t", t=PACK, i=PACK)[:, m0 : m0 + PIECE // PACK],
-                wg_raw[u][:].rearrange("p i (m t) -> p m i t", t=PACK),
+                wg_bf[b][:].rearrange("p (t m i) -> p m i t", t=PACK, i=PACK)[:, m0 + first : m0 + first + count],
+                wg_raw[u][:].rearrange("p i (m t) -> p m i t", t=PACK)[:, first : first + count],
             )
 
         def quantize_wg(b):
@@ -155,7 +155,7 @@ def tile_list_sigm_mulP_kernel(
         first_picked = picks[:, FIRST_PITCH:].rearrange("p (i w) -> p i w", i=PACK)[:, :, 0:STEP]
         staging = keep.tile([P, 2 * CHUNK * PACK], BF16, name="staging", align_bytes=ALIGN)
         first_h = keep.tile([P, R_PASSES * CHUNK * PACK], BF16, name="first_h", align_bytes=ALIGN)
-        xg_bf = {0: staging[:, 0 : CHUNK * PACK], 1: staging[:, CHUNK * PACK :], 2: wg_bf[1][:, 0 : CHUNK * PACK], 3: first_h[:, 0 : CHUNK * PACK]}
+        xg_bf = {0: staging[:, 0 : CHUNK * PACK], 1: staging[:, CHUNK * PACK :], 2: wg_bf[1][:, 0 : CHUNK * PACK], 3: wg_bf[1][:, CHUNK * PACK :]}
         xg_codes = keep.tile([P, J], U32, name="xg_codes", align_bytes=ALIGN)
         xg_s = keep.tile([P, J], U8, name="xg_s", align_bytes=ALIGN)
 
@@ -298,7 +298,10 @@ def tile_list_sigm_mulP_kernel(
                 nc.vector.tensor_tensor(
                     results[s][:, :, j0 : j0 + width], y_ps[s][:, :, j0 : j0 + width], g_of(s, j0, width), MULT
                 )
-                round_out(s, j0, width)
+                if s == 0:
+                    round_on_gpsimd(y_bf[:, 0 : STEP * PACK], results[s][:])
+                else:
+                    round_out(s, j0, width)
             store_out(s)
 
         def empty_bank(s):
@@ -310,11 +313,13 @@ def tile_list_sigm_mulP_kernel(
             nc.gpsimd.tensor_tensor(results[s][:], emptied[s][:], g_of(s, 0, STEP), MULT)
             store_out(s)
 
-        def quantize_out(first, count):
+        def quantize_out(first, count, store_from=None):
             tokens = slice(first * STEP, (first + count) * STEP)
             rounded = y_bf[:, first * STEP * PACK : (first + count) * STEP * PACK]
             nc.vector.quantize_mx(out=out_codes[:, tokens].bitcast(FP8X4), scales=out_s[:, tokens], in_=rounded)
-            nc.sync.dma_start(out_words[:, tokens], out_codes[:, tokens].bitcast(I32))
+            if store_from is not None:
+                stored = slice(store_from * STEP, (first + count) * STEP)
+                nc.sync.dma_start(out_words[:, stored], out_codes[:, stored].bitcast(I32))
 
         def store_scales(first, count, queues):
             tokens = slice(first * STEP, (first + count) * STEP)
@@ -334,12 +339,13 @@ def tile_list_sigm_mulP_kernel(
         round_wg(nc.scalar.copy, 0)
         gather(PACK - 1, 0, STEP)
         round_first(0)
-        gather(PACK - 1, STEP, CHUNK)
+        gather(PACK - 1, STEP, STEP)
+        gather(PACK - 1, CHUNK, CHUNK)
         quantize_first(0)
         make_ub(0, 0)
         make_ub(0, 1, early=True)
         round_first(1)
-        gather(PACK - 1, STEP + CHUNK, J - STEP - CHUNK)
+        gather(PACK - 1, HALF, HALF)
         quantize_first(1)
         round_wg(nc.scalar.copy, 1)
         quantize_wg(0)
@@ -350,10 +356,12 @@ def tile_list_sigm_mulP_kernel(
         make_gate(1, 0)
         make_ub(1, 0)
         make_ub(1, 1, early=True)
-        round_wg(nc.scalar.copy, 3)
+        round_wg(nc.scalar.copy, 3, 0, 32)
+        round_wg(nc.vector.tensor_copy, 3, 32, 32)
         deal_wd()
         quantize_wg(1)
         round_xg(2)
+        round_xg(3)
         make_h(0, 0)
         make_h(1, 0)
 
@@ -367,7 +375,6 @@ def tile_list_sigm_mulP_kernel(
         make_h(1, 1)
         quantize_h(0)
         quantize_xg(2)
-        round_xg(3)
 
         def step(s):
             for b in range(R_PASSES):
@@ -400,22 +407,24 @@ def tile_list_sigm_mulP_kernel(
 
         step(6)
         second_stage(3)
-        finish_on_vector(5)
         round_out(3)
+        finish_on_vector(5)
         quantize_h(4)
-        quantize_out(0, 2)
+        quantize_out(0, 2, 0)
+        store_scales(0, 2, [nc.sync])
 
         last = len(GROUPS) - 1
         make_h(STEPS - 1, 0)
-        quantize_out(2, 4)
-        make_h(STEPS - 1, 1)
         second_stage(4)
-        for b in range(R_PASSES):
-            quantize_h(last, b, 1)
-            second_stage(last, b, 1)
-        store_scales(0, STEPS - 2, [nc.sync])
+        make_h(STEPS - 1, 1)
+        quantize_h(last, 0, 1)
+        second_stage(last, 0, 1)
+        quantize_out(2, 2, 2)
+        quantize_h(last, 1, 1)
+        second_stage(last, 1, 1)
         finish_on_vector(STEPS - 2)
+        quantize_out(4, 2)
         finish_on_vector(STEPS - 1, parts=2)
-        quantize_out(STEPS - 2, 1)
-        quantize_out(STEPS - 1, 1)
-        store_scales(STEPS - 2, 2, [nc.scalar, nc.sync])
+        quantize_out(STEPS - 2, 1, 4)
+        quantize_out(STEPS - 1, 1, STEPS - 1)
+        store_scales(2, 6, [nc.scalar, nc.sync])

@@ -65,7 +65,7 @@ def tile_list_sigm_mulP_kernel(
         wu_raw = keep.tile([P, 2 * R], U8, name="wu_raw", align_bytes=ALIGN)
         planes = [keep.tile([P, T], F32, name=f"plane{i}") for i in range(PACK)]
         wgt_cut = keep.tile([P, CUT], F32, name="wgt_cut", align_bytes=ALIGN)
-        wg_raw = [keep.tile([P, PACK, PIECE], F32, name=f"wg_raw{u}") for u in range(R // PIECE)]
+        wg_raw = [keep.tile([P, PACK, PIECE], F32, name=f"wg_raw{u}", align_bytes=ALIGN) for u in range(R // PIECE)]
         g_sb = [keep.tile([P, PACK, HALF], F32, name=f"g{half}") for half in range(2)]
         wd_raw = keep.tile([P, R_PASSES, N], I32, name="wd_raw")
 
@@ -153,9 +153,9 @@ def tile_list_sigm_mulP_kernel(
         picks = keep.tile([P, (PACK + 1) * FIRST_PITCH], F32, name="picks")
         picked = picks[:, 0 : PACK * PITCH].rearrange("p (i w) -> p i w", i=PACK)
         first_picked = picks[:, FIRST_PITCH:].rearrange("p (i w) -> p i w", i=PACK)[:, :, 0:STEP]
-        staging = keep.tile([P, 2 * CHUNK * PACK], BF16, name="staging", align_bytes=ALIGN)
+        staging = [keep.tile([P, CHUNK * PACK], BF16, name=name, align_bytes=ALIGN) for name in ("staging", "wg_raw1")]
         first_h = keep.tile([P, R_PASSES * CHUNK * PACK], BF16, name="first_h", align_bytes=ALIGN)
-        xg_bf = {0: staging[:, 0 : CHUNK * PACK], 1: staging[:, CHUNK * PACK :], 2: wg_bf[1][:, 0 : CHUNK * PACK], 3: wg_bf[1][:, CHUNK * PACK :]}
+        xg_bf = {0: staging[0][:], 1: staging[1][:], 2: wg_bf[1][:, 0 : CHUNK * PACK], 3: wg_bf[1][:, CHUNK * PACK :]}
         xg_codes = keep.tile([P, J], U32, name="xg_codes", align_bytes=ALIGN)
         xg_s = keep.tile([P, J], U8, name="xg_s", align_bytes=ALIGN)
 
@@ -423,8 +423,8 @@ def tile_list_sigm_mulP_kernel(
         quantize_h(last, 1, 1)
         second_stage(last, 1, 1)
         finish_on_vector(STEPS - 2)
-        quantize_out(4, 2)
+        quantize_out(4, 2, 4)
         finish_on_vector(STEPS - 1, parts=2)
-        quantize_out(STEPS - 2, 1, 4)
-        quantize_out(STEPS - 1, 1, STEPS - 1)
+        quantize_out(STEPS - 2, 1)
+        quantize_out(STEPS - 1, 1, STEPS - 2)
         store_scales(2, 6, [nc.scalar, nc.sync])

@@ -39,6 +39,7 @@ STAGED_AT = {}
 GATE_TAG = {}
 PITCH = J + (PACK - 1) * STEP
 FIRST_PITCH = PITCH - STEP
+LOWER, UPPER = slice(0, 2), slice(2, PACK)
 PIECE = PASS // 2
 LEAD = 2
 ALIGN = 64
@@ -167,10 +168,10 @@ def tile_list_sigm_mulP_kernel(
                 MULT,
             )
 
-        def interleave(copy, dst, src):
+        def interleave(copy, dst, src, rows=slice(0, PACK)):
             copy(
-                dst.rearrange("p (c e i) -> p c i e", e=LINE, i=PACK),
-                src.rearrange("p i (c e) -> p c i e", e=LINE),
+                dst.rearrange("p (c e i) -> p c i e", e=LINE, i=PACK)[:, :, rows],
+                src.rearrange("p i (c e) -> p c i e", e=LINE)[:, :, rows],
             )
 
         def round_on_gpsimd(dst, src):
@@ -186,9 +187,9 @@ def tile_list_sigm_mulP_kernel(
                 for at in range(0, width, STEP):
                     interleave(nc.scalar.copy, xg_bf[c][:, at * PACK : (at + STEP) * PACK], picked[:, :, j0 + at : j0 + at + STEP])
 
-        def round_first(s):
+        def round_first(s, rows):
             source = first_picked if s == 0 else picked[:, :, STEP : 2 * STEP]
-            interleave(nc.scalar.copy, xg_bf[0][:, s * STEP * PACK : (s + 1) * STEP * PACK], source)
+            interleave(nc.scalar.copy, xg_bf[0][:, s * STEP * PACK : (s + 1) * STEP * PACK], source, rows)
 
         def quantize_first(s):
             tokens = slice(s * STEP, (s + 1) * STEP)
@@ -335,16 +336,19 @@ def tile_list_sigm_mulP_kernel(
         for i in (1, 2):
             gather(i, 0, STEP)
             gather(i, STEP, J - STEP)
+            if i == 1:
+                round_first(0, LOWER)
+                round_first(1, LOWER)
         deal_scales()
         round_wg(nc.scalar.copy, 0)
         gather(PACK - 1, 0, STEP)
-        round_first(0)
+        round_first(0, UPPER)
         gather(PACK - 1, STEP, STEP)
         gather(PACK - 1, CHUNK, CHUNK)
         quantize_first(0)
         make_ub(0, 0)
         make_ub(0, 1, early=True)
-        round_first(1)
+        round_first(1, UPPER)
         gather(PACK - 1, HALF, HALF)
         quantize_first(1)
         round_wg(nc.scalar.copy, 1)
@@ -356,8 +360,8 @@ def tile_list_sigm_mulP_kernel(
         make_gate(1, 0)
         make_ub(1, 0)
         make_ub(1, 1, early=True)
-        round_wg(nc.scalar.copy, 3, 0, 32)
-        round_wg(nc.vector.tensor_copy, 3, 32, 32)
+        round_wg(nc.scalar.copy, 3, 0, 48)
+        round_wg(nc.vector.tensor_copy, 3, 48, 16)
         deal_wd()
         quantize_wg(1)
         round_xg(2)

@@ -360,8 +360,8 @@ def tile_list_sigm_mulP_kernel(
         make_gate(1, 0)
         make_ub(1, 0)
         make_ub(1, 1, early=True)
-        round_wg(nc.scalar.copy, 3, 0, 48)
-        round_wg(nc.vector.tensor_copy, 3, 48, 16)
+        round_wg(nc.scalar.copy, 3, 0, 32)
+        round_wg(nc.vector.tensor_copy, 3, 32, 32)
         deal_wd()
         quantize_wg(1)
         round_xg(2)

@@ -17,7 +17,6 @@ MULT = mybir.AluOpType.mult
 ADD = mybir.AluOpType.add
 SIGMOID = mybir.ActivationFunctionType.Sigmoid
 
-
 P = 128
 PACK = 4
 PASS = P * PACK
@@ -28,20 +27,11 @@ HEAD = 16
 CUT = J // HEAD
 LINE = 4
 STEP = 128
-STEPS = J // STEP
+PAIR = 2 * STEP
 HALF = J // 2
-CHUNK = 2 * STEP
-CHUNKS = [(j0, CHUNK) for j0 in range(0, J, CHUNK)]
-GROUPS = [(0, 2), (2, 2), (4, 1), (5, 1), (6, 1), (7, 1)]
-GROUP_OF = {first + member: (group, member) for group, (first, steps) in enumerate(GROUPS) for member in range(steps)}
-ON_GPSIMD = ()
-STAGED_AT = {}
-GATE_TAG = {}
-PITCH = J + (PACK - 1) * STEP
-FIRST_PITCH = PITCH - STEP
 LOWER, UPPER = slice(0, 2), slice(2, PACK)
 PIECE = PASS // 2
-LEAD = 2
+PIECE_M = PIECE // PACK
 ALIGN = 64
 
 
@@ -66,18 +56,24 @@ def tile_list_sigm_mulP_kernel(
         wu_raw = keep.tile([P, 2 * R], U8, name="wu_raw", align_bytes=ALIGN)
         planes = [keep.tile([P, T], F32, name=f"plane{i}") for i in range(PACK)]
         wgt_cut = keep.tile([P, CUT], F32, name="wgt_cut", align_bytes=ALIGN)
-        wg_raw = [keep.tile([P, PACK, PIECE], F32, name=f"wg_raw{u}", align_bytes=ALIGN) for u in range(R // PIECE)]
         g_sb = [keep.tile([P, PACK, HALF], F32, name=f"g{half}") for half in range(2)]
         wd_raw = keep.tile([P, R_PASSES, N], I32, name="wd_raw")
 
+        early = keep.tile([P, PACK, HALF], F32, name="early", align_bytes=ALIGN)
+        late = keep.tile([P, 6 * HALF], F32, name="late", align_bytes=ALIGN)
+        at_wg1 = 3 * HALF + STEP
+        late_rows = late[:, 0 : PACK * HALF].rearrange("p (i w) -> p i w", i=PACK)
+        wg_raw = [keep.tile([P, PACK, PIECE], F32, name=f"wg_raw{u}", align_bytes=ALIGN)[:] for u in range(3)]
+        wg_raw.append(late[:, at_wg1 : at_wg1 + PACK * PIECE].rearrange("p (i c) -> p i c", i=PACK))
+
         def load_wg(u):
-            nc.sync.dma_start(wg_raw[u][:], wg_rows[:, :, u * PIECE : (u + 1) * PIECE])
+            nc.sync.dma_start(wg_raw[u], wg_rows[:, :, u * PIECE : (u + 1) * PIECE])
 
         nc.sync.dma_start(wgt_cut[:], wgt[0:P:HEAD, :].rearrange("a (c j) -> a c j", j=CUT))
         nc.sync.dma_start(offsets[:], offs)
-        nc.sync.dma_start(wu_raw[:].bitcast(I32), wu_words[0].bitcast(I32))
         nc.sync.dma_start(planes[0][:], x_rows[:, 0, :])
         nc.sync.dma_start(planes[1][:], x_rows[:, 1, :])
+        nc.sync.dma_start(wu_raw[:].bitcast(I32), wu_words[0].bitcast(I32))
         for row in range(SCALE_ROWS):
             nc.sync.dma_start(
                 scales_raw[row:P:QUADRANT, :].bitcast(I32), wu_scales[0, row::SCALE_ROWS, :].bitcast(I32)
@@ -88,11 +84,9 @@ def tile_list_sigm_mulP_kernel(
                 scales_raw[SCALE_ROWS + row : P : QUADRANT, :].bitcast(I32).rearrange("q (b n) -> q b n", b=R_PASSES),
                 wd_scales[:, row::SCALE_ROWS, :].bitcast(I32).rearrange("b q n -> q b n"),
             )
-        load_wg(0)
         nc.sync.dma_start(planes[3][:], x_rows[:, 3, :])
-        load_wg(1)
-        load_wg(2)
-        load_wg(3)
+        for u in range(R // PIECE):
+            load_wg(u)
         nc.sync.dma_start(wd_raw[:], wd_words.rearrange("b p n i -> p b (n i)").bitcast(I32))
         for half in range(2):
             nc.sync.dma_start(g_sb[half][:], g_rows[:, :, half * HALF : (half + 1) * HALF])
@@ -100,335 +94,326 @@ def tile_list_sigm_mulP_kernel(
         warm = keep.tile([P, 1], F32, name="warm")
         nc.scalar.activation(warm[:], wgt_cut[:, 0:1], SIGMOID)
 
+        staging = keep.tile([P, 8 * PASS], BF16, name="staging", align_bytes=ALIGN)
+        h_first = staging[:, 0 : PASS * PACK]
+        wg_bf = [keep.tile([P, PASS * PACK], BF16, name="wg_bf0", align_bytes=ALIGN)[:], staging[:, PASS * PACK : 2 * PASS * PACK]]
+        xg45 = staging[:, PASS * PACK : PASS * PACK + PAIR * PACK]
+        xg67 = staging[:, PASS * PACK - 3 * PAIR : PASS * PACK + PAIR]
+        h01 = staging[:, PASS * PACK + PAIR : PASS * PACK + PAIR + 2 * PASS]
+        wgt_sb = [keep.tile([P, HALF], F32, name="wgt0", align_bytes=ALIGN)[:], staging[:, 0 : 2 * HALF].bitcast(F32)]
+
         wgt_turned = keep.tile([P, CUT], F32, name="wgt_turned", align_bytes=ALIGN)
         for j0 in range(0, CUT, QUADRANT):
             nc.vector.transpose(wgt_turned[:, j0 : j0 + QUADRANT], wgt_cut[:, j0 : j0 + QUADRANT])
-        wgt_sb = keep.tile([P, J], F32, name="wgt_sb", align_bytes=ALIGN)
         cuts = HALF // CUT
-        for half in range(2):
+
+        def spread(half):
             repeated = keep.tile([P, HALF], F32, name=f"wgt_repeated{half}", align_bytes=ALIGN)
             source = wgt_turned[:].rearrange("p (sa c) -> p c sa", c=HEAD)[:, half * cuts : (half + 1) * cuts, :]
             nc.scalar.copy(
                 repeated[:].rearrange("p (c sa rep) -> p c sa rep", c=cuts, rep=HEAD),
                 source.unsqueeze(3).to_broadcast([P, cuts, CUT // HEAD, HEAD]),
             )
-            nc.vector.transpose(wgt_sb[:, half * HALF : (half + 1) * HALF], repeated[:])
+            nc.vector.transpose(wgt_sb[half], repeated[:])
 
         wu_codes = keep.tile([P, 2 * R], U8, name="wu_codes", align_bytes=ALIGN)
-        scales = keep.tile([P, R], U8, name="scales", align_bytes=ALIGN)
         dealt = {}
+        wd_codes = keep.tile([P, R_PASSES * N], U32, name="wd_codes", align_bytes=ALIGN)
 
         def deal_wu():
-            nc.vector.tensor_copy(
+            nc.scalar.copy(
                 wu_codes[:].bitcast(U16).rearrange("p (b t m) -> p b t m", b=R_PASSES, t=PACK),
                 wu_raw[:].bitcast(U16).rearrange("p (b m t) -> p b t m", b=R_PASSES, t=PACK),
             )
 
         def deal_scales():
+            dealt["s"] = keep.tile([P, R], U8, name="wgt0", align_bytes=ALIGN)
             nc.vector.tensor_copy(
-                scales[:].rearrange("p (b t m) -> p b t m", b=R_PASSES, t=PACK),
+                dealt["s"][:].rearrange("p (b t m) -> p b t m", b=R_PASSES, t=PACK),
                 scales_raw[:].rearrange("p (b m t) -> p b t m", b=R_PASSES, t=PACK),
             )
 
-        def deal_wd():
-            dealt["wd"] = keep.tile([P, R_PASSES * N], I32, name="wd_codes", align_bytes=ALIGN)
-            nc.vector.tensor_copy(
-                dealt["wd"][:].rearrange("p (b t m) -> p b m t", b=R_PASSES, t=PACK),
-                wd_raw[:].rearrange("p b (m t) -> p b m t", t=PACK),
+        def deal_wd(b):
+            nc.scalar.copy(
+                wd_codes[:, b * N : (b + 1) * N].rearrange("p (t m) -> p m t", t=PACK),
+                wd_raw[:, b].bitcast(U32).rearrange("p (m t) -> p m t", t=PACK),
             )
 
         wg_codes = [keep.tile([P, PASS], U32, name=f"wg_codes{b}", align_bytes=ALIGN) for b in range(R_PASSES)]
         wg_s = [keep.tile([P, PASS], U8, name=f"wg_s{b}", align_bytes=ALIGN) for b in range(R_PASSES)]
-        wg_bf = [keep.tile([P, PASS * PACK], BF16, name=f"wg_bf{b}", align_bytes=ALIGN) for b in range(R_PASSES)]
 
-        def round_wg(copy, u, first=0, count=PIECE // PACK):
-            b, m0 = divmod(u * PIECE // PACK, P)
+        def round_wg(copy, u, slices=slice(0, PACK)):
+            b, m0 = divmod(u * PIECE_M, P)
             copy(
-                wg_bf[b][:].rearrange("p (t m i) -> p m i t", t=PACK, i=PACK)[:, m0 + first : m0 + first + count],
-                wg_raw[u][:].rearrange("p i (m t) -> p m i t", t=PACK)[:, first : first + count],
+                wg_bf[b].rearrange("p (t m i) -> p m i t", t=PACK, i=PACK)[:, m0 : m0 + PIECE_M, :, slices],
+                wg_raw[u].rearrange("p i (m t) -> p m i t", t=PACK)[:, :, :, slices],
             )
 
         def quantize_wg(b):
-            nc.vector.quantize_mx(out=wg_codes[b][:].bitcast(FP8X4), scales=wg_s[b][:], in_=wg_bf[b][:])
+            nc.vector.quantize_mx(out=wg_codes[b][:].bitcast(FP8X4), scales=wg_s[b][:], in_=wg_bf[b])
 
-        picks = keep.tile([P, (PACK + 1) * FIRST_PITCH], F32, name="picks")
-        picked = picks[:, 0 : PACK * PITCH].rearrange("p (i w) -> p i w", i=PACK)
-        first_picked = picks[:, FIRST_PITCH:].rearrange("p (i w) -> p i w", i=PACK)[:, :, 0:STEP]
-        staging = [keep.tile([P, CHUNK * PACK], BF16, name=name, align_bytes=ALIGN) for name in ("staging", "wg_raw1")]
-        first_h = keep.tile([P, R_PASSES * CHUNK * PACK], BF16, name="first_h", align_bytes=ALIGN)
-        xg_bf = {0: staging[0][:], 1: staging[1][:], 2: wg_bf[1][:, 0 : CHUNK * PACK], 3: wg_bf[1][:, CHUNK * PACK :]}
-        xg_codes = keep.tile([P, J], U32, name="xg_codes", align_bytes=ALIGN)
-        xg_s = keep.tile([P, J], U8, name="xg_s", align_bytes=ALIGN)
+        xg_bf = keep.tile([P, HALF * PACK], BF16, name="xg_bf", align_bytes=ALIGN)
+        xg_mx = {}
 
-        def gather(i, j0, width):
+        def gather(dst, i, j0, width):
+            half, inside = divmod(j0, HALF)
             nc.vector.tensor_tensor(
-                picked[:, i, j0 : j0 + width] if j0 > 0 else first_picked[:, i, :],
-                planes[i][:].indirect(offsets[:, j0 // HEAD : (j0 + width) // HEAD]),
-                wgt_sb[:, j0 : j0 + width],
-                MULT,
+                dst, planes[i][:].indirect(offsets[:, j0 // HEAD : (j0 + width) // HEAD]),
+                wgt_sb[half][:, inside : inside + width], MULT,
             )
 
         def interleave(copy, dst, src, rows=slice(0, PACK)):
             copy(
                 dst.rearrange("p (c e i) -> p c i e", e=LINE, i=PACK)[:, :, rows],
-                src.rearrange("p i (c e) -> p c i e", e=LINE)[:, :, rows],
+                src.rearrange("p i (c e) -> p c i e", e=LINE),
             )
+
+        def round_xg(j0, width, src, rows):
+            interleave(nc.scalar.copy, xg_bf[:, j0 * PACK : (j0 + width) * PACK], src, rows)
 
         def round_on_gpsimd(dst, src):
             nc.gpsimd.tensor_scalar(
                 dst.rearrange("p (j t) -> p j t", t=PACK), src.rearrange("p t j -> p j t"), 1.0, 0.0, MULT, ADD
             )
 
-        def round_xg(c):
-            j0, width = CHUNKS[c]
-            if c >= 2:
-                round_on_gpsimd(xg_bf[c], picked[:, :, j0 : j0 + width])
-            else:
-                for at in range(0, width, STEP):
-                    interleave(nc.scalar.copy, xg_bf[c][:, at * PACK : (at + STEP) * PACK], picked[:, :, j0 + at : j0 + at + STEP])
-
-        def round_first(s, rows):
-            source = first_picked if s == 0 else picked[:, :, STEP : 2 * STEP]
-            interleave(nc.scalar.copy, xg_bf[0][:, s * STEP * PACK : (s + 1) * STEP * PACK], source, rows)
-
-        def quantize_first(s):
-            tokens = slice(s * STEP, (s + 1) * STEP)
-            nc.vector.quantize_mx(
-                out=xg_codes[:, tokens].bitcast(FP8X4), scales=xg_s[:, tokens],
-                in_=xg_bf[0][:, s * STEP * PACK : (s + 1) * STEP * PACK],
-            )
-
-        def quantize_xg(c):
-            j0, width = CHUNKS[c]
-            nc.vector.quantize_mx(
-                out=xg_codes[:, j0 : j0 + width].bitcast(FP8X4), scales=xg_s[:, j0 : j0 + width], in_=xg_bf[c]
-            )
+        def quantize_xg(j0, width, rounded=None):
+            if rounded is None:
+                rounded = xg_bf[:, j0 * PACK : (j0 + width) * PACK]
+            name = f"xg_codes{j0}"
+            codes = keep.tile([P, width], U32, name=name, align_bytes=ALIGN)
+            plane = keep.tile([P, width], U8, name=f"xg_s{j0}", align_bytes=ALIGN)
+            nc.vector.quantize_mx(out=codes[:].bitcast(FP8X4), scales=plane[:], in_=rounded)
+            for at in range(0, width, STEP):
+                xg_mx[(j0 + at) // STEP] = (codes[:, at : at + STEP].bitcast(FP8X4), plane[:, at : at + STEP])
 
         out_codes = keep.tile([P, J], U32, name="out_codes", align_bytes=ALIGN)
         out_s = keep.tile([P, J], U8, name="out_s", align_bytes=ALIGN)
-        y_bf = keep.tile([P, J * PACK], BF16, name="y_bf", align_bytes=ALIGN)
-        gates, h_bf, h_mx, y_ps, results, emptied, ubs = {}, {}, {}, {}, {}, {}, {}
+        gates, ubs = {}, {}
+        result23 = keep.tile([P, PACK * PAIR], F32, name="result23", align_bytes=ALIGN)
 
-        def make_gate(s, b):
-            tokens = slice(s * STEP, (s + 1) * STEP)
-            ga = psum.tile([P, PACK, STEP], F32, name="ga", bufs=3)
+        def make_gate(s, b, bank):
+            ga = psum.tile([P, PACK, STEP], F32, name=f"bank{bank}")
             for t in range(PACK):
                 cols = slice(t * P, (t + 1) * P)
                 nc.tensor.matmul_mx(
                     out=ga[:, t, :], lhsT=wg_codes[b][:, cols].bitcast(FP8X4), lhsT_scale=wg_s[b][:, cols],
-                    rhs=xg_codes[:, tokens].bitcast(FP8X4), rhs_scale=xg_s[:, tokens], start=True, stop=True,
+                    rhs=xg_mx[s][0], rhs_scale=xg_mx[s][1], start=True, stop=True,
                 )
-            if (s, b) in GATE_TAG:
-                gates[s, b] = keep.tile([P, STEP, PACK], F32, name=GATE_TAG[s, b], align_bytes=ALIGN)
+            if (s, b) == (4, 0):
+                gates[s, b] = result23[:, 0:PASS].rearrange("p (j t) -> p j t", t=PACK)
+            elif (s, b) in ((0, 1), (6, 0), (7, 0), (7, 1)):
+                gates[s, b] = keep.tile([P, STEP, PACK], F32, name=f"gate{s}{b}", align_bytes=ALIGN)
             else:
                 gates[s, b] = ring.tile([P, STEP, PACK], F32, name="gate", bufs=6)
             nc.scalar.activation(gates[s, b][:], ga[:].rearrange("p t j -> p j t"), SIGMOID)
 
-        def make_ub(s, b, early=False):
-            tokens = slice(s * STEP, (s + 1) * STEP)
-            if early:
-                ub = psum.tile([P, PACK, STEP], F32, name="y_ps", bufs=2)
-            else:
-                ub = psum.tile([P, PACK, STEP], F32, name="ub", bufs=3)
-            ubs[s, b] = ub
+        def make_ub(s, b, bank):
+            ubs[s, b] = psum.tile([P, PACK, STEP], F32, name=f"bank{bank}")
             for t in range(PACK):
                 col = b * PASS + t * P
                 nc.tensor.matmul_mx(
-                    out=ub[:, t, :], lhsT=wu_codes[:, 2 * col : 2 * (col + P)].bitcast(FP4X4),
-                    lhsT_scale=scales[:, col : col + P],
-                    rhs=xg_codes[:, tokens].bitcast(FP8X4), rhs_scale=xg_s[:, tokens], start=True, stop=True,
+                    out=ubs[s, b][:, t, :], lhsT=wu_codes[:, 2 * col : 2 * (col + P)].bitcast(FP4X4),
+                    lhsT_scale=dealt["s"][:, col : col + P],
+                    rhs=xg_mx[s][0], rhs_scale=xg_mx[s][1], start=True, stop=True,
                 )
 
-        def make_h(s, b):
-            if (s, b) not in ubs:
-                make_ub(s, b)
-            ub = ubs[s, b]
-            gate = gates[s, b]
-            group, member = GROUP_OF[s]
-            if (b, member) == (0, 0):
-                steps = GROUPS[group][1]
-                if group == 0:
-                    h_bf[group] = first_h[:].rearrange("p (b s j t) -> p b s j t", b=R_PASSES, s=steps, t=PACK)
-                else:
-                    h_tile = keep.tile([P, R_PASSES, steps, STEP, PACK], BF16, name=f"h{group}", align_bytes=ALIGN)
-                    h_bf[group] = h_tile[:]
-            nc.vector.tensor_tensor(h_bf[group][:, b, member], ub[:].rearrange("p t j -> p j t"), gate[:], MULT)
+        def make_h(s, b, dst):
+            nc.vector.tensor_tensor(
+                dst.rearrange("p (j t) -> p j t", t=PACK), ubs[s, b][:].rearrange("p t j -> p j t"), gates[s, b][:], MULT
+            )
 
-        def quantize_h(group, first=0, count=R_PASSES):
-            width = GROUPS[group][1] * STEP
-            h_codes = ring.tile([P, count * width], U32, name="h_codes", align_bytes=ALIGN)
-            h_s = ring.tile([P, count * width], U8, name="h_s", align_bytes=ALIGN)
-            rounded = h_bf[group][:, first : first + count].rearrange("p b s j t -> p (b s j t)")
-            nc.vector.quantize_mx(out=h_codes[:].bitcast(FP8X4), scales=h_s[:], in_=rounded)
-            h_mx[group, first] = (h_codes, h_s)
+        def quantize_h(name, rounded, words, tag=None):
+            codes = keep.tile([P, words], U32, name=tag or name + "_codes", align_bytes=ALIGN)
+            plane = keep.tile([P, words], U8, name=name + "_s", align_bytes=ALIGN)
+            nc.vector.quantize_mx(out=codes[:].bitcast(FP8X4), scales=plane[:], in_=rounded)
+            return codes, plane
 
-        def second_stage(group, first=0, count=R_PASSES):
-            step0, steps = GROUPS[group]
-            width = steps * STEP
-            h_codes, h_s = h_mx[group, first]
-            for member in range(steps):
-                s = step0 + member
-                if first == 0:
-                    y_ps[s] = psum.tile([P, PACK, STEP], F32, name="y_ps", bufs=2)
-                for b in range(first, first + count):
-                    at = (b - first) * width + member * STEP
-                    for t in range(PACK):
-                        col = b * N + t * P
-                        nc.tensor.matmul_mx(
-                            out=y_ps[s][:, t, :], lhsT=dealt["wd"][:, col : col + P].bitcast(FP8X4),
-                            lhsT_scale=scales[SCALE_ROWS:P, col : col + P],
-                            rhs=h_codes[:, at : at + STEP].bitcast(FP8X4), rhs_scale=h_s[:, at : at + STEP],
-                            start=(b == 0 and t == 0), stop=(b == R_PASSES - 1 and t == PACK - 1),
-                        )
+        def y_bank(slices, bank):
+            return psum.tile([P, slices, PASS // slices], F32, name=f"bank{bank}")
 
-        def g_of(s, j0, width):
-            half, inside = divmod(s * STEP + j0, HALF)
-            return g_sb[half][:, :, inside : inside + width]
-
-        def round_out(s, j0=0, width=STEP):
-            at = (s * STEP + j0) * PACK
-            interleave(nc.scalar.copy, y_bf[:, at : at + width * PACK], results[s][:, :, j0 : j0 + width])
-
-        def store_out(s):
-            nc.sync.dma_start(out_rows[:, :, s * STEP : (s + 1) * STEP], results[s][:])
-
-        def finish_on_vector(s, parts=1):
-            results[s] = ring.tile([P, PACK, STEP], F32, name="result")
-            width = STEP // parts
-            for j0 in range(0, STEP, width):
-                nc.vector.tensor_tensor(
-                    results[s][:, :, j0 : j0 + width], y_ps[s][:, :, j0 : j0 + width], g_of(s, j0, width), MULT
-                )
-                if s == 0:
-                    round_on_gpsimd(y_bf[:, 0 : STEP * PACK], results[s][:])
-                else:
-                    round_out(s, j0, width)
-            store_out(s)
-
-        def empty_bank(s):
-            emptied[s] = ring.tile([P, PACK, STEP], F32, name="emptied", bufs=2)
-            nc.scalar.copy(emptied[s][:], y_ps[s][:])
-
-        def multiply_on_gpsimd(s, group):
-            results[s] = keep.tile([P, PACK, STEP], F32, name=f"h{group}", align_bytes=ALIGN)
-            nc.gpsimd.tensor_tensor(results[s][:], emptied[s][:], g_of(s, 0, STEP), MULT)
-            store_out(s)
-
-        def quantize_out(first, count, store_from=None):
-            tokens = slice(first * STEP, (first + count) * STEP)
-            rounded = y_bf[:, first * STEP * PACK : (first + count) * STEP * PACK]
-            nc.vector.quantize_mx(out=out_codes[:, tokens].bitcast(FP8X4), scales=out_s[:, tokens], in_=rounded)
-            if store_from is not None:
-                stored = slice(store_from * STEP, (first + count) * STEP)
-                nc.sync.dma_start(out_words[:, stored], out_codes[:, stored].bitcast(I32))
-
-        def store_scales(first, count, queues):
-            tokens = slice(first * STEP, (first + count) * STEP)
-            for row in range(SCALE_ROWS):
-                queues[row % len(queues)].dma_start(
-                    out_2[0, row::SCALE_ROWS, tokens].bitcast(I32), out_s[row:P:QUADRANT, tokens].bitcast(I32)
+        def second_stage(bank, first_slice, b, h_mx, at):
+            slices, width = bank.shape[1], bank.shape[2]
+            codes, plane = h_mx
+            for t in range(slices):
+                col = (first_slice + t) * P
+                nc.tensor.matmul_mx(
+                    out=bank[:, t, :], lhsT=wd_codes[:, b * N + col : b * N + col + P].bitcast(FP8X4),
+                    lhsT_scale=dealt["s"][SCALE_ROWS:P, b * N + col : b * N + col + P],
+                    rhs=codes[:, at : at + width].bitcast(FP8X4), rhs_scale=plane[:, at : at + width],
+                    start=(b == 0 and t == 0), stop=(b == R_PASSES - 1 and t == slices - 1),
                 )
 
-        deal_wu()
-        gather(0, 0, STEP)
-        gather(0, STEP, HALF - STEP)
-        gather(0, HALF, HALF)
-        for i in (1, 2):
-            gather(i, 0, STEP)
-            gather(i, STEP, J - STEP)
+        def g_of(j0, width, rows=slice(0, PACK)):
+            half, inside = divmod(j0, HALF)
+            return g_sb[half][:, rows, inside : inside + width]
+
+        def store_out(j0, result):
+            nc.sync.dma_start(out_rows[:, :, j0 : j0 + result.shape[2]], result)
+
+        def quantize_out(j0, width, rounded):
+            nc.vector.quantize_mx(
+                out=out_codes[:, j0 : j0 + width].bitcast(FP8X4), scales=out_s[:, j0 : j0 + width], in_=rounded
+            )
+
+        def store_codes(j0, width):
+            nc.sync.dma_start(out_words[:, j0 : j0 + width], out_codes[:, j0 : j0 + width].bitcast(I32))
+
+        spread(0)
+        spread(1)
+        for i in range(PACK - 1):
+            gather(early[:, i, :], i, 0, HALF)
+            gather(late_rows[:, i, :], i, HALF, HALF)
             if i == 1:
-                round_first(0, LOWER)
-                round_first(1, LOWER)
+                round_xg(0, HALF, early[:, LOWER, :], LOWER)
+                deal_wu()
+
+
+        last = PACK - 1
+        gather(early[:, last, 0:STEP], last, 0, STEP)
+        round_xg(0, STEP, early[:, UPPER, 0:STEP], UPPER)
+        gather(early[:, last, STEP:PAIR], last, STEP, STEP)
+        round_xg(STEP, STEP, early[:, UPPER, STEP:PAIR], UPPER)
+        gather(early[:, last, PAIR:HALF], last, PAIR, PAIR)
+        round_wg(nc.scalar.copy, 0, LOWER)
+        round_wg(nc.vector.tensor_copy, 0, UPPER)
+        round_xg(PAIR, PAIR, early[:, UPPER, PAIR:HALF], UPPER)
+        quantize_xg(0, STEP)
+        quantize_xg(STEP, STEP)
+        gather(late_rows[:, last, 0:STEP], last, HALF, STEP)
         deal_scales()
-        round_wg(nc.scalar.copy, 0)
-        gather(PACK - 1, 0, STEP)
-        round_first(0, UPPER)
-        gather(PACK - 1, STEP, STEP)
-        gather(PACK - 1, CHUNK, CHUNK)
-        quantize_first(0)
-        make_ub(0, 0)
-        make_ub(0, 1, early=True)
-        round_first(1, UPPER)
-        gather(PACK - 1, HALF, HALF)
-        quantize_first(1)
-        round_wg(nc.scalar.copy, 1)
+        make_ub(0, 0, 0)
+        make_ub(1, 0, 1)
+        round_wg(nc.scalar.copy, 1, LOWER)
+        round_wg(nc.vector.tensor_copy, 1, UPPER)
+        quantize_xg(PAIR, PAIR)
         quantize_wg(0)
-        round_wg(nc.vector.tensor_copy, 2)
-        round_xg(1)
-        quantize_xg(1)
-        make_gate(0, 0)
-        make_gate(1, 0)
-        make_ub(1, 0)
-        make_ub(1, 1, early=True)
-        round_wg(nc.scalar.copy, 3, 0, 32)
-        round_wg(nc.vector.tensor_copy, 3, 32, 32)
-        deal_wd()
+        round_wg(nc.scalar.copy, 2)
+        round_wg(nc.vector.tensor_copy, 3)
+        gather(late_rows[:, last, STEP:HALF], last, HALF + STEP, HALF - STEP)
+        make_gate(0, 0, 2)
+        make_gate(1, 0, 3)
+        make_gate(2, 0, 4)
+        make_ub(2, 0, 5)
+        make_gate(3, 0, 6)
+        make_ub(3, 0, 2)
         quantize_wg(1)
-        round_xg(2)
-        round_xg(3)
-        make_h(0, 0)
-        make_h(1, 0)
+        round_on_gpsimd(xg45, late_rows[:, :, 0:PAIR])
 
-        for s, b in ((2, 0), (3, 0), (0, 1), (1, 1)):
-            make_gate(s, b)
-        make_h(2, 0)
-        make_h(3, 0)
-        make_gate(2, 1)
-        make_h(0, 1)
-        make_gate(3, 1)
-        make_h(1, 1)
-        quantize_h(0)
-        quantize_xg(2)
+        make_gate(0, 1, 7)
+        make_gate(1, 1, 3)
+        deal_wd(0)
+        make_h(0, 0, h_first[:, 0:PASS])
+        make_ub(0, 1, 0)
+        make_gate(2, 1, 4)
+        make_h(1, 0, h_first[:, PASS : 2 * PASS])
+        make_ub(1, 1, 1)
+        make_gate(3, 1, 6)
+        deal_wd(1)
+        make_h(2, 0, h_first[:, 2 * PASS : 3 * PASS])
+        make_ub(2, 1, 5)
+        make_h(3, 0, h_first[:, 3 * PASS :])
+        make_ub(3, 1, 2)
+        first_mx = quantize_h("h_first", h_first, HALF)
+        quantize_xg(HALF, PAIR, xg45)
+        round_on_gpsimd(xg67, late_rows[:, :, PAIR:HALF])
 
-        def step(s):
+        make_gate(4, 0, 7)
+        make_ub(4, 0, 3)
+        make_h(0, 1, h01[:, 0:PASS])
+        make_gate(4, 1, 4)
+        upper01 = y_bank(2, 0)
+        second_stage(upper01, 2, 0, first_mx, 0)
+        make_h(1, 1, h01[:, PASS:])
+        make_gate(5, 0, 6)
+        lower01 = y_bank(2, 1)
+        second_stage(lower01, 0, 0, first_mx, 0)
+        h23 = keep.tile([P, 2 * PASS], BF16, name="gate01", align_bytes=ALIGN)
+        make_h(2, 1, h23[:, 0:PASS])
+        make_ub(5, 0, 7)
+        upper23 = y_bank(2, 5)
+        second_stage(upper23, 2, 0, first_mx, PAIR)
+        make_h(3, 1, h23[:, PASS:])
+        make_gate(5, 1, 4)
+        make_ub(4, 1, 2)
+        mx01 = quantize_h("h01", h01, PAIR)
+        second_stage(upper01, 2, 1, mx01, 0)
+        second_stage(lower01, 0, 1, mx01, 0)
+        quantize_xg(HALF + PAIR, PAIR, xg67)
+        mx23 = quantize_h("h23", h23[:], PAIR)
+        second_stage(upper23, 2, 1, mx23, 0)
+        make_ub(5, 1, 6)
+
+        result45 = keep.tile([P, PACK * PAIR], F32, name="result45", align_bytes=ALIGN)
+        result01 = keep.tile([P, PACK * PAIR], F32, name="result01")
+        results = [tile[:].rearrange("p (t j) -> p t j", t=PACK) for tile in (result01, result23, result45)]
+        emptied = [keep.tile([P, 2, PAIR], F32, name=f"emptied{n}") for n in range(3)]
+        h45_second = result23[:, 0:PASS].bitcast(BF16)
+        h6 = result45[:, 0:PASS].bitcast(BF16).rearrange("p (b w) -> p b w", b=R_PASSES)
+        h7 = result45[:, PASS:].bitcast(BF16).rearrange("p (b w) -> p b w", b=R_PASSES)
+        nc.scalar.copy(emptied[0][:], upper01[:])
+        nc.scalar.copy(emptied[1][:], upper23[:])
+        make_h(4, 0, xg67[:, 0:PASS])
+        make_gate(6, 0, 4)
+        lower23 = y_bank(2, 0)
+        second_stage(lower23, 0, 0, first_mx, PAIR)
+        second_stage(lower23, 0, 1, mx23, 0)
+        make_ub(6, 0, 3)
+        make_h(5, 0, xg67[:, PASS:])
+        nc.vector.tensor_tensor(results[0][:, LOWER], lower01[:], g_of(0, PAIR, LOWER), MULT)
+        nc.gpsimd.tensor_tensor(results[0][:, UPPER], emptied[0][:], g_of(0, PAIR, UPPER), MULT)
+        store_out(0, results[0])
+        nc.gpsimd.tensor_tensor(results[1][:, UPPER], emptied[1][:], g_of(PAIR, PAIR, UPPER), MULT)
+        make_gate(6, 1, 5)
+        nc.scalar.copy(emptied[2][:], lower23[:])
+        make_ub(6, 1, 1)
+        make_h(4, 1, h45_second[:, 0:PASS])
+        make_gate(7, 0, 7)
+        make_gate(7, 1, 2)
+        make_ub(7, 0, 4)
+        make_h(5, 1, h45_second[:, PASS:])
+        make_ub(7, 1, 5)
+        make_h(6, 0, h6[:, 0])
+        mx45 = [quantize_h("h45_first", xg67, PAIR, "gate60"), quantize_h("h45_second", h45_second, PAIR)]
+        nc.gpsimd.tensor_tensor(results[1][:, LOWER], emptied[2][:], g_of(PAIR, PAIR, LOWER), MULT)
+        store_out(PAIR, results[1])
+        interleave(nc.scalar.copy, xg67, results[0])
+
+        lower45, upper45 = y_bank(2, 0), y_bank(2, 6)
+        for bank, first_slice in ((lower45, 0), (upper45, 2)):
             for b in range(R_PASSES):
-                if s + 1 < STEPS:
-                    make_gate(s + 1, b)
-                make_h(s, b)
-
-        make_gate(4, 0)
-        make_h(2, 1)
-        make_gate(4, 1)
-        make_h(3, 1)
-        second_stage(0)
-        empty_bank(1)
-        finish_on_vector(0)
-        step(4)
-        quantize_h(1)
-        quantize_h(2)
-        quantize_xg(3)
-        multiply_on_gpsimd(1, 2)
-
-        second_stage(1)
-        empty_bank(3)
-        finish_on_vector(2)
-        step(5)
-        second_stage(2)
-        round_out(1)
-        finish_on_vector(4)
-        quantize_h(3)
-        multiply_on_gpsimd(3, 3)
-
-        step(6)
-        second_stage(3)
-        round_out(3)
-        finish_on_vector(5)
-        quantize_h(4)
-        quantize_out(0, 2, 0)
-        store_scales(0, 2, [nc.sync])
-
-        last = len(GROUPS) - 1
-        make_h(STEPS - 1, 0)
-        second_stage(4)
-        make_h(STEPS - 1, 1)
-        quantize_h(last, 0, 1)
-        second_stage(last, 0, 1)
-        quantize_out(2, 2, 2)
-        quantize_h(last, 1, 1)
-        second_stage(last, 1, 1)
-        finish_on_vector(STEPS - 2)
-        quantize_out(4, 2, 4)
-        finish_on_vector(STEPS - 1, parts=2)
-        quantize_out(STEPS - 2, 1)
-        quantize_out(STEPS - 1, 1, STEPS - 2)
-        store_scales(2, 6, [nc.scalar, nc.sync])
+                second_stage(bank, first_slice, b, mx45[b], 0)
+        make_h(6, 1, h6[:, 1])
+        make_h(7, 0, h7[:, 0])
+        staged = [xg67] + [keep.tile([P, PAIR * PACK], BF16, name=n, align_bytes=ALIGN) for n in ("gate70", "last")]
+        interleave(nc.scalar.copy, staged[1][:], results[1])
+        make_h(7, 1, h7[:, 1])
+        mx6 = quantize_h("h6", h6[:].rearrange("p b w -> p (b w)"), PAIR, "gate71")
+        mx7 = quantize_h("h7", h7[:].rearrange("p b w -> p (b w)"), PAIR)
+        y6, y7 = y_bank(PACK, 3), y_bank(PACK, 1)
+        for bank, mx in ((y6, mx6), (y7, mx7)):
+            for b in range(R_PASSES):
+                second_stage(bank, 0, b, mx, b * STEP)
+        nc.vector.tensor_tensor(results[2][:, LOWER], lower45[:], g_of(HALF, PAIR, LOWER), MULT)
+        nc.vector.tensor_tensor(results[2][:, UPPER], upper45[:], g_of(HALF, PAIR, UPPER), MULT)
+        store_out(HALF, results[2])
+        quantize_out(0, PAIR, staged[0][:])
+        store_codes(0, PAIR)
+        quantize_out(PAIR, PAIR, staged[1][:])
+        interleave(nc.scalar.copy, staged[1][:], results[2])
+        j6, j7 = 6 * STEP, 7 * STEP
+        result6 = staged[0][:].bitcast(F32).rearrange("p (t j) -> p t j", t=PACK)
+        result7 = keep.tile([P, PACK, STEP], F32, name="result7")
+        nc.vector.tensor_tensor(result6, y6[:], g_of(j6, STEP), MULT)
+        store_out(j6, result6)
+        interleave(nc.scalar.copy, staged[2][:, 0:PASS], result6)
+        nc.vector.tensor_tensor(result7[:], y7[:], g_of(j7, STEP), MULT)
+        store_out(j7, result7[:])
+        quantize_out(HALF, PAIR, staged[1][:])
+        store_codes(PAIR, HALF)
+        interleave(nc.vector.tensor_copy, staged[2][:, PASS:], result7[:])
+        quantize_out(j6, STEP, staged[2][:, 0:PASS])
+        quantize_out(j7, STEP, staged[2][:, PASS:])
+        store_codes(j6, PAIR)
+        for row in range(SCALE_ROWS):
+            queue = nc.scalar if row % 2 == 0 else nc.sync
+            queue.dma_start(out_2[0, row::SCALE_ROWS, :].bitcast(I32), out_s[row:P:QUADRANT, :].bitcast(I32))

@@ -201,7 +201,7 @@ def tile_list_sigm_mulP_kernel(
                 )
             if (s, b) == (4, 0):
                 gates[s, b] = result23[:, 0:PASS].rearrange("p (j t) -> p j t", t=PACK)
-            elif (s, b) in ((0, 1), (6, 0), (7, 0), (7, 1)):
+            elif (s, b) in ((0, 1), (6, 0), (6, 1), (7, 0)):
                 gates[s, b] = keep.tile([P, STEP, PACK], F32, name=f"gate{s}{b}", align_bytes=ALIGN)
             else:
                 gates[s, b] = ring.tile([P, STEP, PACK], F32, name="gate", bufs=6)
@@ -247,8 +247,8 @@ def tile_list_sigm_mulP_kernel(
             half, inside = divmod(j0, HALF)
             return g_sb[half][:, rows, inside : inside + width]
 
-        def store_out(j0, result):
-            nc.sync.dma_start(out_rows[:, :, j0 : j0 + result.shape[2]], result)
+        def store_out(j0, result, rows=slice(0, PACK)):
+            nc.sync.dma_start(out_rows[:, rows, j0 : j0 + result.shape[2]], result[:, rows])
 
         def quantize_out(j0, width, rounded):
             nc.vector.quantize_mx(
@@ -343,13 +343,15 @@ def tile_list_sigm_mulP_kernel(
         second_stage(upper23, 2, 1, mx23, 0)
         make_ub(5, 1, 6)
 
-        result45 = keep.tile([P, PACK * PAIR], F32, name="result45", align_bytes=ALIGN)
+        result45 = keep.tile([P, 7 * PAIR], F32, name="result45", align_bytes=ALIGN)
         result01 = keep.tile([P, PACK * PAIR], F32, name="result01")
-        results = [tile[:].rearrange("p (t j) -> p t j", t=PACK) for tile in (result01, result23, result45)]
-        emptied = [keep.tile([P, 2, PAIR], F32, name=f"emptied{n}") for n in range(3)]
+        results = [t[:, 0 : 2 * PASS].rearrange("p (t j) -> p t j", t=PACK) for t in (result01, result23, result45)]
+        emptied = [keep.tile([P, 2, PAIR], F32, name=f"emptied{n}")[:] for n in range(2)]
+        emptied.append(result45[:, 7 * STEP : 11 * STEP].rearrange("p (t j) -> p t j", t=2))
         h45_second = result23[:, 0:PASS].bitcast(BF16)
-        h6 = result45[:, 0:PASS].bitcast(BF16).rearrange("p (b w) -> p b w", b=R_PASSES)
-        h7 = result45[:, PASS:].bitcast(BF16).rearrange("p (b w) -> p b w", b=R_PASSES)
+        h6 = keep.tile([P, R_PASSES, PASS], BF16, name="h6", align_bytes=ALIGN)
+        h70 = keep.tile([P, PASS], BF16, name="h70", align_bytes=ALIGN)
+        h71 = result45[:, 4 * PAIR : 5 * PAIR].bitcast(BF16)
         nc.scalar.copy(emptied[0][:], upper01[:])
         nc.scalar.copy(emptied[1][:], upper23[:])
         make_h(4, 0, xg67[:, 0:PASS])
@@ -363,6 +365,7 @@ def tile_list_sigm_mulP_kernel(
         nc.gpsimd.tensor_tensor(results[0][:, UPPER], emptied[0][:], g_of(0, PAIR, UPPER), MULT)
         store_out(0, results[0])
         nc.gpsimd.tensor_tensor(results[1][:, UPPER], emptied[1][:], g_of(PAIR, PAIR, UPPER), MULT)
+        store_out(PAIR, results[1], UPPER)
         make_gate(6, 1, 5)
         nc.scalar.copy(emptied[2][:], lower23[:])
         make_ub(6, 1, 1)
@@ -375,7 +378,7 @@ def tile_list_sigm_mulP_kernel(
         make_h(6, 0, h6[:, 0])
         mx45 = [quantize_h("h45_first", xg67, PAIR, "gate60"), quantize_h("h45_second", h45_second, PAIR)]
         nc.gpsimd.tensor_tensor(results[1][:, LOWER], emptied[2][:], g_of(PAIR, PAIR, LOWER), MULT)
-        store_out(PAIR, results[1])
+        store_out(PAIR, results[1], LOWER)
         interleave(nc.scalar.copy, xg67, results[0])
 
         lower45, upper45 = y_bank(2, 0), y_bank(2, 6)
@@ -383,37 +386,37 @@ def tile_list_sigm_mulP_kernel(
             for b in range(R_PASSES):
                 second_stage(bank, first_slice, b, mx45[b], 0)
         make_h(6, 1, h6[:, 1])
-        make_h(7, 0, h7[:, 0])
-        staged = [xg67] + [keep.tile([P, PAIR * PACK], BF16, name=n, align_bytes=ALIGN) for n in ("gate70", "last")]
-        interleave(nc.scalar.copy, staged[1][:], results[1])
-        make_h(7, 1, h7[:, 1])
-        mx6 = quantize_h("h6", h6[:].rearrange("p b w -> p (b w)"), PAIR, "gate71")
-        mx7 = quantize_h("h7", h7[:].rearrange("p b w -> p (b w)"), PAIR)
-        y6, y7 = y_bank(PACK, 3), y_bank(PACK, 1)
-        for bank, mx in ((y6, mx6), (y7, mx7)):
-            for b in range(R_PASSES):
-                second_stage(bank, 0, b, mx, b * STEP)
+        make_h(7, 0, h70[:])
+        staged = [xg67] + [keep.tile([P, PAIR * PACK], BF16, name=n, align_bytes=ALIGN)[:] for n in ("gate61", "y45", "y67")]
+        interleave(nc.scalar.copy, staged[1], results[1])
         nc.vector.tensor_tensor(results[2][:, LOWER], lower45[:], g_of(HALF, PAIR, LOWER), MULT)
+        store_out(HALF, results[2], LOWER)
+        mx6 = quantize_h("h6", h6[:].rearrange("p b w -> p (b w)"), PAIR, "gate70")
+        y6, y7 = y_bank(PACK, 3), y_bank(PACK, 1)
+        for b in range(R_PASSES):
+            second_stage(y6, 0, b, mx6, b * STEP)
+        second_stage(y7, 0, 0, quantize_h("h70", h70[:], STEP), 0)
+        make_h(7, 1, h71)
         nc.vector.tensor_tensor(results[2][:, UPPER], upper45[:], g_of(HALF, PAIR, UPPER), MULT)
-        store_out(HALF, results[2])
-        quantize_out(0, PAIR, staged[0][:])
-        store_codes(0, PAIR)
-        quantize_out(PAIR, PAIR, staged[1][:])
-        interleave(nc.scalar.copy, staged[1][:], results[2])
+        store_out(HALF, results[2], UPPER)
+        interleave(nc.scalar.copy, staged[2], results[2])
+        second_stage(y7, 0, 1, quantize_h("h71", h71, STEP), 0)
         j6, j7 = 6 * STEP, 7 * STEP
-        result6 = staged[0][:].bitcast(F32).rearrange("p (t j) -> p t j", t=PACK)
+        result6 = result45[:, 5 * PAIR :].rearrange("p (t j) -> p t j", t=PACK)
         result7 = keep.tile([P, PACK, STEP], F32, name="result7")
         nc.vector.tensor_tensor(result6, y6[:], g_of(j6, STEP), MULT)
         store_out(j6, result6)
-        interleave(nc.scalar.copy, staged[2][:, 0:PASS], result6)
+        interleave(nc.scalar.copy, staged[3][:, 0:PASS], result6)
+        quantize_out(0, PAIR, staged[0])
+        quantize_out(PAIR, PAIR, staged[1])
+        store_codes(0, HALF)
         nc.vector.tensor_tensor(result7[:], y7[:], g_of(j7, STEP), MULT)
         store_out(j7, result7[:])
-        quantize_out(HALF, PAIR, staged[1][:])
-        store_codes(PAIR, HALF)
-        interleave(nc.vector.tensor_copy, staged[2][:, PASS:], result7[:])
-        quantize_out(j6, STEP, staged[2][:, 0:PASS])
-        quantize_out(j7, STEP, staged[2][:, PASS:])
-        store_codes(j6, PAIR)
+        quantize_out(HALF, PAIR, staged[2])
+        interleave(nc.vector.tensor_copy, staged[3][:, PASS:], result7[:])
+        quantize_out(j6, STEP, staged[3][:, 0:PASS])
+        quantize_out(j7, STEP, staged[3][:, PASS:])
+        store_codes(HALF, HALF)
         for row in range(SCALE_ROWS):
             queue = nc.scalar if row % 2 == 0 else nc.sync
             queue.dma_start(out_2[0, row::SCALE_ROWS, :].bitcast(I32), out_s[row:P:QUADRANT, :].bitcast(I32))

@@ -413,10 +413,11 @@ def tile_list_sigm_mulP_kernel(
         nc.vector.tensor_tensor(result7[:], y7[:], g_of(j7, STEP), MULT)
         store_out(j7, result7[:])
         quantize_out(HALF, PAIR, staged[2])
+        store_codes(HALF, PAIR)
         interleave(nc.vector.tensor_copy, staged[3][:, PASS:], result7[:])
         quantize_out(j6, STEP, staged[3][:, 0:PASS])
         quantize_out(j7, STEP, staged[3][:, PASS:])
-        store_codes(HALF, HALF)
+        store_codes(j6, PAIR)
         for row in range(SCALE_ROWS):
             queue = nc.scalar if row % 2 == 0 else nc.sync
             queue.dma_start(out_2[0, row::SCALE_ROWS, :].bitcast(I32), out_s[row:P:QUADRANT, :].bitcast(I32))

@@ -107,10 +107,10 @@ def tile_list_sigm_mulP_kernel(
             nc.vector.transpose(wgt_turned[:, j0 : j0 + QUADRANT], wgt_cut[:, j0 : j0 + QUADRANT])
         cuts = HALF // CUT
 
-        def spread(half):
+        def spread(copy, half):
             repeated = keep.tile([P, HALF], F32, name=f"wgt_repeated{half}", align_bytes=ALIGN)
             source = wgt_turned[:].rearrange("p (sa c) -> p c sa", c=HEAD)[:, half * cuts : (half + 1) * cuts, :]
-            nc.scalar.copy(
+            copy(
                 repeated[:].rearrange("p (c sa rep) -> p c sa rep", c=cuts, rep=HEAD),
                 source.unsqueeze(3).to_broadcast([P, cuts, CUT // HEAD, HEAD]),
             )
@@ -186,9 +186,10 @@ def tile_list_sigm_mulP_kernel(
             for at in range(0, width, STEP):
                 xg_mx[(j0 + at) // STEP] = (codes[:, at : at + STEP].bitcast(FP8X4), plane[:, at : at + STEP])
 
-        out_codes = keep.tile([P, J], U32, name="out_codes", align_bytes=ALIGN)
+        out_codes = {}
         out_s = keep.tile([P, J], U8, name="out_s", align_bytes=ALIGN)
         gates, ubs = {}, {}
+        chain = keep.tile([P, PASS], F32, name="chain", align_bytes=ALIGN)
         result23 = keep.tile([P, PACK * PAIR], F32, name="result23", align_bytes=ALIGN)
 
         def make_gate(s, b, bank):
@@ -200,8 +201,8 @@ def tile_list_sigm_mulP_kernel(
                     rhs=xg_mx[s][0], rhs_scale=xg_mx[s][1], start=True, stop=True,
                 )
             if (s, b) == (4, 0):
-                gates[s, b] = result23[:, 0:PASS].rearrange("p (j t) -> p j t", t=PACK)
-            elif (s, b) in ((0, 1), (6, 0), (6, 1), (7, 0)):
+                gates[s, b] = chain[:].rearrange("p (j t) -> p j t", t=PACK)
+            elif (s, b) in ((0, 1), (6, 1), (7, 0), (7, 1)):
                 gates[s, b] = keep.tile([P, STEP, PACK], F32, name=f"gate{s}{b}", align_bytes=ALIGN)
             else:
                 gates[s, b] = ring.tile([P, STEP, PACK], F32, name="gate", bufs=6)
@@ -250,16 +251,22 @@ def tile_list_sigm_mulP_kernel(
         def store_out(j0, result, rows=slice(0, PACK)):
             nc.sync.dma_start(out_rows[:, rows, j0 : j0 + result.shape[2]], result[:, rows])
 
+        def codes_of(j0, width):
+            half, inside = divmod(j0, HALF)
+            if half not in out_codes:
+                out_codes[half] = keep.tile([P, HALF], U32, name=("gate71", "out_codes")[half], align_bytes=ALIGN)
+            return out_codes[half][:, inside : inside + width]
+
         def quantize_out(j0, width, rounded):
             nc.vector.quantize_mx(
-                out=out_codes[:, j0 : j0 + width].bitcast(FP8X4), scales=out_s[:, j0 : j0 + width], in_=rounded
+                out=codes_of(j0, width).bitcast(FP8X4), scales=out_s[:, j0 : j0 + width], in_=rounded
             )
 
         def store_codes(j0, width):
-            nc.sync.dma_start(out_words[:, j0 : j0 + width], out_codes[:, j0 : j0 + width].bitcast(I32))
+            nc.sync.dma_start(out_words[:, j0 : j0 + width], codes_of(j0, width).bitcast(I32))
 
-        spread(0)
-        spread(1)
+        spread(nc.vector.tensor_copy, 0)
+        spread(nc.scalar.copy, 1)
         for i in range(PACK - 1):
             gather(early[:, i, :], i, 0, HALF)
             gather(late_rows[:, i, :], i, HALF, HALF)
@@ -343,81 +350,78 @@ def tile_list_sigm_mulP_kernel(
         second_stage(upper23, 2, 1, mx23, 0)
         make_ub(5, 1, 6)
 
-        result45 = keep.tile([P, 7 * PAIR], F32, name="result45", align_bytes=ALIGN)
+        result45 = keep.tile([P, PACK * PAIR], F32, name="result45", align_bytes=ALIGN)
         result01 = keep.tile([P, PACK * PAIR], F32, name="result01")
-        results = [t[:, 0 : 2 * PASS].rearrange("p (t j) -> p t j", t=PACK) for t in (result01, result23, result45)]
-        emptied = [keep.tile([P, 2, PAIR], F32, name=f"emptied{n}")[:] for n in range(2)]
-        emptied.append(result45[:, 7 * STEP : 11 * STEP].rearrange("p (t j) -> p t j", t=2))
-        h45_second = result23[:, 0:PASS].bitcast(BF16)
-        h6 = keep.tile([P, R_PASSES, PASS], BF16, name="h6", align_bytes=ALIGN)
-        h70 = keep.tile([P, PASS], BF16, name="h70", align_bytes=ALIGN)
-        h71 = result45[:, 4 * PAIR : 5 * PAIR].bitcast(BF16)
-        nc.scalar.copy(emptied[0][:], upper01[:])
-        nc.scalar.copy(emptied[1][:], upper23[:])
+        results = [t[:].rearrange("p (t j) -> p t j", t=PACK) for t in (result01, result23, result45)]
+        emptied = [keep.tile([P, 2, PAIR], F32, name=f"emptied{n}")[:] for n in range(2)] + [results[2][:, UPPER]]
+        h45_second = chain[:].bitcast(BF16)
+        h6 = result23[:, 0:PASS].bitcast(BF16)
+        h7 = xg67
+        nc.scalar.copy(emptied[0], upper01[:])
+        nc.scalar.copy(emptied[1], upper23[:])
         make_h(4, 0, xg67[:, 0:PASS])
         make_gate(6, 0, 4)
+        make_ub(6, 0, 3)
+        make_h(5, 0, xg67[:, PASS:])
+        make_gate(6, 1, 7)
         lower23 = y_bank(2, 0)
         second_stage(lower23, 0, 0, first_mx, PAIR)
         second_stage(lower23, 0, 1, mx23, 0)
-        make_ub(6, 0, 3)
-        make_h(5, 0, xg67[:, PASS:])
         nc.vector.tensor_tensor(results[0][:, LOWER], lower01[:], g_of(0, PAIR, LOWER), MULT)
-        nc.gpsimd.tensor_tensor(results[0][:, UPPER], emptied[0][:], g_of(0, PAIR, UPPER), MULT)
+        nc.gpsimd.tensor_tensor(results[0][:, UPPER], emptied[0], g_of(0, PAIR, UPPER), MULT)
         store_out(0, results[0])
-        nc.gpsimd.tensor_tensor(results[1][:, UPPER], emptied[1][:], g_of(PAIR, PAIR, UPPER), MULT)
+        nc.gpsimd.tensor_tensor(results[1][:, UPPER], emptied[1], g_of(PAIR, PAIR, UPPER), MULT)
         store_out(PAIR, results[1], UPPER)
-        make_gate(6, 1, 5)
-        nc.scalar.copy(emptied[2][:], lower23[:])
-        make_ub(6, 1, 1)
+        nc.scalar.copy(emptied[2], lower23[:])
+        make_ub(6, 1, 5)
+        make_ub(7, 0, 1)
         make_h(4, 1, h45_second[:, 0:PASS])
-        make_gate(7, 0, 7)
+        make_gate(7, 0, 4)
         make_gate(7, 1, 2)
-        make_ub(7, 0, 4)
+        make_ub(7, 1, 7)
         make_h(5, 1, h45_second[:, PASS:])
-        make_ub(7, 1, 5)
-        make_h(6, 0, h6[:, 0])
-        mx45 = [quantize_h("h45_first", xg67, PAIR, "gate60"), quantize_h("h45_second", h45_second, PAIR)]
-        nc.gpsimd.tensor_tensor(results[1][:, LOWER], emptied[2][:], g_of(PAIR, PAIR, LOWER), MULT)
+        make_h(6, 0, h6[:, 0:PASS])
+        make_h(6, 1, h6[:, PASS:])
+        mx45 = [quantize_h("h45_first", xg67, PAIR, "gate61"), quantize_h("h45_second", h45_second, PAIR)]
+        mx6 = quantize_h("h6", h6, PAIR)
+        nc.gpsimd.tensor_tensor(results[1][:, LOWER], emptied[2], g_of(PAIR, PAIR, LOWER), MULT)
         store_out(PAIR, results[1], LOWER)
-        interleave(nc.scalar.copy, xg67, results[0])
+        staged = [h45_second] + [keep.tile([P, PAIR * PACK], BF16, name=n, align_bytes=ALIGN)[:] for n in ("y23", "y45", "y67")]
+        interleave(nc.scalar.copy, staged[0], results[0])
+        interleave(nc.scalar.copy, staged[1], results[1])
 
-        lower45, upper45 = y_bank(2, 0), y_bank(2, 6)
+        lower45, upper45, y6 = y_bank(2, 0), y_bank(2, 6), y_bank(PACK, 3)
         for bank, first_slice in ((lower45, 0), (upper45, 2)):
             for b in range(R_PASSES):
                 second_stage(bank, first_slice, b, mx45[b], 0)
-        make_h(6, 1, h6[:, 1])
-        make_h(7, 0, h70[:])
-        staged = [xg67] + [keep.tile([P, PAIR * PACK], BF16, name=n, align_bytes=ALIGN)[:] for n in ("gate61", "y45", "y67")]
-        interleave(nc.scalar.copy, staged[1], results[1])
-        nc.vector.tensor_tensor(results[2][:, LOWER], lower45[:], g_of(HALF, PAIR, LOWER), MULT)
-        store_out(HALF, results[2], LOWER)
-        mx6 = quantize_h("h6", h6[:].rearrange("p b w -> p (b w)"), PAIR, "gate70")
-        y6, y7 = y_bank(PACK, 3), y_bank(PACK, 1)
         for b in range(R_PASSES):
             second_stage(y6, 0, b, mx6, b * STEP)
-        second_stage(y7, 0, 0, quantize_h("h70", h70[:], STEP), 0)
-        make_h(7, 1, h71)
+        make_h(7, 1, h7[:, PASS:])
+        make_h(7, 0, h7[:, 0:PASS])
+        nc.vector.tensor_tensor(results[2][:, LOWER], lower45[:], g_of(HALF, PAIR, LOWER), MULT)
+        store_out(HALF, results[2], LOWER)
+        mx7 = quantize_h("h7", h7, PAIR, "gate70")
+        y7 = y_bank(PACK, 5)
+        for b in range(R_PASSES):
+            second_stage(y7, 0, b, mx7, b * STEP)
         nc.vector.tensor_tensor(results[2][:, UPPER], upper45[:], g_of(HALF, PAIR, UPPER), MULT)
         store_out(HALF, results[2], UPPER)
         interleave(nc.scalar.copy, staged[2], results[2])
-        second_stage(y7, 0, 1, quantize_h("h71", h71, STEP), 0)
         j6, j7 = 6 * STEP, 7 * STEP
-        result6 = result45[:, 5 * PAIR :].rearrange("p (t j) -> p t j", t=PACK)
-        result7 = keep.tile([P, PACK, STEP], F32, name="result7")
+        result6, result7 = [g_sb[0][:, row, :].rearrange("p (t j) -> p t j", t=PACK) for row in range(2)]
         nc.vector.tensor_tensor(result6, y6[:], g_of(j6, STEP), MULT)
         store_out(j6, result6)
         interleave(nc.scalar.copy, staged[3][:, 0:PASS], result6)
         quantize_out(0, PAIR, staged[0])
+        nc.vector.tensor_tensor(result7, y7[:], g_of(j7, STEP), MULT)
+        store_out(j7, result7)
         quantize_out(PAIR, PAIR, staged[1])
         store_codes(0, HALF)
-        nc.vector.tensor_tensor(result7[:], y7[:], g_of(j7, STEP), MULT)
-        store_out(j7, result7[:])
+        interleave(nc.vector.tensor_copy, staged[3][:, PASS:], result7)
         quantize_out(HALF, PAIR, staged[2])
-        store_codes(HALF, PAIR)
-        interleave(nc.vector.tensor_copy, staged[3][:, PASS:], result7[:])
         quantize_out(j6, STEP, staged[3][:, 0:PASS])
         quantize_out(j7, STEP, staged[3][:, PASS:])
-        store_codes(j6, PAIR)
+        store_codes(HALF, HALF)
         for row in range(SCALE_ROWS):
             queue = nc.scalar if row % 2 == 0 else nc.sync
             queue.dma_start(out_2[0, row::SCALE_ROWS, :].bitcast(I32), out_s[row:P:QUADRANT, :].bitcast(I32))

@@ -32,7 +32,7 @@ HALF = J // 2
 LOWER, UPPER = slice(0, 2), slice(2, PACK)
 PIECE = PASS // 2
 PIECE_M = PIECE // PACK
-ALIGN = 64
+ALIGN = 256
 
 
 def tile_list_sigm_mulP_kernel(
@@ -364,7 +364,8 @@ def tile_list_sigm_mulP_kernel(
         make_ub(6, 0, 3)
         make_h(5, 0, xg67[:, PASS:])
         make_gate(6, 1, 7)
-        lower23 = y_bank(2, 0)
+        make_ub(6, 1, 0)
+        lower23 = y_bank(2, 5)
         second_stage(lower23, 0, 0, first_mx, PAIR)
         second_stage(lower23, 0, 1, mx23, 0)
         nc.vector.tensor_tensor(results[0][:, LOWER], lower01[:], g_of(0, PAIR, LOWER), MULT)
@@ -373,7 +374,6 @@ def tile_list_sigm_mulP_kernel(
         nc.gpsimd.tensor_tensor(results[1][:, UPPER], emptied[1], g_of(PAIR, PAIR, UPPER), MULT)
         store_out(PAIR, results[1], UPPER)
         nc.scalar.copy(emptied[2], lower23[:])
-        make_ub(6, 1, 5)
         make_ub(7, 0, 1)
         make_h(4, 1, h45_second[:, 0:PASS])
         make_gate(7, 0, 4)
@@ -390,7 +390,7 @@ def tile_list_sigm_mulP_kernel(
         interleave(nc.scalar.copy, staged[0], results[0])
         interleave(nc.scalar.copy, staged[1], results[1])
 
-        lower45, upper45, y6 = y_bank(2, 0), y_bank(2, 6), y_bank(PACK, 3)
+        lower45, upper45, y6 = y_bank(2, 5), y_bank(2, 6), y_bank(PACK, 3)
         for bank, first_slice in ((lower45, 0), (upper45, 2)):
             for b in range(R_PASSES):
                 second_stage(bank, first_slice, b, mx45[b], 0)
@@ -401,7 +401,7 @@ def tile_list_sigm_mulP_kernel(
         nc.vector.tensor_tensor(results[2][:, LOWER], lower45[:], g_of(HALF, PAIR, LOWER), MULT)
         store_out(HALF, results[2], LOWER)
         mx7 = quantize_h("h7", h7, PAIR, "gate70")
-        y7 = y_bank(PACK, 5)
+        y7 = y_bank(PACK, 0)
         for b in range(R_PASSES):
             second_stage(y7, 0, b, mx7, b * STEP)
         nc.vector.tensor_tensor(results[2][:, UPPER], upper45[:], g_of(HALF, PAIR, UPPER), MULT)

@@ -70,8 +70,8 @@ def tile_list_sigm_mulP_kernel(
             nc.sync.dma_start(wg_raw[u], wg_rows[:, :, u * PIECE : (u + 1) * PIECE])
 
         nc.sync.dma_start(wgt_cut[:], wgt[0:P:HEAD, :].rearrange("a (c j) -> a c j", j=CUT))
-        nc.sync.dma_start(offsets[:], offs)
         nc.sync.dma_start(planes[0][:], x_rows[:, 0, :])
+        nc.sync.dma_start(offsets[:], offs)
         nc.sync.dma_start(planes[1][:], x_rows[:, 1, :])
         nc.sync.dma_start(wu_raw[:].bitcast(I32), wu_words[0].bitcast(I32))
         for row in range(SCALE_ROWS):
@@ -127,9 +127,9 @@ def tile_list_sigm_mulP_kernel(
             )
 
         def deal_scales():
-            dealt["s"] = keep.tile([P, R], U8, name="wgt0", align_bytes=ALIGN)
+            dealt["s"] = keep.tile([P, R_PASSES * PACK, 2 * P], U8, name="wgt0", align_bytes=ALIGN)
             nc.vector.tensor_copy(
-                dealt["s"][:].rearrange("p (b t m) -> p b t m", b=R_PASSES, t=PACK),
+                dealt["s"][:, :, 0:P].rearrange("p (b t) m -> p b t m", b=R_PASSES),
                 scales_raw[:].rearrange("p (b m t) -> p b t m", b=R_PASSES, t=PACK),
             )
 
@@ -205,7 +205,7 @@ def tile_list_sigm_mulP_kernel(
             elif (s, b) in ((0, 1), (6, 1), (7, 0), (7, 1)):
                 gates[s, b] = keep.tile([P, STEP, PACK], F32, name=f"gate{s}{b}", align_bytes=ALIGN)
             else:
-                gates[s, b] = ring.tile([P, STEP, PACK], F32, name="gate", bufs=6)
+                gates[s, b] = ring.tile([P, STEP, PACK], F32, name="gate", bufs=6, align_bytes=ALIGN)
             nc.scalar.activation(gates[s, b][:], ga[:].rearrange("p t j -> p j t"), SIGMOID)
 
         def make_ub(s, b, bank):
@@ -214,7 +214,7 @@ def tile_list_sigm_mulP_kernel(
                 col = b * PASS + t * P
                 nc.tensor.matmul_mx(
                     out=ubs[s, b][:, t, :], lhsT=wu_codes[:, 2 * col : 2 * (col + P)].bitcast(FP4X4),
-                    lhsT_scale=dealt["s"][:, col : col + P],
+                    lhsT_scale=dealt["s"][:, b * PACK + t, 0:P],
                     rhs=xg_mx[s][0], rhs_scale=xg_mx[s][1], start=True, stop=True,
                 )
 
@@ -239,7 +239,7 @@ def tile_list_sigm_mulP_kernel(
                 col = (first_slice + t) * P
                 nc.tensor.matmul_mx(
                     out=bank[:, t, :], lhsT=wd_codes[:, b * N + col : b * N + col + P].bitcast(FP8X4),
-                    lhsT_scale=dealt["s"][SCALE_ROWS:P, b * N + col : b * N + col + P],
+                    lhsT_scale=dealt["s"][SCALE_ROWS:P, b * PACK + first_slice + t, 0:P],
                     rhs=codes[:, at : at + width].bitcast(FP8X4), rhs_scale=plane[:, at : at + width],
                     start=(b == 0 and t == 0), stop=(b == R_PASSES - 1 and t == slices - 1),
                 )

from contextlib import ExitStack

import concourse.mybir as mybir

K, R, N, T, J = 512, 1024, 512, 2048, 1024
FLOPS = 2 * (2 * K * R * J + R * N * J)

F32 = mybir.dt.float32
BF16 = mybir.dt.bfloat16
I32 = mybir.dt.int32
U32 = mybir.dt.uint32
U16 = mybir.dt.uint16
U8 = mybir.dt.uint8
FP8X4 = mybir.dt.float8_e4m3fn_x4
FP4X4 = mybir.dt.float4_e2m1fn_x4
MULT = mybir.AluOpType.mult
ADD = mybir.AluOpType.add
SIGMOID = mybir.ActivationFunctionType.Sigmoid

P = 128
PACK = 4
PASS = P * PACK
R_PASSES = R // PASS
QUADRANTS, QUADRANT = 4, 32
SCALE_ROWS = 4
HEAD = 16
CUT = J // HEAD
LINE = 4
STEP = 128
PAIR = 2 * STEP
HALF = J // 2
LOWER, UPPER = slice(0, 2), slice(2, PACK)
PIECE = PASS // 2
PIECE_M = PIECE // PACK
ALIGN = 256


def tile_list_sigm_mulP_kernel(
    tc, xT, wgt, wg, wu_words, wu_scales, wd_words, wd_scales, g, offs, out_0, out_1, out_2
):
    nc = tc.nc
    with ExitStack() as ctx:
        keep = ctx.enter_context(tc.tile_pool(name="keep", bufs=1))
        ring = ctx.enter_context(tc.tile_pool(name="ring", bufs=3))
        psum = ctx.enter_context(tc.psum_pool(name="psum", bufs=1))

        scales_raw = keep.tile([P, R], U8, name="scales_raw", align_bytes=ALIGN)
        nc.vector.memset(scales_raw[:].bitcast(I32), 0)

        x_rows = xT.rearrange("(p i) t -> p i t", i=PACK)
        wg_rows = wg.rearrange("(p i) r -> p i r", i=PACK)
        g_rows = g.rearrange("(p t) j -> p t j", t=PACK)
        out_rows = out_0.rearrange("(p t) j -> p t j", t=PACK)
        out_words = out_1[0].rearrange("p j i -> p (j i)").bitcast(I32)
        offsets = keep.tile([P, J // HEAD], U16, name="offsets")
        wu_raw = keep.tile([P, 2 * R], U8, name="wu_raw", align_bytes=ALIGN)
        planes = [keep.tile([P, T], F32, name=f"plane{i}") for i in range(PACK)]
        wgt_cut = keep.tile([P, CUT], F32, name="wgt_cut", align_bytes=ALIGN)
        g_sb = [keep.tile([P, PACK, HALF], F32, name=f"g{half}") for half in range(2)]
        wd_raw = keep.tile([P, R_PASSES, N], I32, name="wd_raw")

        early = keep.tile([P, PACK, HALF], F32, name="early", align_bytes=ALIGN)
        late = keep.tile([P, 6 * HALF], F32, name="late", align_bytes=ALIGN)
        at_wg1 = 3 * HALF + STEP
        late_rows = late[:, 0 : PACK * HALF].rearrange("p (i w) -> p i w", i=PACK)
        wg_raw = [keep.tile([P, PACK, PIECE], F32, name=f"wg_raw{u}", align_bytes=ALIGN)[:] for u in range(3)]
        wg_raw.append(late[:, at_wg1 : at_wg1 + PACK * PIECE].rearrange("p (i c) -> p i c", i=PACK))

        def load_wg(u):
            nc.sync.dma_start(wg_raw[u], wg_rows[:, :, u * PIECE : (u + 1) * PIECE])

        nc.sync.dma_start(wgt_cut[:], wgt[0:P:HEAD, :].rearrange("a (c j) -> a c j", j=CUT))
        nc.sync.dma_start(planes[0][:], x_rows[:, 0, :])
        nc.sync.dma_start(offsets[:], offs)
        nc.sync.dma_start(planes[1][:], x_rows[:, 1, :])
        nc.sync.dma_start(wu_raw[:].bitcast(I32), wu_words[0].bitcast(I32))
        for row in range(SCALE_ROWS):
            nc.sync.dma_start(
                scales_raw[row:P:QUADRANT, :].bitcast(I32), wu_scales[0, row::SCALE_ROWS, :].bitcast(I32)
            )
        nc.sync.dma_start(planes[2][:], x_rows[:, 2, :])
        for row in range(SCALE_ROWS):
            nc.sync.dma_start(
                scales_raw[SCALE_ROWS + row : P : QUADRANT, :].bitcast(I32).rearrange("q (b n) -> q b n", b=R_PASSES),
                wd_scales[:, row::SCALE_ROWS, :].bitcast(I32).rearrange("b q n -> q b n"),
            )
        nc.sync.dma_start(planes[3][:], x_rows[:, 3, :])
        for u in range(R // PIECE):
            load_wg(u)
        nc.sync.dma_start(wd_raw[:], wd_words.rearrange("b p n i -> p b (n i)").bitcast(I32))
        for half in range(2):
            nc.sync.dma_start(g_sb[half][:], g_rows[:, :, half * HALF : (half + 1) * HALF])

        warm = keep.tile([P, 1], F32, name="warm")
        nc.scalar.activation(warm[:], wgt_cut[:, 0:1], SIGMOID)

        staging = keep.tile([P, 8 * PASS], BF16, name="staging", align_bytes=ALIGN)
        h_first = staging[:, 0 : PASS * PACK]
        wg_bf = [keep.tile([P, PASS * PACK], BF16, name="wg_bf0", align_bytes=ALIGN)[:], staging[:, PASS * PACK : 2 * PASS * PACK]]
        xg45 = staging[:, PASS * PACK : PASS * PACK + PAIR * PACK]
        xg67 = staging[:, PASS * PACK - 3 * PAIR : PASS * PACK + PAIR]
        h01 = staging[:, PASS * PACK + PAIR : PASS * PACK + PAIR + 2 * PASS]
        wgt_sb = [keep.tile([P, HALF], F32, name="wgt0", align_bytes=ALIGN)[:], staging[:, 0 : 2 * HALF].bitcast(F32)]

        wgt_turned = keep.tile([P, CUT], F32, name="wgt_turned", align_bytes=ALIGN)
        for j0 in range(0, CUT, QUADRANT):
            nc.vector.transpose(wgt_turned[:, j0 : j0 + QUADRANT], wgt_cut[:, j0 : j0 + QUADRANT])
        cuts = HALF // CUT

        def spread(copy, half):
            repeated = keep.tile([P, HALF], F32, name=f"wgt_repeated{half}", align_bytes=ALIGN)
            source = wgt_turned[:].rearrange("p (sa c) -> p c sa", c=HEAD)[:, half * cuts : (half + 1) * cuts, :]
            copy(
                repeated[:].rearrange("p (c sa rep) -> p c sa rep", c=cuts, rep=HEAD),
                source.unsqueeze(3).to_broadcast([P, cuts, CUT // HEAD, HEAD]),
            )
            nc.vector.transpose(wgt_sb[half], repeated[:])

        wu_codes = keep.tile([P, 2 * R], U8, name="wu_codes", align_bytes=ALIGN)
        dealt = {}
        wd_codes = keep.tile([P, R_PASSES * N], U32, name="wd_codes", align_bytes=ALIGN)

        def deal_wu():
            nc.scalar.copy(
                wu_codes[:].bitcast(U16).rearrange("p (b t m) -> p b t m", b=R_PASSES, t=PACK),
                wu_raw[:].bitcast(U16).rearrange("p (b m t) -> p b t m", b=R_PASSES, t=PACK),
            )

        def deal_scales():
            dealt["s"] = keep.tile([P, R_PASSES * PACK, 2 * P], U8, name="wgt0", align_bytes=ALIGN)
            nc.vector.tensor_copy(
                dealt["s"][:, :, 0:P].rearrange("p (b t) m -> p b t m", b=R_PASSES),
                scales_raw[:].rearrange("p (b m t) -> p b t m", b=R_PASSES, t=PACK),
            )

        def deal_wd(b):
            nc.scalar.copy(
                wd_codes[:, b * N : (b + 1) * N].rearrange("p (t m) -> p m t", t=PACK),
                wd_raw[:, b].bitcast(U32).rearrange("p (m t) -> p m t", t=PACK),
            )

        wg_codes = [keep.tile([P, PASS], U32, name=f"wg_codes{b}", align_bytes=ALIGN) for b in range(R_PASSES)]
        wg_s = [keep.tile([P, PASS], U8, name=f"wg_s{b}", align_bytes=ALIGN) for b in range(R_PASSES)]

        def round_wg(copy, u, slices=slice(0, PACK)):
            b, m0 = divmod(u * PIECE_M, P)
            copy(
                wg_bf[b].rearrange("p (t m i) -> p m i t", t=PACK, i=PACK)[:, m0 : m0 + PIECE_M, :, slices],
                wg_raw[u].rearrange("p i (m t) -> p m i t", t=PACK)[:, :, :, slices],
            )

        def quantize_wg(b):
            nc.vector.quantize_mx(out=wg_codes[b][:].bitcast(FP8X4), scales=wg_s[b][:], in_=wg_bf[b])

        xg_bf = keep.tile([P, HALF * PACK], BF16, name="xg_bf", align_bytes=ALIGN)
        xg_mx = {}

        def gather(dst, i, j0, width):
            half, inside = divmod(j0, HALF)
            nc.vector.tensor_tensor(
                dst, planes[i][:].indirect(offsets[:, j0 // HEAD : (j0 + width) // HEAD]),
                wgt_sb[half][:, inside : inside + width], MULT,
            )

        def interleave(copy, dst, src, rows=slice(0, PACK)):
            copy(
                dst.rearrange("p (c e i) -> p c i e", e=LINE, i=PACK)[:, :, rows],
                src.rearrange("p i (c e) -> p c i e", e=LINE),
            )

        def round_xg(j0, width, src, rows):
            interleave(nc.scalar.copy, xg_bf[:, j0 * PACK : (j0 + width) * PACK], src, rows)

        def round_on_gpsimd(dst, src):
            nc.gpsimd.tensor_scalar(
                dst.rearrange("p (j t) -> p j t", t=PACK), src.rearrange("p t j -> p j t"), 1.0, 0.0, MULT, ADD
            )

        def quantize_xg(j0, width, rounded=None):
            if rounded is None:
                rounded = xg_bf[:, j0 * PACK : (j0 + width) * PACK]
            name = f"xg_codes{j0}"
            codes = keep.tile([P, width], U32, name=name, align_bytes=ALIGN)
            plane = keep.tile([P, width], U8, name=f"xg_s{j0}", align_bytes=ALIGN)
            nc.vector.quantize_mx(out=codes[:].bitcast(FP8X4), scales=plane[:], in_=rounded)
            for at in range(0, width, STEP):
                xg_mx[(j0 + at) // STEP] = (codes[:, at : at + STEP].bitcast(FP8X4), plane[:, at : at + STEP])

        out_codes = {}
        out_s = keep.tile([P, J], U8, name="out_s", align_bytes=ALIGN)
        gates, ubs = {}, {}
        chain = keep.tile([P, PASS], F32, name="chain", align_bytes=ALIGN)
        result23 = keep.tile([P, PACK * PAIR], F32, name="result23", align_bytes=ALIGN)

        def make_gate(s, b, bank):
            ga = psum.tile([P, PACK, STEP], F32, name=f"bank{bank}")
            for t in range(PACK):
                cols = slice(t * P, (t + 1) * P)
                nc.tensor.matmul_mx(
                    out=ga[:, t, :], lhsT=wg_codes[b][:, cols].bitcast(FP8X4), lhsT_scale=wg_s[b][:, cols],
                    rhs=xg_mx[s][0], rhs_scale=xg_mx[s][1], start=True, stop=True,
                )
            if (s, b) == (4, 0):
                gates[s, b] = chain[:].rearrange("p (j t) -> p j t", t=PACK)
            elif (s, b) in ((0, 1), (6, 1), (7, 0), (7, 1)):
                gates[s, b] = keep.tile([P, STEP, PACK], F32, name=f"gate{s}{b}", align_bytes=ALIGN)
            else:
                gates[s, b] = ring.tile([P, STEP, PACK], F32, name="gate", bufs=6, align_bytes=ALIGN)
            nc.scalar.activation(gates[s, b][:], ga[:].rearrange("p t j -> p j t"), SIGMOID)

        def make_ub(s, b, bank):
            ubs[s, b] = psum.tile([P, PACK, STEP], F32, name=f"bank{bank}")
            for t in range(PACK):
                col = b * PASS + t * P
                nc.tensor.matmul_mx(
                    out=ubs[s, b][:, t, :], lhsT=wu_codes[:, 2 * col : 2 * (col + P)].bitcast(FP4X4),
                    lhsT_scale=dealt["s"][:, b * PACK + t, 0:P],
                    rhs=xg_mx[s][0], rhs_scale=xg_mx[s][1], start=True, stop=True,
                )

        def make_h(s, b, dst):
            nc.vector.tensor_tensor(
                dst.rearrange("p (j t) -> p j t", t=PACK), ubs[s, b][:].rearrange("p t j -> p j t"), gates[s, b][:], MULT
            )

        def quantize_h(name, rounded, words, tag=None):
            codes = keep.tile([P, words], U32, name=tag or name + "_codes", align_bytes=ALIGN)
            plane = keep.tile([P, words], U8, name=name + "_s", align_bytes=ALIGN)
            nc.vector.quantize_mx(out=codes[:].bitcast(FP8X4), scales=plane[:], in_=rounded)
            return codes, plane

        def y_bank(slices, bank):
            return psum.tile([P, slices, PASS // slices], F32, name=f"bank{bank}")

        def second_stage(bank, first_slice, b, h_mx, at):
            slices, width = bank.shape[1], bank.shape[2]
            codes, plane = h_mx
            for t in range(slices):
                col = (first_slice + t) * P
                nc.tensor.matmul_mx(
                    out=bank[:, t, :], lhsT=wd_codes[:, b * N + col : b * N + col + P].bitcast(FP8X4),
                    lhsT_scale=dealt["s"][SCALE_ROWS:P, b * PACK + first_slice + t, 0:P],
                    rhs=codes[:, at : at + width].bitcast(FP8X4), rhs_scale=plane[:, at : at + width],
                    start=(b == 0 and t == 0), stop=(b == R_PASSES - 1 and t == slices - 1),
                )

        def g_of(j0, width, rows=slice(0, PACK)):
            half, inside = divmod(j0, HALF)
            return g_sb[half][:, rows, inside : inside + width]

        def store_out(j0, result, rows=slice(0, PACK)):
            nc.sync.dma_start(out_rows[:, rows, j0 : j0 + result.shape[2]], result[:, rows])

        def codes_of(j0, width):
            half, inside = divmod(j0, HALF)
            if half not in out_codes:
                out_codes[half] = keep.tile([P, HALF], U32, name=("gate71", "out_codes")[half], align_bytes=ALIGN)
            return out_codes[half][:, inside : inside + width]

        def quantize_out(j0, width, rounded):
            nc.vector.quantize_mx(
                out=codes_of(j0, width).bitcast(FP8X4), scales=out_s[:, j0 : j0 + width], in_=rounded
            )

        def store_codes(j0, width):
            nc.sync.dma_start(out_words[:, j0 : j0 + width], codes_of(j0, width).bitcast(I32))

        spread(nc.vector.tensor_copy, 0)
        spread(nc.scalar.copy, 1)
        for i in range(PACK - 1):
            gather(early[:, i, :], i, 0, HALF)
            gather(late_rows[:, i, :], i, HALF, HALF)
            if i == 1:
                round_xg(0, HALF, early[:, LOWER, :], LOWER)
                deal_wu()


        last = PACK - 1
        gather(early[:, last, 0:STEP], last, 0, STEP)
        round_xg(0, STEP, early[:, UPPER, 0:STEP], UPPER)
        gather(early[:, last, STEP:PAIR], last, STEP, STEP)
        round_xg(STEP, STEP, early[:, UPPER, STEP:PAIR], UPPER)
        gather(early[:, last, PAIR:HALF], last, PAIR, PAIR)
        round_wg(nc.scalar.copy, 0, LOWER)
        round_wg(nc.vector.tensor_copy, 0, UPPER)
        round_xg(PAIR, PAIR, early[:, UPPER, PAIR:HALF], UPPER)
        quantize_xg(0, STEP)
        quantize_xg(STEP, STEP)
        gather(late_rows[:, last, 0:STEP], last, HALF, STEP)
        deal_scales()
        make_ub(0, 0, 0)
        make_ub(1, 0, 1)
        round_wg(nc.scalar.copy, 1, LOWER)
        round_wg(nc.vector.tensor_copy, 1, UPPER)
        quantize_xg(PAIR, PAIR)
        quantize_wg(0)
        round_wg(nc.scalar.copy, 2)
        round_wg(nc.vector.tensor_copy, 3)
        gather(late_rows[:, last, STEP:HALF], last, HALF + STEP, HALF - STEP)
        make_gate(0, 0, 2)
        make_gate(1, 0, 3)
        make_gate(2, 0, 4)
        make_ub(2, 0, 5)
        make_gate(3, 0, 6)
        make_ub(3, 0, 2)
        quantize_wg(1)
        round_on_gpsimd(xg45, late_rows[:, :, 0:PAIR])

        make_gate(0, 1, 7)
        make_gate(1, 1, 3)
        deal_wd(0)
        make_h(0, 0, h_first[:, 0:PASS])
        make_ub(0, 1, 0)
        make_gate(2, 1, 4)
        make_h(1, 0, h_first[:, PASS : 2 * PASS])
        make_ub(1, 1, 1)
        make_gate(3, 1, 6)
        deal_wd(1)
        make_h(2, 0, h_first[:, 2 * PASS : 3 * PASS])
        make_ub(2, 1, 5)
        make_h(3, 0, h_first[:, 3 * PASS :])
        make_ub(3, 1, 2)
        first_mx = quantize_h("h_first", h_first, HALF)
        quantize_xg(HALF, PAIR, xg45)
        round_on_gpsimd(xg67, late_rows[:, :, PAIR:HALF])

        make_gate(4, 0, 7)
        make_ub(4, 0, 3)
        make_h(0, 1, h01[:, 0:PASS])
        make_gate(4, 1, 4)
        upper01 = y_bank(2, 0)
        second_stage(upper01, 2, 0, first_mx, 0)
        make_h(1, 1, h01[:, PASS:])
        make_gate(5, 0, 6)
        lower01 = y_bank(2, 1)
        second_stage(lower01, 0, 0, first_mx, 0)
        h23 = keep.tile([P, 2 * PASS], BF16, name="gate01", align_bytes=ALIGN)
        make_h(2, 1, h23[:, 0:PASS])
        make_ub(5, 0, 7)
        upper23 = y_bank(2, 5)
        second_stage(upper23, 2, 0, first_mx, PAIR)
        make_h(3, 1, h23[:, PASS:])
        make_gate(5, 1, 4)
        make_ub(4, 1, 2)
        mx01 = quantize_h("h01", h01, PAIR)
        second_stage(upper01, 2, 1, mx01, 0)
        second_stage(lower01, 0, 1, mx01, 0)
        quantize_xg(HALF + PAIR, PAIR, xg67)
        mx23 = quantize_h("h23", h23[:], PAIR)
        second_stage(upper23, 2, 1, mx23, 0)
        make_ub(5, 1, 6)

        result45 = keep.tile([P, PACK * PAIR], F32, name="result45", align_bytes=ALIGN)
        result01 = keep.tile([P, PACK * PAIR], F32, name="result01")
        results = [t[:].rearrange("p (t j) -> p t j", t=PACK) for t in (result01, result23, result45)]
        emptied = [keep.tile([P, 2, PAIR], F32, name=f"emptied{n}")[:] for n in range(2)] + [results[2][:, UPPER]]
        h45_second = chain[:].bitcast(BF16)
        h6 = result23[:, 0:PASS].bitcast(BF16)
        h7 = xg67
        nc.scalar.copy(emptied[0], upper01[:])
        nc.scalar.copy(emptied[1], upper23[:])
        make_h(4, 0, xg67[:, 0:PASS])
        make_gate(6, 0, 4)
        make_ub(6, 0, 3)
        make_h(5, 0, xg67[:, PASS:])
        make_gate(6, 1, 7)
        make_ub(6, 1, 0)
        lower23 = y_bank(2, 5)
        second_stage(lower23, 0, 0, first_mx, PAIR)
        second_stage(lower23, 0, 1, mx23, 0)
        nc.vector.tensor_tensor(results[0][:, LOWER], lower01[:], g_of(0, PAIR, LOWER), MULT)
        nc.gpsimd.tensor_tensor(results[0][:, UPPER], emptied[0], g_of(0, PAIR, UPPER), MULT)
        store_out(0, results[0])
        nc.gpsimd.tensor_tensor(results[1][:, UPPER], emptied[1], g_of(PAIR, PAIR, UPPER), MULT)
        store_out(PAIR, results[1], UPPER)
        nc.scalar.copy(emptied[2], lower23[:])
        make_ub(7, 0, 1)
        make_h(4, 1, h45_second[:, 0:PASS])
        make_gate(7, 0, 4)
        make_gate(7, 1, 2)
        make_ub(7, 1, 7)
        make_h(5, 1, h45_second[:, PASS:])
        make_h(6, 0, h6[:, 0:PASS])
        make_h(6, 1, h6[:, PASS:])
        mx45 = [quantize_h("h45_first", xg67, PAIR, "gate61"), quantize_h("h45_second", h45_second, PAIR)]
        mx6 = quantize_h("h6", h6, PAIR)
        nc.gpsimd.tensor_tensor(results[1][:, LOWER], emptied[2], g_of(PAIR, PAIR, LOWER), MULT)
        store_out(PAIR, results[1], LOWER)
        staged = [h45_second] + [keep.tile([P, PAIR * PACK], BF16, name=n, align_bytes=ALIGN)[:] for n in ("y23", "y45", "y67")]
        interleave(nc.scalar.copy, staged[0], results[0])
        interleave(nc.scalar.copy, staged[1], results[1])

        lower45, upper45, y6 = y_bank(2, 5), y_bank(2, 6), y_bank(PACK, 3)
        for bank, first_slice in ((lower45, 0), (upper45, 2)):
            for b in range(R_PASSES):
                second_stage(bank, first_slice, b, mx45[b], 0)
        for b in range(R_PASSES):
            second_stage(y6, 0, b, mx6, b * STEP)
        make_h(7, 1, h7[:, PASS:])
        make_h(7, 0, h7[:, 0:PASS])
        nc.vector.tensor_tensor(results[2][:, LOWER], lower45[:], g_of(HALF, PAIR, LOWER), MULT)
        store_out(HALF, results[2], LOWER)
        mx7 = quantize_h("h7", h7, PAIR, "gate70")
        y7 = y_bank(PACK, 0)
        for b in range(R_PASSES):
            second_stage(y7, 0, b, mx7, b * STEP)
        nc.vector.tensor_tensor(results[2][:, UPPER], upper45[:], g_of(HALF, PAIR, UPPER), MULT)
        store_out(HALF, results[2], UPPER)
        interleave(nc.scalar.copy, staged[2], results[2])
        j6, j7 = 6 * STEP, 7 * STEP
        result6, result7 = [g_sb[0][:, row, :].rearrange("p (t j) -> p t j", t=PACK) for row in range(2)]
        nc.vector.tensor_tensor(result6, y6[:], g_of(j6, STEP), MULT)
        store_out(j6, result6)
        interleave(nc.scalar.copy, staged[3][:, 0:PASS], result6)
        quantize_out(0, PAIR, staged[0])
        nc.vector.tensor_tensor(result7, y7[:], g_of(j7, STEP), MULT)
        store_out(j7, result7)
        quantize_out(PAIR, PAIR, staged[1])
        store_codes(0, HALF)
        interleave(nc.vector.tensor_copy, staged[3][:, PASS:], result7)
        quantize_out(HALF, PAIR, staged[2])
        quantize_out(j6, STEP, staged[3][:, 0:PASS])
        quantize_out(j7, STEP, staged[3][:, PASS:])
        store_codes(HALF, HALF)
        for row in range(SCALE_ROWS):
            queue = nc.scalar if row % 2 == 0 else nc.sync
            queue.dma_start(out_2[0, row::SCALE_ROWS, :].bitcast(I32), out_s[row:P:QUADRANT, :].bitcast(I32))
